import numpy as np
import ml_dtypes


def mxq(x, axis, fmt="e4m3"):
    dtype, down = {"e4m3": (ml_dtypes.float8_e4m3fn, 7), "e5m2": (ml_dtypes.float8_e5m2, 14)}[fmt]
    v = np.moveaxis(np.asarray(x, np.float32).astype(ml_dtypes.bfloat16).astype(np.float64), axis, -1)
    blocks = v.reshape(v.shape[:-1] + (-1, 32))
    amax = np.abs(blocks).max(-1, keepdims=True)
    byte = np.maximum(np.where(amax > 0, np.frexp(amax)[1] - 1 + 127, 0) - down, 1)
    scale = np.exp2(byte - 127.0)
    codes = (blocks / scale).astype(np.float32).astype(dtype).astype(np.float64)
    return np.moveaxis((codes * scale).reshape(v.shape), -1, axis)


WIDE = False


def mx_kscale(k):
    if not WIDE:
        return np.ones(k)
    levels = np.array([10, -10, 5, -5, 0])
    if k % 512:
        return np.exp2(np.random.permutation(np.resize(levels, k // 32))).repeat(32)
    a = np.empty((k // 512, 16))
    for p in range(k // 512):
        a[p, :8] = np.random.permutation(np.resize(levels, 8))
        for g in range(8):
            far = levels[np.abs(levels - a[p, g]) >= 10]
            a[p, g + 8] = far[np.random.randint(len(far))]
    return np.exp2(a.ravel()).repeat(32)


BF16 = ml_dtypes.bfloat16


def bf(x):
    return np.asarray(x, np.float32).astype(BF16)


def f64(x):
    return np.asarray(x).astype(np.float64)

def planes(Y):
    n, m = Y.shape
    b = f64(bf(Y)).reshape(n // 32, 32, m)
    amax = np.abs(b).max(1)
    byte = np.clip(np.where(amax > 0, np.frexp(amax)[1] - 1 + 127 - 7, 1), 1, 254)
    codes = (b * np.exp2(127.0 - byte)[:, None, :]).reshape(n, m).astype(np.float32).astype(ml_dtypes.float8_e4m3fn).view(np.uint8)
    words = codes.reshape(n // 512, 128, 4, m).transpose(0, 1, 3, 2)
    return np.ascontiguousarray(words), np.ascontiguousarray(byte.astype(np.uint8).reshape(n // 512, 16, m))


N, D, K = 2048, 1024, 512


def sigmoid(v):
    return 1.0 / (1.0 + np.exp(-v))


def threshold_logits(xgq, w, s, b):
    return (xgq @ mxq(f64(w), 0, "e4m3")) * f64(s)[None, :] + f64(b)[None, :]


def ordinal_labels(y, t):
    return np.where(f64(y)[:, None] > f64(t)[None, :], 1.0, 0.0)


def setup_inputs():
    u, v = mx_kscale(D), mx_kscale(K)
    return {"x": bf(np.random.standard_normal((N, D))),
            "g": bf((1.0 + 0.1 * np.random.standard_normal(D)) * u),
            "w": bf(np.random.standard_normal((D, K)) / np.sqrt(D) / u[:, None] / v[None, :]),
            "s": bf((1.0 + 0.1 * np.random.standard_normal(K)) * v),
            "b": bf(0.5 * np.random.standard_normal(K)),
            "y": bf(np.random.standard_normal(N)),
            "t": bf(np.random.standard_normal(K))}


def core(x, g, w, s, b, y, t):
    xgq = mxq(f64(x) * f64(g)[None, :], 1, "e4m3")
    z = threshold_logits(xgq, w, s, b)
    l = ordinal_labels(y, t)
    d = (sigmoid(z) - l) * f64(s)[None, :]
    return f64(g)[None, :] * (mxq(d, 1, "e4m3") @ mxq(f64(w).T, 0, "e4m3"))


def reference(x, g, w, s, b, y, t):
    R_out = core(x, g, w, s, b, y, t)
    words, scales = planes(R_out)
    return R_out, words, scales

@@ -1,0 +1,425 @@
+from contextlib import ExitStack
+
+import concourse.mybir as mybir
+from concourse.masks import make_identity
+
+N, D, K = 2048, 1024, 512
+FLOPS = 4 * N * D * K
+
+F32 = mybir.dt.float32
+BF16 = mybir.dt.bfloat16
+U32 = mybir.dt.uint32
+I32 = mybir.dt.int32
+U8 = mybir.dt.uint8
+FP8X4 = mybir.dt.float8_e4m3fn_x4
+ALU = mybir.AluOpType
+ACT = mybir.ActivationFunctionType
+
+P = 128
+CH = 512
+NCH = N // CH
+NH = D // 512
+
+
+def tile_ordinaldepththresholdfeaturegradient_x1_kernel(tc, x, g, w, s, b, y, t, out_0, out_1, out_2):
+    nc = tc.nc
+    with ExitStack() as ctx:
+        keep = ctx.enter_context(tc.tile_pool(name="keep", bufs=1))
+        xin = ctx.enter_context(tc.tile_pool(name="xin", bufs=NCH))
+        work = ctx.enter_context(tc.tile_pool(name="work", bufs=2))
+        outs = ctx.enter_context(tc.tile_pool(name="outs", bufs=4))
+        psum = ctx.enter_context(tc.psum_pool(name="psum", bufs=2))
+        psum_o = ctx.enter_context(tc.psum_pool(name="psum_o", bufs=4))
+        ctx.enter_context(tc.manual_schedule())
+
+        w_raw = keep.tile([P, NH, 4, K], BF16, align_bytes=64, name="w_raw")
+        w_v = w.rearrange("(h p j) k -> p h j k", h=NH, j=4)
+        x_raw = []
+        for c in range(NCH):
+            if c == 1:
+                for h in range(NH):
+                    nc.sync.dma_start(out=w_raw[:, h], in_=w_v[:, h])
+            xr = xin.tile([P, 4, D], BF16, align_bytes=64, name="xr")
+            xv = x[c * CH : (c + 1) * CH, :].rearrange("(p t) d -> p t d", t=4)
+            for tp in range(2):
+                nc.sync.dma_start(out=xr[:, 2 * tp : 2 * tp + 2, :], in_=xv[:, 2 * tp : 2 * tp + 2, :])
+            x_raw.append(xr)
+        cols = keep.tile([P, 8, 16], BF16, align_bytes=64, name="cols")
+        nc.scalar.dma_start(out=cols[:, 0, 0:8].rearrange("p (h i) -> p h i", h=NH), in_=g.rearrange("(h p i) -> p h i", h=NH, i=4))
+        nc.scalar.dma_start(out=cols[:, 1, :].rearrange("p (c i) -> p c i", c=NCH), in_=y.rearrange("(c p i) -> p c i", c=NCH, i=4))
+        for i, v in enumerate((t, s, b)):
+            nc.scalar.dma_start(out=cols[:, 2 + i, 0:4], in_=v.rearrange("(p i) -> p i", i=4))
+
+        warm = keep.tile([P, 1], F32, name="warm")
+        warm2 = keep.tile([P, 1], F32, name="warm2")
+        nc.vector.memset(warm[:], 0.0)
+        nc.scalar.activation(out=warm2[:], in_=warm[:], func=ACT.Sigmoid)
+
+        id32 = keep.tile([P, P], F32, align_bytes=64, name="id32")
+        make_identity(nc, id32[:])
+        id16 = keep.tile([P, P], BF16, align_bytes=64, name="id16")
+        nc.vector.tensor_copy(out=id16[:], in_=id32[:])
+        vec32 = keep.tile([P, 3, 4], F32, align_bytes=64, name="vec32")
+        nc.vector.tensor_copy(out=vec32[:], in_=cols[:, 2:5, 0:4])
+        g4 = cols[:, 0, 0:8].rearrange("p (h u e) -> p h u e", h=NH, u=2)
+
+        y_bc = keep.tile([P, N], BF16, align_bytes=64, name="y_bc")
+        def y_spread(halves):
+            for hf in halves:
+                yp = psum_o.tile([P, N // 2], BF16, name="o_ps")
+                for i in range(8):
+                    j = hf * 8 + i
+                    nc.tensor.transpose(
+                        yp[:, i * P : (i + 1) * P],
+                        cols[:, 1, j : j + 1].to_broadcast([P, P]),
+                        id16[:],
+                    )
+                nc.scalar.copy(out=y_bc[:, hf * N // 2 : (hf + 1) * N // 2], in_=yp[:])
+
+        w_gr = keep.tile([P, NH, K, 4], BF16, align_bytes=64, name="w_gr")
+        w_codes = keep.tile([P, NH, K], U32, align_bytes=64, name="w_codes")
+        w_scales = keep.tile([P, NH, K], U8, align_bytes=64, name="w_scales")
+
+        def w_inter(h, eng):
+            dst = w_gr[:, h].rearrange("p (q m) j -> p q m j", q=4)
+            srcv = w_raw[:, h].rearrange("p j (m q) -> p q m j", q=4)
+            for q in range(4):
+                if eng == 0:
+                    nc.scalar.copy(out=dst[:, q], in_=srcv[:, q])
+                else:
+                    nc.vector.tensor_copy(out=dst[:, q], in_=srcv[:, q])
+
+        def w_quant():
+            nc.vector.quantize_mx(
+                out=w_codes[:].rearrange("p h k -> p (h k)").bitcast(FP8X4),
+                scales=w_scales[:].rearrange("p h k -> p (h k)"),
+                in_=w_gr[:].rearrange("p h k j -> p (h k j)"),
+            )
+
+        xs = {}
+
+        def x_alloc(c):
+            xs[c] = (
+                work.tile([P, NH, CH, 4], BF16, align_bytes=64, name="x_gr"),
+                work.tile([P, NH, CH], U32, align_bytes=64, name="x_codes"),
+                work.tile([P, NH, CH], U8, align_bytes=64, name="x_scales"),
+            )
+
+        def x_turn(c, tp):
+            words = x_raw[c][:].bitcast(F32)
+            xts = []
+            for h in range(NH):
+                xt = psum.tile([P, 2, 256], F32, name="xt")
+                for tt in range(2):
+                    for u in range(2):
+                        cols_tt = slice(tt * P, (tt + 1) * P)
+                        nc.tensor.transpose(
+                            xt[:, u, cols_tt],
+                            words[:, 2 * tp + tt, 256 * h + u : 256 * (h + 1) : 2],
+                            id32[:],
+                        )
+                xts.append(xt)
+            return xts
+
+        def x_mul(c, tp, xts):
+            for h in range(NH):
+                nc.vector.tensor_tensor(
+                    out=xs[c][0][:, h, 256 * tp : 256 * (tp + 1), :].rearrange("p n (u e) -> p n u e", u=2),
+                    in0=xts[h][:].bitcast(BF16).rearrange("p u (n e) -> p n u e", e=2),
+                    in1=g4[:, h].unsqueeze(1).to_broadcast([P, 256, 2, 2]),
+                    op=ALU.mult,
+                )
+
+        def x_quant(c):
+            gr, codes, scales = xs[c]
+            nc.vector.quantize_mx(
+                out=codes[:].rearrange("p h n -> p (h n)").bitcast(FP8X4),
+                scales=scales[:].rearrange("p h n -> p (h n)"),
+                in_=gr[:].rearrange("p h n j -> p (h n j)"),
+            )
+
+        wt_gr = keep.tile([P, D, 4], BF16, align_bytes=64, name="wt_gr")
+        wt_codes = keep.tile([P, D], U32, align_bytes=64, name="wt_codes")
+        wt_scales = keep.tile([P, D], U8, align_bytes=64, name="wt_scales")
+
+        def wt_turn(blocks):
+            words = w_raw[:].bitcast(F32)
+            dst = wt_gr[:].rearrange("p d e -> p (d e)").bitcast(F32).rearrange("p (h m j u) -> p h m j u", h=NH, j=4, u=2)
+            for blk in blocks:
+                h, jp = blk // 2, blk % 2
+                wt = psum_o.tile([P, 2, 2, P], F32, name="o_ps")
+                for jj in range(2):
+                    for u in range(2):
+                        nc.tensor.transpose(wt[:, jj, u, :], words[:, h, 2 * jp + jj, u : 256 : 2], id32[:])
+                nc.scalar.copy(out=dst[:, h, :, 2 * jp : 2 * jp + 2, :], in_=wt[:].rearrange("p j u m -> p m j u"))
+
+        def wt_quant():
+            nc.vector.quantize_mx(
+                out=wt_codes[:].bitcast(FP8X4), scales=wt_scales[:], in_=wt_gr[:].rearrange("p d j -> p (d j)")
+            )
+
+        g_bc = keep.tile([P, D], BF16, align_bytes=64, name="g_bc")
+
+        def g_spread():
+            gp = psum_o.tile([P, 4, P], F32, name="o_ps")
+            gw = cols[:, 0, :].bitcast(F32)
+            for i in range(4):
+                nc.tensor.transpose(gp[:, i, :], gw[:, i : i + 1].to_broadcast([P, P]), id32[:])
+            nc.scalar.copy(
+                out=g_bc[:].bitcast(F32).rearrange("p (h m u) -> p h m u", h=NH, u=2),
+                in_=gp[:].rearrange("p (h u) m -> p h m u", h=NH),
+            )
+
+        ls = keep.tile([P, 4, N], BF16, align_bytes=64, name="ls")
+
+        def labels(q):
+            nc.vector.tensor_scalar(
+                out=ls[:, q, :],
+                in0=y_bc[:],
+                scalar1=vec32[:, 0, q : q + 1],
+                scalar2=vec32[:, 1, q : q + 1],
+                op0=ALU.is_gt,
+                op1=ALU.mult,
+            )
+
+        ds = {}
+
+        def d_alloc(c):
+            ds[c] = dict(
+                sig=work.tile([P, 4, CH], F32, align_bytes=64, name="sig"),
+                d=work.tile([P, 4, CH], F32, align_bytes=64, name="d32"),
+                gr=work.tile([P, CH, 4], BF16, align_bytes=64, name="d_gr"),
+                codes=work.tile([P, CH], U32, align_bytes=64, name="d_codes"),
+                scales=work.tile([P, CH], U8, align_bytes=64, name="d_scales"),
+            )
+
+        def mm1(c, q):
+            z = psum.tile([P, CH], F32, name="z")
+            for h in range(NH):
+                nc.tensor.matmul_mx(
+                    out=z[:],
+                    lhsT=w_codes[:, h, q * P : (q + 1) * P].bitcast(FP8X4),
+                    lhsT_scale=w_scales[:, h, q * P : (q + 1) * P],
+                    rhs=xs[c][1][:, h].bitcast(FP8X4),
+                    rhs_scale=xs[c][2][:, h],
+                    start=(h == 0),
+                    stop=(h == NH - 1),
+                )
+            nc.scalar.activation(
+                out=ds[c]["sig"][:, q, :],
+                in_=z[:],
+                func=ACT.Sigmoid,
+                bias=vec32[:, 2, q : q + 1],
+                scale=vec32[:, 1, q : q + 1],
+            )
+
+        def d_sub(c, q):
+            nc.vector.scalar_tensor_tensor(
+                out=ds[c]["d"][:, q, :],
+                in0=ds[c]["sig"][:, q, :],
+                scalar=vec32[:, 1, q : q + 1],
+                in1=ls[:, q, c * CH : (c + 1) * CH],
+                op0=ALU.mult,
+                op1=ALU.subtract,
+            )
+
+        def inter(dst, srct, lo, hi, on_vector):
+            o = dst[:, lo:hi, :].rearrange("p (c i) q -> p c q i", i=4)
+            i_ = srct[:, :, lo:hi].rearrange("p q (c i) -> p c q i", i=4)
+            if on_vector:
+                nc.vector.tensor_copy(out=o, in_=i_)
+            else:
+                nc.scalar.copy(out=o, in_=i_)
+
+        def d_quant(c):
+            e = ds[c]
+            nc.vector.quantize_mx(
+                out=e["codes"][:].bitcast(FP8X4), scales=e["scales"][:], in_=e["gr"][:].rearrange("p n j -> p (n j)")
+            )
+
+        outp = {}
+
+        def o_alloc(c, dh):
+            outp[(c, dh)] = dict(
+                o=outs.tile([P, 4, 512], F32, align_bytes=64, name="o32"),
+                gr=outs.tile([P, 512, 4], BF16, align_bytes=64, name="o_gr"),
+                codes=outs.tile([P, 512], U32, align_bytes=64, name="o_codes"),
+            )
+            if dh == 0:
+                outp[c] = work.tile([P, D], U8, align_bytes=64, name="o_scales")
+
+        def mm2(c, dh, tt, lo=0, hi=512):
+            o = psum_o.tile([P, hi - lo], F32, name="o_ps")
+            nc.tensor.matmul_mx(
+                out=o[:],
+                lhsT=ds[c]["codes"][:, tt * P : (tt + 1) * P].bitcast(FP8X4),
+                lhsT_scale=ds[c]["scales"][:, tt * P : (tt + 1) * P],
+                rhs=wt_codes[:, dh * 512 + lo : dh * 512 + hi].bitcast(FP8X4),
+                rhs_scale=wt_scales[:, dh * 512 + lo : dh * 512 + hi],
+                start=True,
+                stop=True,
+            )
+            return o
+
+        def o_mul(c, dh, tt, o, lo=0, hi=512):
+            nc.vector.tensor_tensor(
+                out=outp[(c, dh)]["o"][:, tt, lo:hi], in0=o[:], in1=g_bc[:, dh * 512 + lo : dh * 512 + hi], op=ALU.mult
+            )
+
+        def o_store(c, dh, t0, t1, lo=0, hi=512):
+            nc.sync.dma_start(
+                out=out_0[c * CH : (c + 1) * CH, dh * 512 + lo : dh * 512 + hi].rearrange("(p t) d -> p t d", t=4)[:, t0:t1, :],
+                in_=outp[(c, dh)]["o"][:, t0:t1, lo:hi],
+            )
+
+        def o_quant(c, dh, lo=0, hi=512):
+            e = outp[(c, dh)]
+            nc.vector.quantize_mx(
+                out=e["codes"][:, lo:hi].bitcast(FP8X4),
+                scales=outp[c][:, dh * 512 + lo : dh * 512 + hi],
+                in_=e["gr"][:, lo:hi, :].rearrange("p d j -> p (d j)"),
+            )
+            nc.sync.dma_start(
+                out=out_1[c, :, dh * 512 + lo : dh * 512 + hi, :].rearrange("p m t -> p (m t)").bitcast(I32),
+                in_=e["codes"][:, lo:hi].bitcast(I32),
+            )
+
+        def scale_store(c):
+            for qd in range(4):
+                nc.sync.dma_start(
+                    out=out_2[c, 4 * qd : 4 * qd + 4, :].bitcast(I32),
+                    in_=outp[c][32 * qd : 32 * qd + 4, :].bitcast(I32),
+                )
+
+        def o_inter(c, dh, lo, hi, on_vector):
+            inter(outp[(c, dh)]["gr"], outp[(c, dh)]["o"], lo, hi, on_vector)
+
+        def d_inter(c, lo, hi, on_vector):
+            inter(ds[c]["gr"], ds[c]["d"], lo, hi, on_vector)
+
+        d_split = [0,0,0,0]
+
+        def d_turn(c):
+            if d_split[c] > 0:
+                d_inter(c, 0, d_split[c], True)
+            d_inter(c, d_split[c], CH, False)
+
+        x_alloc(0)
+        x_mul(0, 0, x_turn(0, 0))
+        x_mul(0, 1, x_turn(0, 1))
+        w_inter(0, 0)
+        y_spread((0, 1))
+        w_inter(1, 0)
+        x_quant(0)
+        x_alloc(1)
+        x_mul(1, 0, x_turn(1, 0))
+        x_mul(1, 1, x_turn(1, 1))
+        for q in range(4):
+            labels(q)
+        wt_turn((0, 1, 2, 3))
+        xt20 = x_turn(2, 0)
+        w_quant()
+        d_alloc(0)
+        mm1(0, 0)
+        mm1(0, 1)
+        x_quant(1)
+        x_alloc(2)
+        x_mul(2, 0, xt20)
+        xt21 = x_turn(2, 1)
+        mm1(0, 2)
+        mm1(0, 3)
+        wt_quant()
+        d_sub(0, 0)
+        d_sub(0, 1)
+        x_mul(2, 1, xt21)
+        d_alloc(1)
+        mm1(1, 0)
+        xt30 = x_turn(3, 0)
+        d_sub(0, 2)
+        d_sub(0, 3)
+        d_turn(0)
+        x_alloc(3)
+        x_mul(3, 0, xt30)
+        mm1(1, 1)
+        xt31 = x_turn(3, 1)
+        mm1(1, 2)
+        g_spread()
+        mm1(1, 3)
+        x_quant(2)
+        d_sub(1, 0)
+        d_quant(0)
+        d_sub(1, 1)
+        d_sub(1, 2)
+        d_sub(1, 3)
+        for c in range(NCH):
+            last = c == NCH - 1
+            ahead = c + 2 < NCH
+            o_alloc(c, 0)
+            o_alloc(c, 1)
+            banks = [mm2(c, 0, tt) for tt in range(4)]
+            if not last:
+                if ahead:
+                    d_alloc(c + 2)
+                o_mul(c, 0, 0, banks[0])
+                banks.append(mm2(c, 1, 0))
+                d_turn(c + 1)
+                if ahead:
+                    mm1(c + 2, 0)
+                    mm1(c + 2, 1)
+                for tt in range(1, 4):
+                    o_mul(c, 0, tt, banks[tt])
+                    banks.append(mm2(c, 1, tt))
+                    if tt % 2 == 1:
+                        o_store(c, 0, tt - 1, tt + 1)
+                if ahead:
+                    mm1(c + 2, 2)
+                    mm1(c + 2, 3)
+                o_inter(c, 0, 0, 512, False)
+                o_mul(c, 1, 0, banks[4])
+                if c > 0:
+                    o_quant(c - 1, 0)
+                o_mul(c, 1, 1, banks[5])
+                o_store(c, 1, 0, 2)
+                if ahead:
+                    d_sub(c + 2, 0)
+                if c == 0:
+                    x_mul(3, 1, xt31)
+                o_mul(c, 1, 2, banks[6])
+                d_quant(c + 1)
+                o_mul(c, 1, 3, banks[7])
+                o_store(c, 1, 2, 4)
+                o_inter(c, 1, 0, 512, False)
+                if ahead:
+                    d_sub(c + 2, 1)
+                if c == 0:
+                    x_quant(3)
+                if ahead:
+                    d_sub(c + 2, 2)
+                    d_sub(c + 2, 3)
+                if c > 0:
+                    o_quant(c - 1, 1)
+                    scale_store(c - 1)
+            else:
+                for tt in range(4):
+                    o_mul(c, 0, tt, banks[tt])
+                    if tt % 2 == 1:
+                        o_store(c, 0, tt - 1, tt + 1)
+                    banks.append(mm2(c, 1, tt, 0, 256))
+                o_quant(c - 1, 0)
+                o_inter(c, 0, 0, 512, False)
+                for tt in range(4):
+                    o_mul(c, 1, tt, banks[4 + tt], 0, 256)
+                    banks.append(mm2(c, 1, tt, 256, 512))
+                o_store(c, 1, 0, 4, 0, 256)
+                o_quant(c - 1, 1)
+                scale_store(c - 1)
+                o_inter(c, 1, 0, 256, False)
+                for tt in range(4):
+                    o_mul(c, 1, tt, banks[8 + tt], 256, 512)
+                o_store(c, 1, 0, 4, 256, 512)
+                o_quant(c, 0)
+                o_inter(c, 1, 256, 384, False)
+                o_inter(c, 1, 384, 512, True)
+                o_quant(c, 1, 0, 256)
+                o_quant(c, 1, 256, 512)
+                scale_store(c)

@@ -25,78 +25,93 @@ def tile_ordinaldepththresholdfeaturegradient_x1_kernel(tc, x, g, w, s, b, y, t,
     nc = tc.nc
     with ExitStack() as ctx:
         keep = ctx.enter_context(tc.tile_pool(name="keep", bufs=1))
-        xin = ctx.enter_context(tc.tile_pool(name="xin", bufs=NCH))
         work = ctx.enter_context(tc.tile_pool(name="work", bufs=2))
         outs = ctx.enter_context(tc.tile_pool(name="outs", bufs=4))
-        psum = ctx.enter_context(tc.psum_pool(name="psum", bufs=2))
-        psum_o = ctx.enter_context(tc.psum_pool(name="psum_o", bufs=4))
+        psum_v = ctx.enter_context(tc.psum_pool(name="psum_v", bufs=5))
+        psum_s = ctx.enter_context(tc.psum_pool(name="psum_s", bufs=3))
         ctx.enter_context(tc.manual_schedule())
 
-        w_raw = keep.tile([P, NH, 4, K], BF16, align_bytes=64, name="w_raw")
-        w_v = w.rearrange("(h p j) k -> p h j k", h=NH, j=4)
-        x_raw = []
-        for c in range(NCH):
-            if c == 1:
-                for h in range(NH):
-                    nc.sync.dma_start(out=w_raw[:, h], in_=w_v[:, h])
-            xr = xin.tile([P, 4, D], BF16, align_bytes=64, name="xr")
-            xv = x[c * CH : (c + 1) * CH, :].rearrange("(p t) d -> p t d", t=4)
-            for tp in range(2):
-                nc.sync.dma_start(out=xr[:, 2 * tp : 2 * tp + 2, :], in_=xv[:, 2 * tp : 2 * tp + 2, :])
-            x_raw.append(xr)
-        cols = keep.tile([P, 8, 16], BF16, align_bytes=64, name="cols")
-        nc.scalar.dma_start(out=cols[:, 0, 0:8].rearrange("p (h i) -> p h i", h=NH), in_=g.rearrange("(h p i) -> p h i", h=NH, i=4))
-        nc.scalar.dma_start(out=cols[:, 1, :].rearrange("p (c i) -> p c i", c=NCH), in_=y.rearrange("(c p i) -> p c i", c=NCH, i=4))
-        for i, v in enumerate((t, s, b)):
-            nc.scalar.dma_start(out=cols[:, 2 + i, 0:4], in_=v.rearrange("(p i) -> p i", i=4))
+        x_raw = {}
+
+        def x_load(c, tp0, tp1):
+            xr = keep.tile([P, 2 * (tp1 - tp0) * D], BF16, align_bytes=64, name="xr%d%d" % (c, tp0))
+            xv = x[c * CH : (c + 1) * CH, :].rearrange("(p t) d -> p (t d)", t=4)
+            nc.sync.dma_start(out=xr[:], in_=xv[:, 2 * tp0 * D : 2 * tp1 * D])
+            for tp in range(tp0, tp1):
+                x_raw[(c, tp)] = xr[:, 2 * (tp - tp0) * D : 2 * (tp - tp0 + 1) * D]
+
+        w_raw = {}
+
+        def w_load(h):
+            wr = keep.tile([P, 4 * K], BF16, align_bytes=64, name="wr%d" % h)
+            nc.sync.dma_start(out=wr[:], in_=w[h * 512 : (h + 1) * 512, :].rearrange("(p j) k -> p (j k)", j=4))
+            w_raw[h] = wr
+
+        g_col = keep.tile([P, 8], BF16, align_bytes=64, name="g_col")
+        y_col = keep.tile([P, 16], BF16, align_bytes=64, name="y_col")
+        t_col = keep.tile([P, 4], BF16, align_bytes=64, name="t_col")
+        s_col = keep.tile([P, 4], BF16, align_bytes=64, name="s_col")
+        b_col = keep.tile([P, 4], BF16, align_bytes=64, name="b_col")
+        s32 = keep.tile([P, 4], F32, align_bytes=64, name="s32")
+
+        def g_load():
+            nc.scalar.dma_start(out=g_col[:].rearrange("p (h i) -> p h i", h=NH), in_=g.rearrange("(h p i) -> p h i", h=NH, i=4))
+
+        def y_load():
+            nc.scalar.dma_start(out=y_col[:].rearrange("p (c i) -> p c i", c=NCH), in_=y.rearrange("(c p i) -> p c i", c=NCH, i=4))
+
+        def col_load(dst, v):
+            nc.scalar.dma_start(out=dst[:], in_=v.rearrange("(p i) -> p i", i=4))
+
+        def s_widen():
+            nc.vector.tensor_copy(out=s32[:], in_=s_col[:])
 
         warm = keep.tile([P, 1], F32, name="warm")
         warm2 = keep.tile([P, 1], F32, name="warm2")
-        nc.vector.memset(warm[:], 0.0)
-        nc.scalar.activation(out=warm2[:], in_=warm[:], func=ACT.Sigmoid)
+
+        def warm_up():
+            nc.vector.memset(warm[:], 0.0)
+            nc.scalar.activation(out=warm2[:], in_=warm[:], func=ACT.Sigmoid)
 
         id32 = keep.tile([P, P], F32, align_bytes=64, name="id32")
-        make_identity(nc, id32[:])
         id16 = keep.tile([P, P], BF16, align_bytes=64, name="id16")
-        nc.vector.tensor_copy(out=id16[:], in_=id32[:])
-        vec32 = keep.tile([P, 3, 4], F32, align_bytes=64, name="vec32")
-        nc.vector.tensor_copy(out=vec32[:], in_=cols[:, 2:5, 0:4])
-        g4 = cols[:, 0, 0:8].rearrange("p (h u e) -> p h u e", h=NH, u=2)
+
+        def identities():
+            make_identity(nc, id32[:])
+            make_identity(nc, id16[:])
+
+        g4 = g_col[:].rearrange("p (h u e) -> p h u e", h=NH, u=2)
 
         y_bc = keep.tile([P, N], BF16, align_bytes=64, name="y_bc")
-        def y_spread(halves):
-            for hf in halves:
-                yp = psum_o.tile([P, N // 2], BF16, name="o_ps")
-                for i in range(8):
-                    j = hf * 8 + i
-                    nc.tensor.transpose(
-                        yp[:, i * P : (i + 1) * P],
-                        cols[:, 1, j : j + 1].to_broadcast([P, P]),
-                        id16[:],
-                    )
-                nc.scalar.copy(out=y_bc[:, hf * N // 2 : (hf + 1) * N // 2], in_=yp[:])
+
+        def y_spread(hf):
+            yp = psum_s.tile([P, N // 2], BF16, name="s_bank")
+            for i in range(8):
+                j = hf * 8 + i
+                nc.tensor.transpose(yp[:, i * P : (i + 1) * P], y_col[:, j : j + 1].to_broadcast([P, P]), id16[:])
+            nc.scalar.copy(out=y_bc[:, hf * N // 2 : (hf + 1) * N // 2], in_=yp[:])
 
         w_gr = keep.tile([P, NH, K, 4], BF16, align_bytes=64, name="w_gr")
         w_codes = keep.tile([P, NH, K], U32, align_bytes=64, name="w_codes")
         w_scales = keep.tile([P, NH, K], U8, align_bytes=64, name="w_scales")
 
-        def w_inter(h, eng):
-            dst = w_gr[:, h].rearrange("p (q m) j -> p q m j", q=4)
-            srcv = w_raw[:, h].rearrange("p j (m q) -> p q m j", q=4)
-            for q in range(4):
-                if eng == 0:
-                    nc.scalar.copy(out=dst[:, q], in_=srcv[:, q])
-                else:
-                    nc.vector.tensor_copy(out=dst[:, q], in_=srcv[:, q])
+        def w_inter(h, on_vector, lo=0, hi=64):
+            dst = w_gr[:, h].rearrange("p (q a m) j -> p a q m j", q=4, m=2)[:, lo:hi]
+            src = w_raw[h][:].rearrange("p (j a m q) -> p a q m j", j=4, m=2, q=4)[:, lo:hi]
+            if on_vector:
+                nc.vector.tensor_copy(out=dst, in_=src)
+            else:
+                nc.scalar.copy(out=dst, in_=src)
 
-        def w_quant():
+        def w_quant(h0, h1):
             nc.vector.quantize_mx(
-                out=w_codes[:].rearrange("p h k -> p (h k)").bitcast(FP8X4),
-                scales=w_scales[:].rearrange("p h k -> p (h k)"),
-                in_=w_gr[:].rearrange("p h k j -> p (h k j)"),
+                out=w_codes[:, h0:h1].rearrange("p h k -> p (h k)").bitcast(FP8X4),
+                scales=w_scales[:, h0:h1].rearrange("p h k -> p (h k)"),
+                in_=w_gr[:, h0:h1].rearrange("p h k j -> p (h k j)"),
             )
 
         xs = {}
+        xts = {}
 
         def x_alloc(c):
             xs[c] = (
@@ -105,30 +120,21 @@ def tile_ordinaldepththresholdfeaturegradient_x1_kernel(tc, x, g, w, s, b, y, t,
                 work.tile([P, NH, CH], U8, align_bytes=64, name="x_scales"),
             )
 
-        def x_turn(c, tp):
-            words = x_raw[c][:].bitcast(F32)
-            xts = []
-            for h in range(NH):
-                xt = psum.tile([P, 2, 256], F32, name="xt")
-                for tt in range(2):
-                    for u in range(2):
-                        cols_tt = slice(tt * P, (tt + 1) * P)
-                        nc.tensor.transpose(
-                            xt[:, u, cols_tt],
-                            words[:, 2 * tp + tt, 256 * h + u : 256 * (h + 1) : 2],
-                            id32[:],
-                        )
-                xts.append(xt)
-            return xts
+        def x_turn(c, tp, h):
+            words = x_raw[(c, tp)].bitcast(F32).rearrange("p (t d) -> p t d", t=2)
+            xt = psum_v.tile([P, 2, 256], F32, name="v_bank")
+            for tt in range(2):
+                for u in range(2):
+                    nc.tensor.transpose(xt[:, u, tt * P : (tt + 1) * P], words[:, tt, 256 * h + u : 256 * (h + 1) : 2], id32[:])
+            xts[(c, tp, h)] = xt
 
-        def x_mul(c, tp, xts):
-            for h in range(NH):
-                nc.vector.tensor_tensor(
-                    out=xs[c][0][:, h, 256 * tp : 256 * (tp + 1), :].rearrange("p n (u e) -> p n u e", u=2),
-                    in0=xts[h][:].bitcast(BF16).rearrange("p u (n e) -> p n u e", e=2),
-                    in1=g4[:, h].unsqueeze(1).to_broadcast([P, 256, 2, 2]),
-                    op=ALU.mult,
-                )
+        def x_mul(c, tp, h):
+            nc.vector.tensor_tensor(
+                out=xs[c][0][:, h, 256 * tp : 256 * (tp + 1), :].rearrange("p n (u e) -> p n u e", u=2),
+                in0=xts[(c, tp, h)][:].bitcast(BF16).rearrange("p u (n e) -> p n u e", e=2),
+                in1=g4[:, h].unsqueeze(1).to_broadcast([P, 256, 2, 2]),
+                op=ALU.mult,
+            )
 
         def x_quant(c):
             gr, codes, scales = xs[c]
@@ -138,46 +144,47 @@ def tile_ordinaldepththresholdfeaturegradient_x1_kernel(tc, x, g, w, s, b, y, t,
                 in_=gr[:].rearrange("p h n j -> p (h n j)"),
             )
 
+        def x_quant_part(c, h, lo, hi):
+            gr, codes, scales = xs[c]
+            nc.vector.quantize_mx(
+                out=codes[:, h, lo:hi].bitcast(FP8X4),
+                scales=scales[:, h, lo:hi],
+                in_=gr[:, h, lo:hi, :].rearrange("p n j -> p (n j)"),
+            )
+
         wt_gr = keep.tile([P, D, 4], BF16, align_bytes=64, name="wt_gr")
         wt_codes = keep.tile([P, D], U32, align_bytes=64, name="wt_codes")
         wt_scales = keep.tile([P, D], U8, align_bytes=64, name="wt_scales")
 
-        def wt_turn(blocks):
-            words = w_raw[:].bitcast(F32)
+        def wt_turn(h, jp):
+            words = w_raw[h][:].bitcast(F32).rearrange("p (j k) -> p j k", j=4)
             dst = wt_gr[:].rearrange("p d e -> p (d e)").bitcast(F32).rearrange("p (h m j u) -> p h m j u", h=NH, j=4, u=2)
-            for blk in blocks:
-                h, jp = blk // 2, blk % 2
-                wt = psum_o.tile([P, 2, 2, P], F32, name="o_ps")
-                for jj in range(2):
-                    for u in range(2):
-                        nc.tensor.transpose(wt[:, jj, u, :], words[:, h, 2 * jp + jj, u : 256 : 2], id32[:])
-                nc.scalar.copy(out=dst[:, h, :, 2 * jp : 2 * jp + 2, :], in_=wt[:].rearrange("p j u m -> p m j u"))
+            wt = psum_s.tile([P, 2, 2, P], F32, name="s_bank")
+            for jj in range(2):
+                for u in range(2):
+                    nc.tensor.transpose(wt[:, jj, u, :], words[:, 2 * jp + jj, u : 256 : 2], id32[:])
+            nc.scalar.copy(out=dst[:, h, :, 2 * jp : 2 * jp + 2, :], in_=wt[:].rearrange("p j u m -> p m j u"))
 
-        def wt_quant():
+        def wt_quant(h0, h1):
             nc.vector.quantize_mx(
-                out=wt_codes[:].bitcast(FP8X4), scales=wt_scales[:], in_=wt_gr[:].rearrange("p d j -> p (d j)")
+                out=wt_codes[:, h0 * 512 : h1 * 512].bitcast(FP8X4),
+                scales=wt_scales[:, h0 * 512 : h1 * 512],
+                in_=wt_gr[:, h0 * 512 : h1 * 512, :].rearrange("p d j -> p (d j)"),
             )
 
         g_bc = keep.tile([P, D], BF16, align_bytes=64, name="g_bc")
 
         def g_spread():
-            gp = psum_o.tile([P, 4, P], F32, name="o_ps")
-            gw = cols[:, 0, :].bitcast(F32)
-            for i in range(4):
-                nc.tensor.transpose(gp[:, i, :], gw[:, i : i + 1].to_broadcast([P, P]), id32[:])
-            nc.scalar.copy(
-                out=g_bc[:].bitcast(F32).rearrange("p (h m u) -> p h m u", h=NH, u=2),
-                in_=gp[:].rearrange("p (h u) m -> p h m u", h=NH),
-            )
+            nc.sync.dma_start(out=g_bc[:], in_=g.partition_broadcast(P))
 
         ls = keep.tile([P, 4, N], BF16, align_bytes=64, name="ls")
 
-        def labels(q):
+        def labels(q, lo=0, hi=N):
             nc.vector.tensor_scalar(
-                out=ls[:, q, :],
-                in0=y_bc[:],
-                scalar1=vec32[:, 0, q : q + 1],
-                scalar2=vec32[:, 1, q : q + 1],
+                out=ls[:, q, lo:hi],
+                in0=y_bc[:, lo:hi],
+                scalar1=t_col[:, q : q + 1],
+                scalar2=s_col[:, q : q + 1],
                 op0=ALU.is_gt,
                 op1=ALU.mult,
             )
@@ -193,51 +200,58 @@ def tile_ordinaldepththresholdfeaturegradient_x1_kernel(tc, x, g, w, s, b, y, t,
                 scales=work.tile([P, CH], U8, align_bytes=64, name="d_scales"),
             )
 
-        def mm1(c, q):
-            z = psum.tile([P, CH], F32, name="z")
+        def mm1(c, q, lo=0, hi=CH):
+            z = psum_s.tile([P, hi - lo], F32, name="s_bank")
             for h in range(NH):
                 nc.tensor.matmul_mx(
                     out=z[:],
                     lhsT=w_codes[:, h, q * P : (q + 1) * P].bitcast(FP8X4),
                     lhsT_scale=w_scales[:, h, q * P : (q + 1) * P],
-                    rhs=xs[c][1][:, h].bitcast(FP8X4),
-                    rhs_scale=xs[c][2][:, h],
+                    rhs=xs[c][1][:, h, lo:hi].bitcast(FP8X4),
+                    rhs_scale=xs[c][2][:, h, lo:hi],
                     start=(h == 0),
                     stop=(h == NH - 1),
                 )
             nc.scalar.activation(
-                out=ds[c]["sig"][:, q, :],
+                out=ds[c]["sig"][:, q, lo:hi],
                 in_=z[:],
                 func=ACT.Sigmoid,
-                bias=vec32[:, 2, q : q + 1],
-                scale=vec32[:, 1, q : q + 1],
+                bias=b_col[:, q : q + 1],
+                scale=s32[:, q : q + 1],
             )
 
-        def d_sub(c, q):
+        def d_sub(c, q, lo=0, hi=CH):
             nc.vector.scalar_tensor_tensor(
-                out=ds[c]["d"][:, q, :],
-                in0=ds[c]["sig"][:, q, :],
-                scalar=vec32[:, 1, q : q + 1],
-                in1=ls[:, q, c * CH : (c + 1) * CH],
+                out=ds[c]["d"][:, q, lo:hi],
+                in0=ds[c]["sig"][:, q, lo:hi],
+                scalar=s32[:, q : q + 1],
+                in1=ls[:, q, c * CH + lo : c * CH + hi],
                 op0=ALU.mult,
                 op1=ALU.subtract,
             )
 
-        def inter(dst, srct, lo, hi, on_vector):
-            o = dst[:, lo:hi, :].rearrange("p (c i) q -> p c q i", i=4)
-            i_ = srct[:, :, lo:hi].rearrange("p q (c i) -> p c q i", i=4)
+        def inter(dst, src, lo, hi, on_vector):
+            o = dst[:, lo:hi, :].rearrange("p (a i) q -> p a q i", i=4)
+            i_ = src[:, :, lo:hi].rearrange("p q (a i) -> p a q i", i=4)
             if on_vector:
                 nc.vector.tensor_copy(out=o, in_=i_)
             else:
                 nc.scalar.copy(out=o, in_=i_)
 
-        def d_quant(c):
+        def d_inter(c, lo=0, hi=CH, on_vector=False):
+            inter(ds[c]["gr"], ds[c]["d"], lo, hi, on_vector)
+
+        def d_quant(c, lo=0, hi=CH):
             e = ds[c]
             nc.vector.quantize_mx(
-                out=e["codes"][:].bitcast(FP8X4), scales=e["scales"][:], in_=e["gr"][:].rearrange("p n j -> p (n j)")
+                out=e["codes"][:, lo:hi].bitcast(FP8X4),
+                scales=e["scales"][:, lo:hi],
+                in_=e["gr"][:, lo:hi, :].rearrange("p n j -> p (n j)"),
             )
 
         outp = {}
+        banks = {}
+        o_scales = keep.tile([P, D], U8, align_bytes=64, name="o_scales")
 
         def o_alloc(c, dh):
             outp[(c, dh)] = dict(
@@ -245,11 +259,9 @@ def tile_ordinaldepththresholdfeaturegradient_x1_kernel(tc, x, g, w, s, b, y, t,
                 gr=outs.tile([P, 512, 4], BF16, align_bytes=64, name="o_gr"),
                 codes=outs.tile([P, 512], U32, align_bytes=64, name="o_codes"),
             )
-            if dh == 0:
-                outp[c] = work.tile([P, D], U8, align_bytes=64, name="o_scales")
 
         def mm2(c, dh, tt, lo=0, hi=512):
-            o = psum_o.tile([P, hi - lo], F32, name="o_ps")
+            o = psum_v.tile([P, hi - lo], F32, name="v_bank")
             nc.tensor.matmul_mx(
                 out=o[:],
                 lhsT=ds[c]["codes"][:, tt * P : (tt + 1) * P].bitcast(FP8X4),
@@ -259,11 +271,11 @@ def tile_ordinaldepththresholdfeaturegradient_x1_kernel(tc, x, g, w, s, b, y, t,
                 start=True,
                 stop=True,
             )
-            return o
+            banks[(c, dh, tt, lo)] = o
 
-        def o_mul(c, dh, tt, o, lo=0, hi=512):
+        def o_mul(c, dh, tt, lo=0, hi=512):
             nc.vector.tensor_tensor(
-                out=outp[(c, dh)]["o"][:, tt, lo:hi], in0=o[:], in1=g_bc[:, dh * 512 + lo : dh * 512 + hi], op=ALU.mult
+                out=outp[(c, dh)]["o"][:, tt, lo:hi], in0=banks[(c, dh, tt, lo)][:], in1=g_bc[:, dh * 512 + lo : dh * 512 + hi], op=ALU.mult
             )
 
         def o_store(c, dh, t0, t1, lo=0, hi=512):
@@ -272,154 +284,206 @@ def tile_ordinaldepththresholdfeaturegradient_x1_kernel(tc, x, g, w, s, b, y, t,
                 in_=outp[(c, dh)]["o"][:, t0:t1, lo:hi],
             )
 
+        def o_inter(c, dh, lo=0, hi=512, on_vector=False):
+            inter(outp[(c, dh)]["gr"], outp[(c, dh)]["o"], lo, hi, on_vector)
+
         def o_quant(c, dh, lo=0, hi=512):
             e = outp[(c, dh)]
             nc.vector.quantize_mx(
                 out=e["codes"][:, lo:hi].bitcast(FP8X4),
-                scales=outp[c][:, dh * 512 + lo : dh * 512 + hi],
+                scales=o_scales[4 * c : P, dh * 512 + lo : dh * 512 + hi],
                 in_=e["gr"][:, lo:hi, :].rearrange("p d j -> p (d j)"),
             )
+
+        def code_store(c, dh, lo=0, hi=512):
             nc.sync.dma_start(
                 out=out_1[c, :, dh * 512 + lo : dh * 512 + hi, :].rearrange("p m t -> p (m t)").bitcast(I32),
-                in_=e["codes"][:, lo:hi].bitcast(I32),
+                in_=outp[(c, dh)]["codes"][:, lo:hi].bitcast(I32),
             )
 
-        def scale_store(c):
-            for qd in range(4):
-                nc.sync.dma_start(
-                    out=out_2[c, 4 * qd : 4 * qd + 4, :].bitcast(I32),
-                    in_=outp[c][32 * qd : 32 * qd + 4, :].bitcast(I32),
-                )
+        def scale_store(qd, queue):
+            queue.dma_start(
+                out=out_2[:, 4 * qd : 4 * qd + 4, :].bitcast(I32),
+                in_=o_scales[32 * qd : 32 * qd + 16, :].bitcast(I32),
+            )
 
-        def o_inter(c, dh, lo, hi, on_vector):
-            inter(outp[(c, dh)]["gr"], outp[(c, dh)]["o"], lo, hi, on_vector)
-
-        def d_inter(c, lo, hi, on_vector):
-            inter(ds[c]["gr"], ds[c]["d"], lo, hi, on_vector)
-
-        d_split = [0,0,0,0]
-
-        def d_turn(c):
-            if d_split[c] > 0:
-                d_inter(c, 0, d_split[c], True)
-            d_inter(c, d_split[c], CH, False)
-
+        x_load(0, 0, 1)
+        g_load()
+        w_load(0)
+        y_load()
+        w_load(1)
+        col_load(s_col, s)
+        x_load(0, 1, 2)
+        col_load(t_col, t)
+        col_load(b_col, b)
+        for c in range(1, NCH):
+            x_load(c, 0, 2)
+        g_spread()
+        warm_up()
+        identities()
         x_alloc(0)
-        x_mul(0, 0, x_turn(0, 0))
-        x_mul(0, 1, x_turn(0, 1))
-        w_inter(0, 0)
-        y_spread((0, 1))
-        w_inter(1, 0)
-        x_quant(0)
+        for h in range(NH):
+            x_turn(0, 0, h)
+        for h in range(NH):
+            x_mul(0, 0, h)
+        w_inter(0, False)
+        y_spread(0)
+        s_widen()
+        w_inter(1, True)
+        wt_turn(0, 0)
+        for h in range(NH):
+            x_turn(0, 1, h)
+        w_quant(1, 2)
+        w_quant(0, 1)
+        for h in range(NH):
+            x_mul(0, 1, h)
+        wt_turn(0, 1)
         x_alloc(1)
-        x_mul(1, 0, x_turn(1, 0))
-        x_mul(1, 1, x_turn(1, 1))
-        for q in range(4):
-            labels(q)
-        wt_turn((0, 1, 2, 3))
-        xt20 = x_turn(2, 0)
-        w_quant()
+        for h in range(NH):
+            x_turn(1, 0, h)
+        labels(0, 0, 1024)
+        x_quant(0)
+        wt_turn(1, 0)
+        for q in range(1, 4):
+            labels(q, 0, 1024)
         d_alloc(0)
         mm1(0, 0)
         mm1(0, 1)
-        x_quant(1)
-        x_alloc(2)
-        x_mul(2, 0, xt20)
-        xt21 = x_turn(2, 1)
+        for h in range(NH):
+            x_mul(1, 0, h)
+            x_turn(1, 1, h)
         mm1(0, 2)
         mm1(0, 3)
-        wt_quant()
+        wt_turn(1, 1)
+        wt_quant(0, 1)
         d_sub(0, 0)
+        for h in range(NH):
+            x_mul(1, 1, h)
+        x_alloc(2)
+        for h in range(NH):
+            x_turn(2, 0, h)
         d_sub(0, 1)
-        x_mul(2, 1, xt21)
-        d_alloc(1)
-        mm1(1, 0)
-        xt30 = x_turn(3, 0)
+        x_quant(1)
         d_sub(0, 2)
         d_sub(0, 3)
-        d_turn(0)
-        x_alloc(3)
-        x_mul(3, 0, xt30)
+        d_alloc(1)
+        mm1(1, 0)
         mm1(1, 1)
-        xt31 = x_turn(3, 1)
+        d_inter(0)
+        for h in range(NH):
+            x_turn(2, 1, h)
         mm1(1, 2)
-        g_spread()
         mm1(1, 3)
-        x_quant(2)
+        y_spread(1)
+        wt_quant(1, 2)
+        for tp in range(2):
+            for h in range(NH):
+                x_mul(2, tp, h)
+        x_alloc(3)
+        x_turn(3, 0, 0)
         d_sub(1, 0)
         d_quant(0)
-        d_sub(1, 1)
-        d_sub(1, 2)
-        d_sub(1, 3)
-        for c in range(NCH):
-            last = c == NCH - 1
-            ahead = c + 2 < NCH
-            o_alloc(c, 0)
-            o_alloc(c, 1)
-            banks = [mm2(c, 0, tt) for tt in range(4)]
-            if not last:
-                if ahead:
-                    d_alloc(c + 2)
-                o_mul(c, 0, 0, banks[0])
-                banks.append(mm2(c, 1, 0))
-                d_turn(c + 1)
-                if ahead:
-                    mm1(c + 2, 0)
-                    mm1(c + 2, 1)
-                for tt in range(1, 4):
-                    o_mul(c, 0, tt, banks[tt])
-                    banks.append(mm2(c, 1, tt))
-                    if tt % 2 == 1:
-                        o_store(c, 0, tt - 1, tt + 1)
-                if ahead:
-                    mm1(c + 2, 2)
-                    mm1(c + 2, 3)
-                o_inter(c, 0, 0, 512, False)
-                o_mul(c, 1, 0, banks[4])
-                if c > 0:
-                    o_quant(c - 1, 0)
-                o_mul(c, 1, 1, banks[5])
-                o_store(c, 1, 0, 2)
-                if ahead:
-                    d_sub(c + 2, 0)
-                if c == 0:
-                    x_mul(3, 1, xt31)
-                o_mul(c, 1, 2, banks[6])
-                d_quant(c + 1)
-                o_mul(c, 1, 3, banks[7])
-                o_store(c, 1, 2, 4)
-                o_inter(c, 1, 0, 512, False)
-                if ahead:
-                    d_sub(c + 2, 1)
-                if c == 0:
-                    x_quant(3)
-                if ahead:
-                    d_sub(c + 2, 2)
-                    d_sub(c + 2, 3)
-                if c > 0:
-                    o_quant(c - 1, 1)
-                    scale_store(c - 1)
-            else:
-                for tt in range(4):
-                    o_mul(c, 0, tt, banks[tt])
-                    if tt % 2 == 1:
-                        o_store(c, 0, tt - 1, tt + 1)
-                    banks.append(mm2(c, 1, tt, 0, 256))
+        o_alloc(0, 0)
+        o_alloc(0, 1)
+        for tt in range(4):
+            mm2(0, 0, tt)
+        x_quant(2)
+        for q in range(1, 4):
+            d_sub(1, q)
+        d_alloc(2)
+        mm1(2, 0)
+        mm1(2, 1)
+        d_inter(1)
+        mm1(2, 2)
+        mm1(2, 3)
+        x_mul(3, 0, 0)
+        for tt in range(4):
+            if tt < 3:
+                x_turn(3, (tt + 1) // 2, (tt + 1) % 2)
+            o_mul(0, 0, tt)
+            if tt % 2 == 1:
+                o_store(0, 0, tt - 1, tt + 1)
+        o_inter(0, 0)
+        for tt in range(1, 4):
+            x_mul(3, tt // 2, tt % 2)
+            mm2(0, 1, tt - 1)
+        mm2(0, 1, 3)
+        d_quant(1)
+        x_quant(3)
+        d_alloc(3)
+        for q in range(4):
+            labels(q, 1024, 2048)
+        o_alloc(1, 0)
+        o_alloc(1, 1)
+        for tt in range(4):
+            mm1(3, tt)
+            o_mul(0, 1, tt)
+            mm2(1, 0, tt)
+            if tt % 2 == 1:
+                o_store(0, 1, tt - 1, tt + 1)
+        for q in range(4):
+            d_sub(2, q)
+        o_inter(0, 1)
+        d_inter(2)
+        for tt in range(4):
+            o_mul(1, 0, tt)
+            mm2(1, 1, tt)
+            if tt % 2 == 1:
+                o_store(1, 0, tt - 1, tt + 1)
+        o_inter(1, 0)
+        o_quant(0, 0)
+        code_store(0, 0)
+        for q in range(4):
+            d_sub(3, q)
+        d_quant(2)
+        o_alloc(2, 0)
+        for tt in range(4):
+            o_mul(1, 1, tt)
+            mm2(2, 0, tt)
+            if tt % 2 == 1:
+                o_store(1, 1, tt - 1, tt + 1)
+        d_inter(3)
+        o_inter(1, 1)
+        o_quant(0, 1)
+        code_store(0, 1)
+        o_alloc(2, 1)
+        for tt in range(4):
+            o_mul(2, 0, tt)
+            mm2(2, 1, tt)
+            if tt % 2 == 1:
+                o_store(2, 0, tt - 1, tt + 1)
+        o_inter(2, 0)
+        d_quant(3)
+        o_quant(1, 0)
+        code_store(1, 0)
+        c = NCH - 1
+        o_alloc(c, 0)
+        for tt in range(4):
+            o_mul(2, 1, tt)
+            mm2(c, 0, tt, 0, 256)
+            if tt % 2 == 1:
+                o_store(2, 1, tt - 1, tt + 1)
+        o_inter(2, 1)
+        o_quant(1, 1)
+        code_store(1, 1)
+        o_alloc(c, 1)
+        for qt in range(4):
+            dh, lo = qt // 2, 256 * (qt % 2)
+            for tt in range(4):
+                o_mul(c, dh, tt, lo, lo + 256)
+                if qt < 3:
+                    mm2(c, (qt + 1) // 2, tt, 256 * ((qt + 1) % 2), 256 * ((qt + 1) % 2) + 256)
+            o_store(c, dh, 0, 4, lo, lo + 256)
+            o_inter(c, dh, lo, lo + 256)
+            if qt == 1:
                 o_quant(c - 1, 0)
-                o_inter(c, 0, 0, 512, False)
-                for tt in range(4):
-                    o_mul(c, 1, tt, banks[4 + tt], 0, 256)
-                    banks.append(mm2(c, 1, tt, 256, 512))
-                o_store(c, 1, 0, 4, 0, 256)
-                o_quant(c - 1, 1)
-                scale_store(c - 1)
-                o_inter(c, 1, 0, 256, False)
-                for tt in range(4):
-                    o_mul(c, 1, tt, banks[8 + tt], 256, 512)
-                o_store(c, 1, 0, 4, 256, 512)
-                o_quant(c, 0)
-                o_inter(c, 1, 256, 384, False)
-                o_inter(c, 1, 384, 512, True)
-                o_quant(c, 1, 0, 256)
-                o_quant(c, 1, 256, 512)
-                scale_store(c)
+                code_store(c - 1, 0)
+        o_quant(c - 1, 1)
+        code_store(c - 1, 1)
+        o_quant(c, 0)
+        code_store(c, 0)
+        o_quant(c, 1, 0, 256)
+        o_quant(c, 1, 256, 512)
+        code_store(c, 1)
+        for qd in range(4):
+            scale_store(qd, nc.scalar if qd % 2 else nc.sync)

@@ -26,10 +26,17 @@ def tile_ordinaldepththresholdfeaturegradient_x1_kernel(tc, x, g, w, s, b, y, t,
     with ExitStack() as ctx:
         keep = ctx.enter_context(tc.tile_pool(name="keep", bufs=1))
         work = ctx.enter_context(tc.tile_pool(name="work", bufs=2))
+        big = ctx.enter_context(tc.tile_pool(name="big", bufs=8))
         outs = ctx.enter_context(tc.tile_pool(name="outs", bufs=4))
-        psum_v = ctx.enter_context(tc.psum_pool(name="psum_v", bufs=5))
+        psum_v = ctx.enter_context(tc.psum_pool(name="psum_v", bufs=1))
         psum_s = ctx.enter_context(tc.psum_pool(name="psum_s", bufs=3))
         ctx.enter_context(tc.manual_schedule())
+
+        v_free = list(range(5))
+
+        def v_bank(shape):
+            i = v_free.pop(0)
+            return psum_v.tile(shape, F32, name="v_bank%d" % i), i
 
         x_raw = {}
 
@@ -91,7 +98,7 @@ def tile_ordinaldepththresholdfeaturegradient_x1_kernel(tc, x, g, w, s, b, y, t,
                 nc.tensor.transpose(yp[:, i * P : (i + 1) * P], y_col[:, j : j + 1].to_broadcast([P, P]), id16[:])
             nc.scalar.copy(out=y_bc[:, hf * N // 2 : (hf + 1) * N // 2], in_=yp[:])
 
-        w_gr = keep.tile([P, NH, K, 4], BF16, align_bytes=64, name="w_gr")
+        w_gr = big.tile([P, NH, K, 4], BF16, align_bytes=64, name="big")
         w_codes = keep.tile([P, NH, K], U32, align_bytes=64, name="w_codes")
         w_scales = keep.tile([P, NH, K], U8, align_bytes=64, name="w_scales")
 
@@ -114,29 +121,28 @@ def tile_ordinaldepththresholdfeaturegradient_x1_kernel(tc, x, g, w, s, b, y, t,
         xts = {}
 
         def x_alloc(c):
-            xs[c] = (
-                work.tile([P, NH, CH, 4], BF16, align_bytes=64, name="x_gr"),
-                work.tile([P, NH, CH], U32, align_bytes=64, name="x_codes"),
-                work.tile([P, NH, CH], U8, align_bytes=64, name="x_scales"),
-            )
+            xs[c] = [big.tile([P, NH, CH, 4], BF16, align_bytes=64, name="big")]
 
         def x_turn(c, tp, h):
             words = x_raw[(c, tp)].bitcast(F32).rearrange("p (t d) -> p t d", t=2)
-            xt = psum_v.tile([P, 2, 256], F32, name="v_bank")
+            xt, bank = v_bank([P, 2, 256])
             for tt in range(2):
                 for u in range(2):
                     nc.tensor.transpose(xt[:, u, tt * P : (tt + 1) * P], words[:, tt, 256 * h + u : 256 * (h + 1) : 2], id32[:])
-            xts[(c, tp, h)] = xt
+            xts[(c, tp, h)] = (xt, bank)
 
         def x_mul(c, tp, h):
             nc.vector.tensor_tensor(
                 out=xs[c][0][:, h, 256 * tp : 256 * (tp + 1), :].rearrange("p n (u e) -> p n u e", u=2),
-                in0=xts[(c, tp, h)][:].bitcast(BF16).rearrange("p u (n e) -> p n u e", e=2),
+                in0=xts[(c, tp, h)][0][:].bitcast(BF16).rearrange("p u (n e) -> p n u e", e=2),
                 in1=g4[:, h].unsqueeze(1).to_broadcast([P, 256, 2, 2]),
                 op=ALU.mult,
             )
+            v_free.append(xts[(c, tp, h)][1])
 
         def x_quant(c):
+            xs[c].append(work.tile([P, NH, CH], U32, align_bytes=64, name="x_codes"))
+            xs[c].append(work.tile([P, NH, CH], U8, align_bytes=64, name="x_scales"))
             gr, codes, scales = xs[c]
             nc.vector.quantize_mx(
                 out=codes[:].rearrange("p h n -> p (h n)").bitcast(FP8X4),
@@ -144,15 +150,7 @@ def tile_ordinaldepththresholdfeaturegradient_x1_kernel(tc, x, g, w, s, b, y, t,
                 in_=gr[:].rearrange("p h n j -> p (h n j)"),
             )
 
-        def x_quant_part(c, h, lo, hi):
-            gr, codes, scales = xs[c]
-            nc.vector.quantize_mx(
-                out=codes[:, h, lo:hi].bitcast(FP8X4),
-                scales=scales[:, h, lo:hi],
-                in_=gr[:, h, lo:hi, :].rearrange("p n j -> p (n j)"),
-            )
-
-        wt_gr = keep.tile([P, D, 4], BF16, align_bytes=64, name="wt_gr")
+        wt_gr = big.tile([P, D, 4], BF16, align_bytes=64, name="big")
         wt_codes = keep.tile([P, D], U32, align_bytes=64, name="wt_codes")
         wt_scales = keep.tile([P, D], U8, align_bytes=64, name="wt_scales")
 
@@ -190,6 +188,7 @@ def tile_ordinaldepththresholdfeaturegradient_x1_kernel(tc, x, g, w, s, b, y, t,
             )
 
         ds = {}
+        zs = {}
 
         def d_alloc(c):
             ds[c] = dict(
@@ -212,9 +211,12 @@ def tile_ordinaldepththresholdfeaturegradient_x1_kernel(tc, x, g, w, s, b, y, t,
                     start=(h == 0),
                     stop=(h == NH - 1),
                 )
+            zs[(c, q)] = z
+
+        def sigm(c, q, lo=0, hi=CH):
             nc.scalar.activation(
                 out=ds[c]["sig"][:, q, lo:hi],
-                in_=z[:],
+                in_=zs[(c, q)][:],
                 func=ACT.Sigmoid,
                 bias=b_col[:, q : q + 1],
                 scale=s32[:, q : q + 1],
@@ -255,13 +257,13 @@ def tile_ordinaldepththresholdfeaturegradient_x1_kernel(tc, x, g, w, s, b, y, t,
 
         def o_alloc(c, dh):
             outp[(c, dh)] = dict(
-                o=outs.tile([P, 4, 512], F32, align_bytes=64, name="o32"),
+                o=big.tile([P, 4, 512], F32, align_bytes=64, name="big"),
                 gr=outs.tile([P, 512, 4], BF16, align_bytes=64, name="o_gr"),
-                codes=outs.tile([P, 512], U32, align_bytes=64, name="o_codes"),
+                codes=keep.tile([P, 512], U32, align_bytes=64, name="o_codes%d%d" % (c, dh)),
             )
 
         def mm2(c, dh, tt, lo=0, hi=512):
-            o = psum_v.tile([P, hi - lo], F32, name="v_bank")
+            o, bank = v_bank([P, hi - lo])
             nc.tensor.matmul_mx(
                 out=o[:],
                 lhsT=ds[c]["codes"][:, tt * P : (tt + 1) * P].bitcast(FP8X4),
@@ -271,12 +273,37 @@ def tile_ordinaldepththresholdfeaturegradient_x1_kernel(tc, x, g, w, s, b, y, t,
                 start=True,
                 stop=True,
             )
-            banks[(c, dh, tt, lo)] = o
+            banks[(c, dh, tt, lo)] = (o, bank)
 
         def o_mul(c, dh, tt, lo=0, hi=512):
             nc.vector.tensor_tensor(
-                out=outp[(c, dh)]["o"][:, tt, lo:hi], in0=banks[(c, dh, tt, lo)][:], in1=g_bc[:, dh * 512 + lo : dh * 512 + hi], op=ALU.mult
+                out=outp[(c, dh)]["o"][:, tt, lo:hi], in0=banks[(c, dh, tt, lo)][0][:], in1=g_bc[:, dh * 512 + lo : dh * 512 + hi], op=ALU.mult
             )
+            v_free.append(banks[(c, dh, tt, lo)][1])
+
+        def mm2_pair(c, dh, tp, lo):
+            o, bank = v_bank([P, 2, 256])
+            for tt in range(2):
+                cols = slice((2 * tp + tt) * P, (2 * tp + tt + 1) * P)
+                nc.tensor.matmul_mx(
+                    out=o[:, tt, :],
+                    lhsT=ds[c]["codes"][:, cols].bitcast(FP8X4),
+                    lhsT_scale=ds[c]["scales"][:, cols],
+                    rhs=wt_codes[:, dh * 512 + lo : dh * 512 + lo + 256].bitcast(FP8X4),
+                    rhs_scale=wt_scales[:, dh * 512 + lo : dh * 512 + lo + 256],
+                    start=True,
+                    stop=True,
+                )
+            banks[(c, dh, tp, lo)] = (o, bank)
+
+        def o_mul_pair(c, dh, tp, lo):
+            nc.vector.tensor_tensor(
+                out=outp[(c, dh)]["o"][:, 2 * tp : 2 * tp + 2, lo : lo + 256],
+                in0=banks[(c, dh, tp, lo)][0][:],
+                in1=g_bc[:, dh * 512 + lo : dh * 512 + lo + 256].unsqueeze(1).to_broadcast([P, 2, 256]),
+                op=ALU.mult,
+            )
+            v_free.append(banks[(c, dh, tp, lo)][1])
 
         def o_store(c, dh, t0, t1, lo=0, hi=512):
             nc.sync.dma_start(
@@ -307,13 +334,59 @@ def tile_ordinaldepththresholdfeaturegradient_x1_kernel(tc, x, g, w, s, b, y, t,
                 in_=o_scales[32 * qd : 32 * qd + 16, :].bitcast(I32),
             )
 
+        LAST_FIRST = (3, 2, 1, 0)
+
+
+        def x_muls(c, refill):
+            for j, i in enumerate(LAST_FIRST):
+                x_mul(c, i // 2, i % 2)
+                if j < 3:
+                    refill(j + 1)
+
+
+        def o_muls(c, dh, refill):
+            for j, tt in enumerate(LAST_FIRST):
+                o_mul(c, dh, tt)
+                if j < 3:
+                    refill(j + 1)
+                if tt % 2 == 0:
+                    o_store(c, dh, tt, tt + 2)
+
+
+        def x_fill(c):
+            x_turn(c, 0, 0)
+            return lambda i: x_turn(c, i // 2, i % 2)
+
+
+        def o_fill(c, dh):
+            o_alloc(c, dh)
+            mm2(c, dh, 0)
+            return lambda tt: mm2(c, dh, tt)
+
+
+        def stage1(c, qs):
+            for q in qs:
+                mm1(c, q)
+                sigm(c, q)
+
+
+        def d_subs(c):
+            for q in LAST_FIRST:
+                d_sub(c, q)
+
+
+        def o_pack(c, dh):
+            o_quant(c, dh)
+            code_store(c, dh)
+
+
         x_load(0, 0, 1)
         g_load()
-        w_load(0)
-        y_load()
-        w_load(1)
-        col_load(s_col, s)
         x_load(0, 1, 2)
+        y_load()
+        w_load(0)
+        col_load(s_col, s)
+        w_load(1)
         col_load(t_col, t)
         col_load(b_col, b)
         for c in range(1, NCH):
@@ -321,167 +394,97 @@ def tile_ordinaldepththresholdfeaturegradient_x1_kernel(tc, x, g, w, s, b, y, t,
         g_spread()
         warm_up()
         identities()
-        x_alloc(0)
-        for h in range(NH):
-            x_turn(0, 0, h)
-        for h in range(NH):
-            x_mul(0, 0, h)
-        w_inter(0, False)
+        for c in range(NCH):
+            x_alloc(c)
+        for i in range(4):
+            x_turn(0, i // 2, i % 2)
+        for i in (0, 1, 3, 2):
+            x_mul(0, i // 2, i % 2)
+        w_inter(0, False, 0, 32)
         y_spread(0)
+        wt_turn(0, 0)
+        w_inter(0, False, 32, 64)
+        wt_turn(0, 1)
+        wt_turn(1, 0)
         s_widen()
         w_inter(1, True)
-        wt_turn(0, 0)
-        for h in range(NH):
-            x_turn(0, 1, h)
-        w_quant(1, 2)
-        w_quant(0, 1)
-        for h in range(NH):
-            x_mul(0, 1, h)
-        wt_turn(0, 1)
-        x_alloc(1)
-        for h in range(NH):
-            x_turn(1, 0, h)
-        labels(0, 0, 1024)
         x_quant(0)
-        wt_turn(1, 0)
-        for q in range(1, 4):
+        for i in range(4):
+            x_turn(1, i // 2, i % 2)
+        w_quant(0, 2)
+        for q in range(4):
             labels(q, 0, 1024)
-        d_alloc(0)
-        mm1(0, 0)
-        mm1(0, 1)
-        for h in range(NH):
-            x_mul(1, 0, h)
-            x_turn(1, 1, h)
-        mm1(0, 2)
-        mm1(0, 3)
         wt_turn(1, 1)
+        d_alloc(0)
+        stage1(0, range(4))
+        x_muls(1, x_fill(2))
         wt_quant(0, 1)
-        d_sub(0, 0)
-        for h in range(NH):
-            x_mul(1, 1, h)
-        x_alloc(2)
-        for h in range(NH):
-            x_turn(2, 0, h)
-        d_sub(0, 1)
         x_quant(1)
-        d_sub(0, 2)
-        d_sub(0, 3)
         d_alloc(1)
-        mm1(1, 0)
-        mm1(1, 1)
+        stage1(1, (0,))
+        d_subs(0)
         d_inter(0)
-        for h in range(NH):
-            x_turn(2, 1, h)
-        mm1(1, 2)
-        mm1(1, 3)
+        stage1(1, (1, 2, 3))
         y_spread(1)
+        x_muls(2, lambda i: None)
         wt_quant(1, 2)
-        for tp in range(2):
-            for h in range(NH):
-                x_mul(2, tp, h)
-        x_alloc(3)
-        x_turn(3, 0, 0)
-        d_sub(1, 0)
         d_quant(0)
-        o_alloc(0, 0)
-        o_alloc(0, 1)
-        for tt in range(4):
-            mm2(0, 0, tt)
-        x_quant(2)
-        for q in range(1, 4):
-            d_sub(1, q)
-        d_alloc(2)
-        mm1(2, 0)
-        mm1(2, 1)
-        d_inter(1)
-        mm1(2, 2)
-        mm1(2, 3)
-        x_mul(3, 0, 0)
-        for tt in range(4):
-            if tt < 3:
-                x_turn(3, (tt + 1) // 2, (tt + 1) % 2)
-            o_mul(0, 0, tt)
-            if tt % 2 == 1:
-                o_store(0, 0, tt - 1, tt + 1)
-        o_inter(0, 0)
+        fill = o_fill(0, 0)
         for tt in range(1, 4):
-            x_mul(3, tt // 2, tt % 2)
-            mm2(0, 1, tt - 1)
-        mm2(0, 1, 3)
+            fill(tt)
+        x_quant(2)
+        d_alloc(2)
+        stage1(2, (0, 1))
+        d_subs(1)
+        d_inter(1)
+        stage1(2, (2, 3))
+        o_muls(0, 0, x_fill(3))
+        o_inter(0, 0)
+        for q in range(4):
+            labels(q, 1024, 2048)
+        x_muls(3, o_fill(0, 1))
         d_quant(1)
         x_quant(3)
         d_alloc(3)
-        for q in range(4):
-            labels(q, 1024, 2048)
-        o_alloc(1, 0)
-        o_alloc(1, 1)
-        for tt in range(4):
-            mm1(3, tt)
-            o_mul(0, 1, tt)
-            mm2(1, 0, tt)
-            if tt % 2 == 1:
-                o_store(0, 1, tt - 1, tt + 1)
-        for q in range(4):
-            d_sub(2, q)
-        o_inter(0, 1)
+        d_subs(2)
         d_inter(2)
-        for tt in range(4):
-            o_mul(1, 0, tt)
-            mm2(1, 1, tt)
-            if tt % 2 == 1:
-                o_store(1, 0, tt - 1, tt + 1)
+        stage1(3, (0, 1, 2))
+        o_muls(0, 1, o_fill(1, 0))
+        stage1(3, (3,))
+        o_pack(0, 0)
+        o_inter(0, 1)
+        o_muls(1, 0, o_fill(1, 1))
         o_inter(1, 0)
-        o_quant(0, 0)
-        code_store(0, 0)
-        for q in range(4):
-            d_sub(3, q)
         d_quant(2)
-        o_alloc(2, 0)
-        for tt in range(4):
-            o_mul(1, 1, tt)
-            mm2(2, 0, tt)
-            if tt % 2 == 1:
-                o_store(1, 1, tt - 1, tt + 1)
+        d_subs(3)
         d_inter(3)
+        o_muls(1, 1, o_fill(2, 0))
         o_inter(1, 1)
-        o_quant(0, 1)
-        code_store(0, 1)
-        o_alloc(2, 1)
-        for tt in range(4):
-            o_mul(2, 0, tt)
-            mm2(2, 1, tt)
-            if tt % 2 == 1:
-                o_store(2, 0, tt - 1, tt + 1)
+        o_pack(0, 1)
+        o_muls(2, 0, o_fill(2, 1))
         o_inter(2, 0)
         d_quant(3)
-        o_quant(1, 0)
-        code_store(1, 0)
+        o_pack(1, 0)
         c = NCH - 1
         o_alloc(c, 0)
-        for tt in range(4):
-            o_mul(2, 1, tt)
-            mm2(c, 0, tt, 0, 256)
-            if tt % 2 == 1:
-                o_store(2, 1, tt - 1, tt + 1)
-        o_inter(2, 1)
-        o_quant(1, 1)
-        code_store(1, 1)
         o_alloc(c, 1)
+        mm2_pair(c, 0, 0, 0)
+        o_muls(c - 1, 1, lambda i: mm2_pair(c, 0, i % 2, 256 * (i // 2)))
+        o_inter(c - 1, 1)
+        o_pack(c - 2, 1)
         for qt in range(4):
             dh, lo = qt // 2, 256 * (qt % 2)
-            for tt in range(4):
-                o_mul(c, dh, tt, lo, lo + 256)
-                if qt < 3:
-                    mm2(c, (qt + 1) // 2, tt, 256 * ((qt + 1) % 2), 256 * ((qt + 1) % 2) + 256)
+            for tp in (1, 0):
+                o_mul_pair(c, dh, tp, lo)
+            if qt < 2:
+                for tp in range(2):
+                    mm2_pair(c, 1, tp, lo)
             o_store(c, dh, 0, 4, lo, lo + 256)
             o_inter(c, dh, lo, lo + 256)
             if qt == 1:
-                o_quant(c - 1, 0)
-                code_store(c - 1, 0)
-        o_quant(c - 1, 1)
-        code_store(c - 1, 1)
-        o_quant(c, 0)
-        code_store(c, 0)
+                o_pack(c - 1, 0)
+        o_pack(c - 1, 1)
+        o_pack(c, 0)
         o_quant(c, 1, 0, 256)
         o_quant(c, 1, 256, 512)
         code_store(c, 1)

@@ -27,25 +27,26 @@ def tile_ordinaldepththresholdfeaturegradient_x1_kernel(tc, x, g, w, s, b, y, t,
         keep = ctx.enter_context(tc.tile_pool(name="keep", bufs=1))
         work = ctx.enter_context(tc.tile_pool(name="work", bufs=2))
         big = ctx.enter_context(tc.tile_pool(name="big", bufs=8))
-        outs = ctx.enter_context(tc.tile_pool(name="outs", bufs=4))
-        psum_v = ctx.enter_context(tc.psum_pool(name="psum_v", bufs=1))
-        psum_s = ctx.enter_context(tc.psum_pool(name="psum_s", bufs=3))
+        outs = ctx.enter_context(tc.tile_pool(name="outs", bufs=6))
+        psum = ctx.enter_context(tc.psum_pool(name="psum", bufs=1))
         ctx.enter_context(tc.manual_schedule())
 
-        v_free = list(range(5))
+        free = list(range(8))
 
-        def v_bank(shape):
-            i = v_free.pop(0)
-            return psum_v.tile(shape, F32, name="v_bank%d" % i), i
+        def take_bank(shape, dtype=F32):
+            i = free.pop(0)
+            return psum.tile(shape, dtype, name="bank%d" % i), i
 
         x_raw = {}
 
-        def x_load(c, tp0, tp1):
-            xr = keep.tile([P, 2 * (tp1 - tp0) * D], BF16, align_bytes=64, name="xr%d%d" % (c, tp0))
-            xv = x[c * CH : (c + 1) * CH, :].rearrange("(p t) d -> p (t d)", t=4)
-            nc.sync.dma_start(out=xr[:], in_=xv[:, 2 * tp0 * D : 2 * tp1 * D])
+        def x_load(c, tp0, tp1, h0=0, h1=NH):
+            nt, nd = 2 * (tp1 - tp0), 512 * (h1 - h0)
+            xr = keep.tile([P, nt, nd], BF16, align_bytes=64, name="xr%d%d%d" % (c, tp0, h0))
+            xv = x[c * CH : (c + 1) * CH, :].rearrange("(p t) d -> p t d", t=4)
+            nc.sync.dma_start(out=xr[:], in_=xv[:, 2 * tp0 : 2 * tp1, 512 * h0 : 512 * h1])
             for tp in range(tp0, tp1):
-                x_raw[(c, tp)] = xr[:, 2 * (tp - tp0) * D : 2 * (tp - tp0 + 1) * D]
+                for h in range(h0, h1):
+                    x_raw[(c, tp, h)] = xr[:].bitcast(F32)[:, 2 * (tp - tp0) : 2 * (tp - tp0 + 1), 256 * (h - h0) : 256 * (h - h0 + 1)]
 
         w_raw = {}
 
@@ -71,7 +72,7 @@ def tile_ordinaldepththresholdfeaturegradient_x1_kernel(tc, x, g, w, s, b, y, t,
             nc.scalar.dma_start(out=dst[:], in_=v.rearrange("(p i) -> p i", i=4))
 
         def s_widen():
-            nc.vector.tensor_copy(out=s32[:], in_=s_col[:])
+            nc.gpsimd.tensor_copy(out=s32[:], in_=s_col[:])
 
         warm = keep.tile([P, 1], F32, name="warm")
         warm2 = keep.tile([P, 1], F32, name="warm2")
@@ -91,12 +92,18 @@ def tile_ordinaldepththresholdfeaturegradient_x1_kernel(tc, x, g, w, s, b, y, t,
 
         y_bc = keep.tile([P, N], BF16, align_bytes=64, name="y_bc")
 
+        ys = {}
+
         def y_spread(hf):
-            yp = psum_s.tile([P, N // 2], BF16, name="s_bank")
+            yp, bank = take_bank([P, N // 2], BF16)
             for i in range(8):
                 j = hf * 8 + i
                 nc.tensor.transpose(yp[:, i * P : (i + 1) * P], y_col[:, j : j + 1].to_broadcast([P, P]), id16[:])
-            nc.scalar.copy(out=y_bc[:, hf * N // 2 : (hf + 1) * N // 2], in_=yp[:])
+            ys[hf] = (yp, bank)
+
+        def y_copy(hf):
+            nc.scalar.copy(out=y_bc[:, hf * N // 2 : (hf + 1) * N // 2], in_=ys[hf][0][:])
+            free.append(ys[hf][1])
 
         w_gr = big.tile([P, NH, K, 4], BF16, align_bytes=64, name="big")
         w_codes = keep.tile([P, NH, K], U32, align_bytes=64, name="w_codes")
@@ -124,11 +131,11 @@ def tile_ordinaldepththresholdfeaturegradient_x1_kernel(tc, x, g, w, s, b, y, t,
             xs[c] = [big.tile([P, NH, CH, 4], BF16, align_bytes=64, name="big")]
 
         def x_turn(c, tp, h):
-            words = x_raw[(c, tp)].bitcast(F32).rearrange("p (t d) -> p t d", t=2)
-            xt, bank = v_bank([P, 2, 256])
+            words = x_raw[(c, tp, h)]
+            xt, bank = take_bank([P, 2, 256])
             for tt in range(2):
                 for u in range(2):
-                    nc.tensor.transpose(xt[:, u, tt * P : (tt + 1) * P], words[:, tt, 256 * h + u : 256 * (h + 1) : 2], id32[:])
+                    nc.tensor.transpose(xt[:, u, tt * P : (tt + 1) * P], words[:, tt, u:256:2], id32[:])
             xts[(c, tp, h)] = (xt, bank)
 
         def x_mul(c, tp, h):
@@ -138,7 +145,7 @@ def tile_ordinaldepththresholdfeaturegradient_x1_kernel(tc, x, g, w, s, b, y, t,
                 in1=g4[:, h].unsqueeze(1).to_broadcast([P, 256, 2, 2]),
                 op=ALU.mult,
             )
-            v_free.append(xts[(c, tp, h)][1])
+            free.append(xts[(c, tp, h)][1])
 
         def x_quant(c):
             xs[c].append(work.tile([P, NH, CH], U32, align_bytes=64, name="x_codes"))
@@ -154,14 +161,20 @@ def tile_ordinaldepththresholdfeaturegradient_x1_kernel(tc, x, g, w, s, b, y, t,
         wt_codes = keep.tile([P, D], U32, align_bytes=64, name="wt_codes")
         wt_scales = keep.tile([P, D], U8, align_bytes=64, name="wt_scales")
 
+        wts = {}
+
         def wt_turn(h, jp):
             words = w_raw[h][:].bitcast(F32).rearrange("p (j k) -> p j k", j=4)
-            dst = wt_gr[:].rearrange("p d e -> p (d e)").bitcast(F32).rearrange("p (h m j u) -> p h m j u", h=NH, j=4, u=2)
-            wt = psum_s.tile([P, 2, 2, P], F32, name="s_bank")
+            wt, bank = take_bank([P, 2, 2, P])
             for jj in range(2):
                 for u in range(2):
                     nc.tensor.transpose(wt[:, jj, u, :], words[:, 2 * jp + jj, u : 256 : 2], id32[:])
-            nc.scalar.copy(out=dst[:, h, :, 2 * jp : 2 * jp + 2, :], in_=wt[:].rearrange("p j u m -> p m j u"))
+            wts[(h, jp)] = (wt, bank)
+
+        def wt_copy(h, jp):
+            dst = wt_gr[:].rearrange("p d e -> p (d e)").bitcast(F32).rearrange("p (h m j u) -> p h m j u", h=NH, j=4, u=2)
+            nc.scalar.copy(out=dst[:, h, :, 2 * jp : 2 * jp + 2, :], in_=wts[(h, jp)][0][:].rearrange("p j u m -> p m j u"))
+            free.append(wts[(h, jp)][1])
 
         def wt_quant(h0, h1):
             nc.vector.quantize_mx(
@@ -190,17 +203,13 @@ def tile_ordinaldepththresholdfeaturegradient_x1_kernel(tc, x, g, w, s, b, y, t,
         ds = {}
         zs = {}
 
-        def d_alloc(c):
-            ds[c] = dict(
-                sig=work.tile([P, 4, CH], F32, align_bytes=64, name="sig"),
-                d=work.tile([P, 4, CH], F32, align_bytes=64, name="d32"),
-                gr=work.tile([P, CH, 4], BF16, align_bytes=64, name="d_gr"),
-                codes=work.tile([P, CH], U32, align_bytes=64, name="d_codes"),
-                scales=work.tile([P, CH], U8, align_bytes=64, name="d_scales"),
-            )
+        def d_tile(c, name, shape, dtype):
+            if (c, name) not in ds:
+                ds[(c, name)] = work.tile(shape, dtype, align_bytes=64, name=name)
+            return ds[(c, name)]
 
         def mm1(c, q, lo=0, hi=CH):
-            z = psum_s.tile([P, hi - lo], F32, name="s_bank")
+            z, bank = take_bank([P, hi - lo])
             for h in range(NH):
                 nc.tensor.matmul_mx(
                     out=z[:],
@@ -211,22 +220,23 @@ def tile_ordinaldepththresholdfeaturegradient_x1_kernel(tc, x, g, w, s, b, y, t,
                     start=(h == 0),
                     stop=(h == NH - 1),
                 )
-            zs[(c, q)] = z
+            zs[(c, q)] = (z, bank)
 
         def sigm(c, q, lo=0, hi=CH):
             nc.scalar.activation(
-                out=ds[c]["sig"][:, q, lo:hi],
-                in_=zs[(c, q)][:],
+                out=d_tile(c, "sig", [P, 4, CH], F32)[:, q, lo:hi],
+                in_=zs[(c, q)][0][:],
                 func=ACT.Sigmoid,
                 bias=b_col[:, q : q + 1],
                 scale=s32[:, q : q + 1],
             )
+            free.append(zs[(c, q)][1])
 
         def d_sub(c, q, lo=0, hi=CH):
             nc.vector.scalar_tensor_tensor(
-                out=ds[c]["d"][:, q, lo:hi],
-                in0=ds[c]["sig"][:, q, lo:hi],
-                scalar=s32[:, q : q + 1],
+                out=d_tile(c, "d32", [P, 4, CH], F32)[:, q, lo:hi],
+                in0=ds[(c, "sig")][:, q, lo:hi],
+                scalar=s_col[:, q : q + 1],
                 in1=ls[:, q, c * CH + lo : c * CH + hi],
                 op0=ALU.mult,
                 op1=ALU.subtract,
@@ -241,14 +251,13 @@ def tile_ordinaldepththresholdfeaturegradient_x1_kernel(tc, x, g, w, s, b, y, t,
                 nc.scalar.copy(out=o, in_=i_)
 
         def d_inter(c, lo=0, hi=CH, on_vector=False):
-            inter(ds[c]["gr"], ds[c]["d"], lo, hi, on_vector)
+            inter(d_tile(c, "d_gr", [P, CH, 4], BF16), ds[(c, "d32")], lo, hi, on_vector)
 
         def d_quant(c, lo=0, hi=CH):
-            e = ds[c]
             nc.vector.quantize_mx(
-                out=e["codes"][:, lo:hi].bitcast(FP8X4),
-                scales=e["scales"][:, lo:hi],
-                in_=e["gr"][:, lo:hi, :].rearrange("p n j -> p (n j)"),
+                out=d_tile(c, "d_codes", [P, CH], U32)[:, lo:hi].bitcast(FP8X4),
+                scales=d_tile(c, "d_scales", [P, CH], U8)[:, lo:hi],
+                in_=ds[(c, "d_gr")][:, lo:hi, :].rearrange("p n j -> p (n j)"),
             )
 
         outp = {}
@@ -263,11 +272,11 @@ def tile_ordinaldepththresholdfeaturegradient_x1_kernel(tc, x, g, w, s, b, y, t,
             )
 
         def mm2(c, dh, tt, lo=0, hi=512):
-            o, bank = v_bank([P, hi - lo])
+            o, bank = take_bank([P, hi - lo])
             nc.tensor.matmul_mx(
                 out=o[:],
-                lhsT=ds[c]["codes"][:, tt * P : (tt + 1) * P].bitcast(FP8X4),
-                lhsT_scale=ds[c]["scales"][:, tt * P : (tt + 1) * P],
+                lhsT=ds[(c, "d_codes")][:, tt * P : (tt + 1) * P].bitcast(FP8X4),
+                lhsT_scale=ds[(c, "d_scales")][:, tt * P : (tt + 1) * P],
                 rhs=wt_codes[:, dh * 512 + lo : dh * 512 + hi].bitcast(FP8X4),
                 rhs_scale=wt_scales[:, dh * 512 + lo : dh * 512 + hi],
                 start=True,
@@ -279,16 +288,16 @@ def tile_ordinaldepththresholdfeaturegradient_x1_kernel(tc, x, g, w, s, b, y, t,
             nc.vector.tensor_tensor(
                 out=outp[(c, dh)]["o"][:, tt, lo:hi], in0=banks[(c, dh, tt, lo)][0][:], in1=g_bc[:, dh * 512 + lo : dh * 512 + hi], op=ALU.mult
             )
-            v_free.append(banks[(c, dh, tt, lo)][1])
+            free.append(banks[(c, dh, tt, lo)][1])
 
         def mm2_pair(c, dh, tp, lo):
-            o, bank = v_bank([P, 2, 256])
+            o, bank = take_bank([P, 2, 256])
             for tt in range(2):
                 cols = slice((2 * tp + tt) * P, (2 * tp + tt + 1) * P)
                 nc.tensor.matmul_mx(
                     out=o[:, tt, :],
-                    lhsT=ds[c]["codes"][:, cols].bitcast(FP8X4),
-                    lhsT_scale=ds[c]["scales"][:, cols],
+                    lhsT=ds[(c, "d_codes")][:, cols].bitcast(FP8X4),
+                    lhsT_scale=ds[(c, "d_scales")][:, cols],
                     rhs=wt_codes[:, dh * 512 + lo : dh * 512 + lo + 256].bitcast(FP8X4),
                     rhs_scale=wt_scales[:, dh * 512 + lo : dh * 512 + lo + 256],
                     start=True,
@@ -303,7 +312,7 @@ def tile_ordinaldepththresholdfeaturegradient_x1_kernel(tc, x, g, w, s, b, y, t,
                 in1=g_bc[:, dh * 512 + lo : dh * 512 + lo + 256].unsqueeze(1).to_broadcast([P, 2, 256]),
                 op=ALU.mult,
             )
-            v_free.append(banks[(c, dh, tp, lo)][1])
+            free.append(banks[(c, dh, tp, lo)][1])
 
         def o_store(c, dh, t0, t1, lo=0, hi=512):
             nc.sync.dma_start(
@@ -337,41 +346,41 @@ def tile_ordinaldepththresholdfeaturegradient_x1_kernel(tc, x, g, w, s, b, y, t,
         LAST_FIRST = (3, 2, 1, 0)
 
 
-        def x_muls(c, refill):
-            for j, i in enumerate(LAST_FIRST):
+        def x_turns(c, parts=range(4)):
+            for i in parts:
+                x_turn(c, i // 2, i % 2)
+
+
+        def x_muls(c):
+            for i in LAST_FIRST:
                 x_mul(c, i // 2, i % 2)
-                if j < 3:
-                    refill(j + 1)
 
 
-        def o_muls(c, dh, refill):
-            for j, tt in enumerate(LAST_FIRST):
+        def mm1s(c, qs=range(4)):
+            for q in qs:
+                mm1(c, q)
+
+
+        def sigms(c, qs=(1, 0, 3, 2)):
+            for q in qs:
+                sigm(c, q)
+
+
+        def mm2s(c, dh):
+            o_alloc(c, dh)
+            for tt in range(4):
+                mm2(c, dh, tt)
+
+
+        def o_muls(c, dh):
+            for tt in LAST_FIRST:
                 o_mul(c, dh, tt)
-                if j < 3:
-                    refill(j + 1)
                 if tt % 2 == 0:
                     o_store(c, dh, tt, tt + 2)
 
 
-        def x_fill(c):
-            x_turn(c, 0, 0)
-            return lambda i: x_turn(c, i // 2, i % 2)
-
-
-        def o_fill(c, dh):
-            o_alloc(c, dh)
-            mm2(c, dh, 0)
-            return lambda tt: mm2(c, dh, tt)
-
-
-        def stage1(c, qs):
-            for q in qs:
-                mm1(c, q)
-                sigm(c, q)
-
-
         def d_subs(c):
-            for q in LAST_FIRST:
+            for q in (2, 3, 1, 0):
                 d_sub(c, q)
 
 
@@ -380,113 +389,128 @@ def tile_ordinaldepththresholdfeaturegradient_x1_kernel(tc, x, g, w, s, b, y, t,
             code_store(c, dh)
 
 
-        x_load(0, 0, 1)
+        x_load(0, 0, 1, 0, 1)
         g_load()
-        x_load(0, 1, 2)
+        x_load(0, 0, 1, 1, 2)
         y_load()
-        w_load(0)
+        x_load(0, 1, 2)
         col_load(s_col, s)
-        w_load(1)
+        w_load(0)
         col_load(t_col, t)
+        w_load(1)
+        x_load(1, 0, 1)
         col_load(b_col, b)
-        for c in range(1, NCH):
+        x_load(1, 1, 2)
+        for c in range(2, NCH):
             x_load(c, 0, 2)
         g_spread()
         warm_up()
         identities()
         for c in range(NCH):
             x_alloc(c)
-        for i in range(4):
-            x_turn(0, i // 2, i % 2)
-        for i in (0, 1, 3, 2):
-            x_mul(0, i // 2, i % 2)
-        w_inter(0, False, 0, 32)
+        s_widen()
+        x_turns(0, (0,))
         y_spread(0)
+        x_turns(0, (1, 2, 3))
+        y_copy(0)
+        x_mul(0, 0, 0)
+        labels(0, 0, 1024)
+        x_mul(0, 0, 1)
+        for q in range(1, 4):
+            labels(q, 0, 1024)
+        x_mul(0, 1, 1)
+        x_mul(0, 1, 0)
         wt_turn(0, 0)
-        w_inter(0, False, 32, 64)
         wt_turn(0, 1)
         wt_turn(1, 0)
-        s_widen()
-        w_inter(1, True)
+        w_inter(0, False)
+        w_inter(1, False, 0, 24)
+        wt_copy(0, 1)
+        wt_copy(0, 0)
+        w_inter(1, True, 24, 64)
+        wt_copy(1, 0)
         x_quant(0)
-        for i in range(4):
-            x_turn(1, i // 2, i % 2)
+        x_turns(1)
+        y_spread(1)
+        y_copy(1)
         w_quant(0, 2)
-        for q in range(4):
-            labels(q, 0, 1024)
+        mm1s(0, (0, 1, 2))
+        x_muls(1)
+        mm1s(0, (3,))
         wt_turn(1, 1)
-        d_alloc(0)
-        stage1(0, range(4))
-        x_muls(1, x_fill(2))
+        sigms(0, (0, 1, 3, 2))
+        wt_copy(1, 1)
+        x_turns(2, (0, 1))
         wt_quant(0, 1)
         x_quant(1)
-        d_alloc(1)
-        stage1(1, (0,))
-        d_subs(0)
-        d_inter(0)
-        stage1(1, (1, 2, 3))
-        y_spread(1)
-        x_muls(2, lambda i: None)
-        wt_quant(1, 2)
-        d_quant(0)
-        fill = o_fill(0, 0)
-        for tt in range(1, 4):
-            fill(tt)
-        x_quant(2)
-        d_alloc(2)
-        stage1(2, (0, 1))
-        d_subs(1)
-        d_inter(1)
-        stage1(2, (2, 3))
-        o_muls(0, 0, x_fill(3))
-        o_inter(0, 0)
+        mm1s(1, (0, 1))
+        x_turns(2, (2, 3))
+        mm1s(1, (2, 3))
+        sigms(1, (1, 0))
         for q in range(4):
             labels(q, 1024, 2048)
-        x_muls(3, o_fill(0, 1))
-        d_quant(1)
-        x_quant(3)
-        d_alloc(3)
-        d_subs(2)
-        d_inter(2)
-        stage1(3, (0, 1, 2))
-        o_muls(0, 1, o_fill(1, 0))
-        stage1(3, (3,))
-        o_pack(0, 0)
+        d_subs(0)
+        d_inter(0)
+        sigms(1, (3, 2))
+        x_muls(2)
+        wt_quant(1, 2)
+        d_quant(0)
+        x_quant(2)
+        mm2s(0, 0)
+        mm1s(2)
+        d_subs(1)
+        sigms(2)
+        d_inter(1)
+        o_muls(0, 0)
+        mm2s(0, 1)
+        o_inter(0, 0)
+        o_muls(0, 1)
+        x_turns(3)
         o_inter(0, 1)
-        o_muls(1, 0, o_fill(1, 1))
+        d_quant(1)
+        mm2s(1, 0)
+        x_muls(3)
+        o_pack(0, 0)
+        x_quant(3)
+        mm1s(3)
+        d_subs(2)
+        sigms(3)
+        d_inter(2)
+        o_muls(1, 0)
+        mm2s(1, 1)
         o_inter(1, 0)
-        d_quant(2)
+        o_pack(0, 1)
         d_subs(3)
         d_inter(3)
-        o_muls(1, 1, o_fill(2, 0))
+        d_quant(2)
+        mm2s(2, 0)
+        o_muls(1, 1)
+        mm2s(2, 1)
         o_inter(1, 1)
-        o_pack(0, 1)
-        o_muls(2, 0, o_fill(2, 1))
+        o_muls(2, 0)
         o_inter(2, 0)
         d_quant(3)
         o_pack(1, 0)
         c = NCH - 1
         o_alloc(c, 0)
         o_alloc(c, 1)
-        mm2_pair(c, 0, 0, 0)
-        o_muls(c - 1, 1, lambda i: mm2_pair(c, 0, i % 2, 256 * (i // 2)))
-        o_inter(c - 1, 1)
-        o_pack(c - 2, 1)
-        for qt in range(4):
-            dh, lo = qt // 2, 256 * (qt % 2)
-            for tp in (1, 0):
-                o_mul_pair(c, dh, tp, lo)
-            if qt < 2:
-                for tp in range(2):
-                    mm2_pair(c, 1, tp, lo)
-            o_store(c, dh, 0, 4, lo, lo + 256)
-            o_inter(c, dh, lo, lo + 256)
-            if qt == 1:
-                o_pack(c - 1, 0)
-        o_pack(c - 1, 1)
+        for i in range(4):
+            mm2_pair(c, 0, i % 2, 256 * (i // 2))
+        o_muls(2, 1)
+        for i in range(4):
+            mm2_pair(c, 1, i % 2, 256 * (i // 2))
+        o_inter(2, 1)
+        o_pack(1, 1)
+        for dh in range(2):
+            for lo in (256, 0):
+                for tp in (1, 0):
+                    o_mul_pair(c, dh, tp, lo)
+                o_store(c, dh, 0, 4, lo, lo + 256)
+                o_inter(c, dh, lo, lo + 256)
+            o_pack(c - 1, dh)
         o_pack(c, 0)
-        o_quant(c, 1, 0, 256)
         o_quant(c, 1, 256, 512)
+        o_quant(c, 1, 0, 256)
         code_store(c, 1)
         for qd in range(4):
             scale_store(qd, nc.scalar if qd % 2 else nc.sync)

@@ -55,24 +55,25 @@ def tile_ordinaldepththresholdfeaturegradient_x1_kernel(tc, x, g, w, s, b, y, t,
             nc.sync.dma_start(out=wr[:], in_=w[h * 512 : (h + 1) * 512, :].rearrange("(p j) k -> p (j k)", j=4))
             w_raw[h] = wr
 
-        g_col = keep.tile([P, 8], BF16, align_bytes=64, name="g_col")
-        y_col = keep.tile([P, 16], BF16, align_bytes=64, name="y_col")
-        t_col = keep.tile([P, 4], BF16, align_bytes=64, name="t_col")
-        s_col = keep.tile([P, 4], BF16, align_bytes=64, name="s_col")
-        b_col = keep.tile([P, 4], BF16, align_bytes=64, name="b_col")
+        rows = keep.tile([P, 512], BF16, align_bytes=64, name="rows")
+        cols = keep.tile([P, 9, 4], BF16, align_bytes=64, name="cols")
         s32 = keep.tile([P, 4], F32, align_bytes=64, name="s32")
+        g_col, s_col, b_col, t_col, y_col = cols[:, 0:2], cols[:, 2], cols[:, 3], cols[:, 4], cols[:, 5:9]
 
-        def g_load():
-            nc.scalar.dma_start(out=g_col[:].rearrange("p (h i) -> p h i", h=NH), in_=g.rearrange("(h p i) -> p h i", h=NH, i=4))
+        def row_loads():
+            nc.vector.memset(rows[:].bitcast(U32), 0)
+            for r0, r1, v in ((0, 2, g), (5, 9, y), (4, 5, t), (2, 3, s), (3, 4, b)):
+                nc.sync.dma_start(out=rows[r0:r1, :], in_=v.rearrange("(r k) -> r k", k=512))
 
-        def y_load():
-            nc.scalar.dma_start(out=y_col[:].rearrange("p (c i) -> p c i", c=NCH), in_=y.rearrange("(c p i) -> p c i", c=NCH, i=4))
-
-        def col_load(dst, v):
-            nc.scalar.dma_start(out=dst[:], in_=v.rearrange("(p i) -> p i", i=4))
+        def rows_turn():
+            bank_tile, bank = take_bank([P, 2, P])
+            for u in range(2):
+                nc.tensor.transpose(bank_tile[:, u, :], rows[:].bitcast(F32)[:, u:256:2], id32[:])
+            nc.vector.tensor_copy(out=cols[:].bitcast(F32), in_=bank_tile[:, :, 0:9].rearrange("p u r -> p r u"))
+            free.append(bank)
 
         def s_widen():
-            nc.gpsimd.tensor_copy(out=s32[:], in_=s_col[:])
+            nc.vector.tensor_copy(out=s32[:], in_=s_col)
 
         warm = keep.tile([P, 1], F32, name="warm")
         warm2 = keep.tile([P, 1], F32, name="warm2")
@@ -88,7 +89,7 @@ def tile_ordinaldepththresholdfeaturegradient_x1_kernel(tc, x, g, w, s, b, y, t,
             make_identity(nc, id32[:])
             make_identity(nc, id16[:])
 
-        g4 = g_col[:].rearrange("p (h u e) -> p h u e", h=NH, u=2)
+        g4 = g_col.rearrange("p h (u e) -> p h u e", u=2)
 
         y_bc = keep.tile([P, N], BF16, align_bytes=64, name="y_bc")
 
@@ -98,7 +99,7 @@ def tile_ordinaldepththresholdfeaturegradient_x1_kernel(tc, x, g, w, s, b, y, t,
             yp, bank = take_bank([P, N // 2], BF16)
             for i in range(8):
                 j = hf * 8 + i
-                nc.tensor.transpose(yp[:, i * P : (i + 1) * P], y_col[:, j : j + 1].to_broadcast([P, P]), id16[:])
+                nc.tensor.transpose(yp[:, i * P : (i + 1) * P], y_col[:, j // 4, j % 4 : j % 4 + 1].to_broadcast([P, P]), id16[:])
             ys[hf] = (yp, bank)
 
         def y_copy(hf):
@@ -147,14 +148,15 @@ def tile_ordinaldepththresholdfeaturegradient_x1_kernel(tc, x, g, w, s, b, y, t,
             )
             free.append(xts[(c, tp, h)][1])
 
-        def x_quant(c):
-            xs[c].append(work.tile([P, NH, CH], U32, align_bytes=64, name="x_codes"))
-            xs[c].append(work.tile([P, NH, CH], U8, align_bytes=64, name="x_scales"))
+        def x_quant(c, h0=0, h1=NH):
+            if h0 == 0:
+                xs[c].append(work.tile([P, NH, CH], U32, align_bytes=64, name="x_codes"))
+                xs[c].append(work.tile([P, NH, CH], U8, align_bytes=64, name="x_scales"))
             gr, codes, scales = xs[c]
             nc.vector.quantize_mx(
-                out=codes[:].rearrange("p h n -> p (h n)").bitcast(FP8X4),
-                scales=scales[:].rearrange("p h n -> p (h n)"),
-                in_=gr[:].rearrange("p h n j -> p (h n j)"),
+                out=codes[:, h0:h1].rearrange("p h n -> p (h n)").bitcast(FP8X4),
+                scales=scales[:, h0:h1].rearrange("p h n -> p (h n)"),
+                in_=gr[:, h0:h1].rearrange("p h n j -> p (h n j)"),
             )
 
         wt_gr = big.tile([P, D, 4], BF16, align_bytes=64, name="big")
@@ -208,19 +210,19 @@ def tile_ordinaldepththresholdfeaturegradient_x1_kernel(tc, x, g, w, s, b, y, t,
                 ds[(c, name)] = work.tile(shape, dtype, align_bytes=64, name=name)
             return ds[(c, name)]
 
-        def mm1(c, q, lo=0, hi=CH):
-            z, bank = take_bank([P, hi - lo])
-            for h in range(NH):
+        def mm1(c, q, passes=range(NH)):
+            if (c, q) not in zs:
+                zs[(c, q)] = take_bank([P, CH])
+            for h in passes:
                 nc.tensor.matmul_mx(
-                    out=z[:],
+                    out=zs[(c, q)][0][:],
                     lhsT=w_codes[:, h, q * P : (q + 1) * P].bitcast(FP8X4),
                     lhsT_scale=w_scales[:, h, q * P : (q + 1) * P],
-                    rhs=xs[c][1][:, h, lo:hi].bitcast(FP8X4),
-                    rhs_scale=xs[c][2][:, h, lo:hi],
+                    rhs=xs[c][1][:, h].bitcast(FP8X4),
+                    rhs_scale=xs[c][2][:, h],
                     start=(h == 0),
                     stop=(h == NH - 1),
                 )
-            zs[(c, q)] = (z, bank)
 
         def sigm(c, q, lo=0, hi=CH):
             nc.scalar.activation(
@@ -240,6 +242,18 @@ def tile_ordinaldepththresholdfeaturegradient_x1_kernel(tc, x, g, w, s, b, y, t,
                 in1=ls[:, q, c * CH + lo : c * CH + hi],
                 op0=ALU.mult,
                 op1=ALU.subtract,
+            )
+
+        def d_scale(c, q):
+            sig = ds[(c, "sig")]
+            nc.scalar.activation(out=sig[:, q, :], in_=sig[:, q, :], func=ACT.Copy, scale=s32[:, q : q + 1])
+
+        def d_sub_pool(c, lo, hi):
+            nc.gpsimd.tensor_tensor(
+                out=d_tile(c, "d_gr", [P, CH, 4], BF16)[:, lo:hi, :],
+                in0=ds[(c, "sig")][:, :, lo:hi].rearrange("p q n -> p n q"),
+                in1=ls[:, :, c * CH + lo : c * CH + hi].rearrange("p q n -> p n q"),
+                op=ALU.subtract,
             )
 
         def inter(dst, src, lo, hi, on_vector):
@@ -379,6 +393,16 @@ def tile_ordinaldepththresholdfeaturegradient_x1_kernel(tc, x, g, w, s, b, y, t,
                     o_store(c, dh, tt, tt + 2)
 
 
+        def d_scales(c, qs=(1, 0, 3, 2)):
+            for q in qs:
+                d_scale(c, q)
+
+
+        def d_pool(c):
+            for tt in range(4):
+                d_sub_pool(c, tt * P, (tt + 1) * P)
+
+
         def d_subs(c):
             for q in (2, 3, 1, 0):
                 d_sub(c, q)
@@ -390,16 +414,12 @@ def tile_ordinaldepththresholdfeaturegradient_x1_kernel(tc, x, g, w, s, b, y, t,
 
 
         x_load(0, 0, 1, 0, 1)
-        g_load()
         x_load(0, 0, 1, 1, 2)
-        y_load()
+        row_loads()
         x_load(0, 1, 2)
-        col_load(s_col, s)
         w_load(0)
-        col_load(t_col, t)
         w_load(1)
         x_load(1, 0, 1)
-        col_load(b_col, b)
         x_load(1, 1, 2)
         for c in range(2, NCH):
             x_load(c, 0, 2)
@@ -408,78 +428,80 @@ def tile_ordinaldepththresholdfeaturegradient_x1_kernel(tc, x, g, w, s, b, y, t,
         identities()
         for c in range(NCH):
             x_alloc(c)
+        rows_turn()
         s_widen()
-        x_turns(0, (0,))
+        x_turns(0)
         y_spread(0)
-        x_turns(0, (1, 2, 3))
-        y_copy(0)
         x_mul(0, 0, 0)
-        labels(0, 0, 1024)
         x_mul(0, 0, 1)
-        for q in range(1, 4):
-            labels(q, 0, 1024)
-        x_mul(0, 1, 1)
+        w_inter(0, False)
+        y_copy(0)
+        w_inter(1, True)
         x_mul(0, 1, 0)
+        x_mul(0, 1, 1)
+        x_turns(1)
+        for h in range(NH):
+            w_quant(h, h + 1)
+            x_quant(0, h, h + 1)
+            for q in range(4 - 2 * h):
+                mm1(0, q, (h,))
+        x_muls(1)
         wt_turn(0, 0)
         wt_turn(0, 1)
+        for q in (2, 3):
+            mm1(0, q, (1,))
         wt_turn(1, 0)
-        w_inter(0, False)
-        w_inter(1, False, 0, 24)
-        wt_copy(0, 1)
-        wt_copy(0, 0)
-        w_inter(1, True, 24, 64)
-        wt_copy(1, 0)
-        x_quant(0)
-        x_turns(1)
-        y_spread(1)
-        y_copy(1)
-        w_quant(0, 2)
-        mm1s(0, (0, 1, 2))
-        x_muls(1)
-        mm1s(0, (3,))
         wt_turn(1, 1)
-        sigms(0, (0, 1, 3, 2))
-        wt_copy(1, 1)
-        x_turns(2, (0, 1))
-        wt_quant(0, 1)
+        sigms(0, (1, 0))
+        wt_copy(0, 0)
+        sigms(0, (3, 2))
+        for i in (1, 3, 2):
+            wt_copy(i // 2, i % 2)
+        for q in LAST_FIRST:
+            labels(q, 0, 1024)
         x_quant(1)
         mm1s(1, (0, 1))
+        x_turns(2, (0, 1))
+        mm1s(1, (2,))
         x_turns(2, (2, 3))
-        mm1s(1, (2, 3))
+        mm1s(1, (3,))
+        for q in (0, 1, 3, 2):
+            d_sub(0, q)
         sigms(1, (1, 0))
-        for q in range(4):
-            labels(q, 1024, 2048)
-        d_subs(0)
         d_inter(0)
         sigms(1, (3, 2))
-        x_muls(2)
-        wt_quant(1, 2)
+        wt_quant(0, 2)
+        for i in (1, 0, 3, 2):
+            x_mul(2, i // 2, i % 2)
+        y_spread(1)
+        y_copy(1)
         d_quant(0)
         x_quant(2)
         mm2s(0, 0)
         mm1s(2)
         d_subs(1)
-        sigms(2)
-        d_inter(1)
         o_muls(0, 0)
         mm2s(0, 1)
-        o_inter(0, 0)
-        o_muls(0, 1)
+        sigms(2)
+        d_inter(1)
         x_turns(3)
+        o_inter(0, 0)
+        for q in range(4):
+            labels(q, 1024, 2048)
+        o_muls(0, 1)
         o_inter(0, 1)
+        x_muls(3)
         d_quant(1)
         mm2s(1, 0)
-        x_muls(3)
-        o_pack(0, 0)
         x_quant(3)
         mm1s(3)
         d_subs(2)
-        sigms(3)
-        d_inter(2)
         o_muls(1, 0)
         mm2s(1, 1)
+        sigms(3)
+        d_inter(2)
         o_inter(1, 0)
-        o_pack(0, 1)
+        o_pack(0, 0)
         d_subs(3)
         d_inter(3)
         d_quant(2)
@@ -487,6 +509,7 @@ def tile_ordinaldepththresholdfeaturegradient_x1_kernel(tc, x, g, w, s, b, y, t,
         o_muls(1, 1)
         mm2s(2, 1)
         o_inter(1, 1)
+        o_pack(0, 1)
         o_muls(2, 0)
         o_inter(2, 0)
         d_quant(3)

@@ -55,25 +55,18 @@ def tile_ordinaldepththresholdfeaturegradient_x1_kernel(tc, x, g, w, s, b, y, t,
             nc.sync.dma_start(out=wr[:], in_=w[h * 512 : (h + 1) * 512, :].rearrange("(p j) k -> p (j k)", j=4))
             w_raw[h] = wr
 
-        rows = keep.tile([P, 512], BF16, align_bytes=64, name="rows")
-        cols = keep.tile([P, 9, 4], BF16, align_bytes=64, name="cols")
+        g_col = keep.tile([P, NH, 4], BF16, align_bytes=64, name="g_col")
+        y_col = keep.tile([P, NCH, 4], BF16, align_bytes=64, name="y_col")
+        t_col = keep.tile([P, 4], BF16, align_bytes=64, name="t_col")
+        s_col = keep.tile([P, 4], BF16, align_bytes=64, name="s_col")
+        b_col = keep.tile([P, 4], BF16, align_bytes=64, name="b_col")
         s32 = keep.tile([P, 4], F32, align_bytes=64, name="s32")
-        g_col, s_col, b_col, t_col, y_col = cols[:, 0:2], cols[:, 2], cols[:, 3], cols[:, 4], cols[:, 5:9]
 
-        def row_loads():
-            nc.vector.memset(rows[:].bitcast(U32), 0)
-            for r0, r1, v in ((0, 2, g), (5, 9, y), (4, 5, t), (2, 3, s), (3, 4, b)):
-                nc.sync.dma_start(out=rows[r0:r1, :], in_=v.rearrange("(r k) -> r k", k=512))
-
-        def rows_turn():
-            bank_tile, bank = take_bank([P, 2, P])
-            for u in range(2):
-                nc.tensor.transpose(bank_tile[:, u, :], rows[:].bitcast(F32)[:, u:256:2], id32[:])
-            nc.vector.tensor_copy(out=cols[:].bitcast(F32), in_=bank_tile[:, :, 0:9].rearrange("p u r -> p r u"))
-            free.append(bank)
+        def col_load(dst, v):
+            nc.scalar.dma_start(out=dst, in_=v.rearrange("(a p i) -> p a i", p=P, i=4))
 
         def s_widen():
-            nc.vector.tensor_copy(out=s32[:], in_=s_col)
+            nc.scalar.copy(out=s32[:], in_=s_col[:])
 
         warm = keep.tile([P, 1], F32, name="warm")
         warm2 = keep.tile([P, 1], F32, name="warm2")
@@ -89,7 +82,7 @@ def tile_ordinaldepththresholdfeaturegradient_x1_kernel(tc, x, g, w, s, b, y, t,
             make_identity(nc, id32[:])
             make_identity(nc, id16[:])
 
-        g4 = g_col.rearrange("p h (u e) -> p h u e", u=2)
+        g4 = g_col[:].rearrange("p h (u e) -> p h u e", u=2)
 
         y_bc = keep.tile([P, N], BF16, align_bytes=64, name="y_bc")
 
@@ -413,14 +406,16 @@ def tile_ordinaldepththresholdfeaturegradient_x1_kernel(tc, x, g, w, s, b, y, t,
             code_store(c, dh)
 
 
-        x_load(0, 0, 1, 0, 1)
-        x_load(0, 0, 1, 1, 2)
-        row_loads()
+        x_load(0, 0, 1)
+        col_load(g_col[:], g)
         x_load(0, 1, 2)
+        col_load(t_col[:].unsqueeze(1), t)
         w_load(0)
+        col_load(s_col[:].unsqueeze(1), s)
         w_load(1)
-        x_load(1, 0, 1)
-        x_load(1, 1, 2)
+        col_load(y_col[:], y)
+        x_load(1, 0, 2)
+        col_load(b_col[:].unsqueeze(1), b)
         for c in range(2, NCH):
             x_load(c, 0, 2)
         g_spread()
@@ -428,81 +423,72 @@ def tile_ordinaldepththresholdfeaturegradient_x1_kernel(tc, x, g, w, s, b, y, t,
         identities()
         for c in range(NCH):
             x_alloc(c)
-        rows_turn()
-        s_widen()
         x_turns(0)
-        y_spread(0)
-        x_mul(0, 0, 0)
-        x_mul(0, 0, 1)
+        for i in (0, 1, 3, 2):
+            x_mul(0, i // 2, i % 2)
+        s_widen()
         w_inter(0, False)
-        y_copy(0)
-        w_inter(1, True)
-        x_mul(0, 1, 0)
-        x_mul(0, 1, 1)
-        x_turns(1)
-        for h in range(NH):
-            w_quant(h, h + 1)
-            x_quant(0, h, h + 1)
-            for q in range(4 - 2 * h):
-                mm1(0, q, (h,))
-        x_muls(1)
         wt_turn(0, 0)
         wt_turn(0, 1)
-        for q in (2, 3):
-            mm1(0, q, (1,))
+        y_spread(0)
         wt_turn(1, 0)
         wt_turn(1, 1)
-        sigms(0, (1, 0))
-        wt_copy(0, 0)
-        sigms(0, (3, 2))
-        for i in (1, 3, 2):
+        y_spread(1)
+        y_copy(0)
+        for i in (1, 0, 3, 2):
             wt_copy(i // 2, i % 2)
+        y_copy(1)
+        w_inter(1, True)
+        x_turns(1)
+        x_quant(0)
+        w_quant(0, 2)
+        mm1s(0, (0, 1, 2))
         for q in LAST_FIRST:
             labels(q, 0, 1024)
+        x_muls(1)
+        x_turns(2, (0, 1))
+        mm1s(0, (3,))
+        x_turns(2, (2, 3))
+        sigms(0, range(4))
+        wt_quant(0, 2)
         x_quant(1)
         mm1s(1, (0, 1))
-        x_turns(2, (0, 1))
-        mm1s(1, (2,))
-        x_turns(2, (2, 3))
-        mm1s(1, (3,))
-        for q in (0, 1, 3, 2):
+        x_turns(3, (0, 1))
+        for q in (2, 1, 0, 3):
             d_sub(0, q)
-        sigms(1, (1, 0))
         d_inter(0)
-        sigms(1, (3, 2))
-        wt_quant(0, 2)
-        for i in (1, 0, 3, 2):
-            x_mul(2, i // 2, i % 2)
-        y_spread(1)
-        y_copy(1)
+        x_muls(2)
+        mm1s(1, (2, 3))
+        sigms(1)
+        x_turns(3, (2, 3))
+        for q in LAST_FIRST:
+            labels(q, 1024, 2048)
         d_quant(0)
-        x_quant(2)
         mm2s(0, 0)
+        x_quant(2)
+        x_muls(3)
         mm1s(2)
         d_subs(1)
+        sigms(2, (1, 0))
+        d_inter(1)
+        sigms(2, (3, 2))
+        x_quant(3)
         o_muls(0, 0)
         mm2s(0, 1)
-        sigms(2)
-        d_inter(1)
-        x_turns(3)
-        o_inter(0, 0)
-        for q in range(4):
-            labels(q, 1024, 2048)
-        o_muls(0, 1)
-        o_inter(0, 1)
-        x_muls(3)
-        d_quant(1)
-        mm2s(1, 0)
-        x_quant(3)
         mm1s(3)
+        o_inter(0, 0)
+        d_quant(1)
         d_subs(2)
-        o_muls(1, 0)
-        mm2s(1, 1)
+        o_muls(0, 1)
+        mm2s(1, 0)
         sigms(3)
         d_inter(2)
-        o_inter(1, 0)
+        o_inter(0, 1)
         o_pack(0, 0)
+        o_muls(1, 0)
+        mm2s(1, 1)
         d_subs(3)
+        o_inter(1, 0)
         d_inter(3)
         d_quant(2)
         mm2s(2, 0)

@@ -27,7 +27,7 @@ def tile_ordinaldepththresholdfeaturegradient_x1_kernel(tc, x, g, w, s, b, y, t,
         keep = ctx.enter_context(tc.tile_pool(name="keep", bufs=1))
         work = ctx.enter_context(tc.tile_pool(name="work", bufs=2))
         big = ctx.enter_context(tc.tile_pool(name="big", bufs=8))
-        outs = ctx.enter_context(tc.tile_pool(name="outs", bufs=6))
+        outs = ctx.enter_context(tc.tile_pool(name="outs", bufs=7))
         psum = ctx.enter_context(tc.psum_pool(name="psum", bufs=1))
         ctx.enter_context(tc.manual_schedule())
 
@@ -200,7 +200,8 @@ def tile_ordinaldepththresholdfeaturegradient_x1_kernel(tc, x, g, w, s, b, y, t,
 
         def d_tile(c, name, shape, dtype):
             if (c, name) not in ds:
-                ds[(c, name)] = work.tile(shape, dtype, align_bytes=64, name=name)
+                pool = keep if name == "d_gr" else work
+                ds[(c, name)] = pool.tile(shape, dtype, align_bytes=64, name=name)
             return ds[(c, name)]
 
         def mm1(c, q, passes=range(NH)):
@@ -237,9 +238,9 @@ def tile_ordinaldepththresholdfeaturegradient_x1_kernel(tc, x, g, w, s, b, y, t,
                 op1=ALU.subtract,
             )
 
-        def d_scale(c, q):
+        def d_scale(c, q, hi):
             sig = ds[(c, "sig")]
-            nc.scalar.activation(out=sig[:, q, :], in_=sig[:, q, :], func=ACT.Copy, scale=s32[:, q : q + 1])
+            nc.scalar.activation(out=sig[:, q, :hi], in_=sig[:, q, :hi], func=ACT.Copy, scale=s32[:, q : q + 1])
 
         def d_sub_pool(c, lo, hi):
             nc.gpsimd.tensor_tensor(
@@ -351,6 +352,7 @@ def tile_ordinaldepththresholdfeaturegradient_x1_kernel(tc, x, g, w, s, b, y, t,
             )
 
         LAST_FIRST = (3, 2, 1, 0)
+        POOL_COLS = 384
 
 
         def x_turns(c, parts=range(4)):
@@ -386,19 +388,19 @@ def tile_ordinaldepththresholdfeaturegradient_x1_kernel(tc, x, g, w, s, b, y, t,
                     o_store(c, dh, tt, tt + 2)
 
 
-        def d_scales(c, qs=(1, 0, 3, 2)):
-            for q in qs:
-                d_scale(c, q)
+        def d_scales(c):
+            for q in (2, 3, 1, 0):
+                d_scale(c, q, POOL_COLS)
 
 
         def d_pool(c):
-            for tt in range(4):
-                d_sub_pool(c, tt * P, (tt + 1) * P)
+            for lo in range(0, POOL_COLS, P):
+                d_sub_pool(c, lo, lo + P)
 
 
         def d_subs(c):
             for q in (2, 3, 1, 0):
-                d_sub(c, q)
+                d_sub(c, q, POOL_COLS, CH)
 
 
         def o_pack(c, dh):
@@ -456,50 +458,61 @@ def tile_ordinaldepththresholdfeaturegradient_x1_kernel(tc, x, g, w, s, b, y, t,
         x_turns(3, (0, 1))
         for q in (2, 1, 0, 3):
             d_sub(0, q)
+        sigms(1, (1, 0))
         d_inter(0)
         x_muls(2)
         mm1s(1, (2, 3))
-        sigms(1)
+        sigms(1, (3, 2))
         x_turns(3, (2, 3))
         for q in LAST_FIRST:
             labels(q, 1024, 2048)
         d_quant(0)
         mm2s(0, 0)
         x_quant(2)
+        d_subs(1)
+        d_scales(1)
+        d_inter(1, POOL_COLS, CH)
+        d_pool(1)
         x_muls(3)
         mm1s(2)
-        d_subs(1)
-        sigms(2, (1, 0))
-        d_inter(1)
-        sigms(2, (3, 2))
-        x_quant(3)
+        sigms(2)
+        d_scales(2)
         o_muls(0, 0)
         mm2s(0, 1)
-        mm1s(3)
         o_inter(0, 0)
-        d_quant(1)
+        x_quant(3)
+        mm1s(3, (0, 1))
         d_subs(2)
+        d_quant(1)
+        d_pool(2)
+        o_alloc(1, 0)
+        mm2(1, 0, 0)
+        mm2(1, 0, 1)
         o_muls(0, 1)
-        mm2s(1, 0)
+        mm2(1, 0, 2)
+        mm2(1, 0, 3)
+        mm1s(3, (2, 3))
+        d_inter(2, POOL_COLS, CH)
         sigms(3)
-        d_inter(2)
+        d_scales(3)
         o_inter(0, 1)
-        o_pack(0, 0)
         o_muls(1, 0)
         mm2s(1, 1)
         d_subs(3)
-        o_inter(1, 0)
-        d_inter(3)
+        o_pack(0, 0)
         d_quant(2)
+        d_pool(3)
         mm2s(2, 0)
+        d_inter(3, POOL_COLS, CH)
+        o_inter(1, 0)
         o_muls(1, 1)
         mm2s(2, 1)
         o_inter(1, 1)
-        o_pack(0, 1)
         o_muls(2, 0)
         o_inter(2, 0)
-        d_quant(3)
+        o_pack(0, 1)
         o_pack(1, 0)
+        d_quant(3)
         c = NCH - 1
         o_alloc(c, 0)
         o_alloc(c, 1)
@@ -515,11 +528,12 @@ def tile_ordinaldepththresholdfeaturegradient_x1_kernel(tc, x, g, w, s, b, y, t,
                 for tp in (1, 0):
                     o_mul_pair(c, dh, tp, lo)
                 o_store(c, dh, 0, 4, lo, lo + 256)
-                o_inter(c, dh, lo, lo + 256)
+                if dh == 0:
+                    o_inter(c, dh, lo, lo + 256)
             o_pack(c - 1, dh)
+        o_inter(c, 1, 384, 512)
+        o_inter(c, 1, 0, 384, True)
         o_pack(c, 0)
-        o_quant(c, 1, 256, 512)
-        o_quant(c, 1, 0, 256)
-        code_store(c, 1)
+        o_pack(c, 1)
         for qd in range(4):
             scale_store(qd, nc.scalar if qd % 2 else nc.sync)

@@ -27,7 +27,7 @@ def tile_ordinaldepththresholdfeaturegradient_x1_kernel(tc, x, g, w, s, b, y, t,
         keep = ctx.enter_context(tc.tile_pool(name="keep", bufs=1))
         work = ctx.enter_context(tc.tile_pool(name="work", bufs=2))
         big = ctx.enter_context(tc.tile_pool(name="big", bufs=8))
-        outs = ctx.enter_context(tc.tile_pool(name="outs", bufs=7))
+        outs = ctx.enter_context(tc.tile_pool(name="outs", bufs=6))
         psum = ctx.enter_context(tc.psum_pool(name="psum", bufs=1))
         ctx.enter_context(tc.manual_schedule())
 
@@ -183,6 +183,15 @@ def tile_ordinaldepththresholdfeaturegradient_x1_kernel(tc, x, g, w, s, b, y, t,
         def g_spread():
             nc.sync.dma_start(out=g_bc[:], in_=g.partition_broadcast(P))
 
+        g_rows = keep.tile([P, 2], F32, align_bytes=64, name="g_rows")
+
+        def g_turn():
+            bank_tile, bank = take_bank([P, 2, P], BF16)
+            for j in range(2):
+                nc.tensor.transpose(bank_tile[:, j, :], g_bc[:, D - 256 + j * P : D - 256 + (j + 1) * P], id16[:])
+            nc.scalar.copy(out=g_rows[:], in_=bank_tile[:, :, 0])
+            free.append(bank)
+
         ls = keep.tile([P, 4, N], BF16, align_bytes=64, name="ls")
 
         def labels(q, lo=0, hi=N):
@@ -200,8 +209,7 @@ def tile_ordinaldepththresholdfeaturegradient_x1_kernel(tc, x, g, w, s, b, y, t,
 
         def d_tile(c, name, shape, dtype):
             if (c, name) not in ds:
-                pool = keep if name == "d_gr" else work
-                ds[(c, name)] = pool.tile(shape, dtype, align_bytes=64, name=name)
+                ds[(c, name)] = work.tile(shape, dtype, align_bytes=64, name=name)
             return ds[(c, name)]
 
         def mm1(c, q, passes=range(NH)):
@@ -238,18 +246,6 @@ def tile_ordinaldepththresholdfeaturegradient_x1_kernel(tc, x, g, w, s, b, y, t,
                 op1=ALU.subtract,
             )
 
-        def d_scale(c, q, hi):
-            sig = ds[(c, "sig")]
-            nc.scalar.activation(out=sig[:, q, :hi], in_=sig[:, q, :hi], func=ACT.Copy, scale=s32[:, q : q + 1])
-
-        def d_sub_pool(c, lo, hi):
-            nc.gpsimd.tensor_tensor(
-                out=d_tile(c, "d_gr", [P, CH, 4], BF16)[:, lo:hi, :],
-                in0=ds[(c, "sig")][:, :, lo:hi].rearrange("p q n -> p n q"),
-                in1=ls[:, :, c * CH + lo : c * CH + hi].rearrange("p q n -> p n q"),
-                op=ALU.subtract,
-            )
-
         def inter(dst, src, lo, hi, on_vector):
             o = dst[:, lo:hi, :].rearrange("p (a i) q -> p a q i", i=4)
             i_ = src[:, :, lo:hi].rearrange("p q (a i) -> p a q i", i=4)
@@ -257,6 +253,21 @@ def tile_ordinaldepththresholdfeaturegradient_x1_kernel(tc, x, g, w, s, b, y, t,
                 nc.vector.tensor_copy(out=o, in_=i_)
             else:
                 nc.scalar.copy(out=o, in_=i_)
+
+        def inter_pool(dst, src, lo, hi):
+            nc.gpsimd.tensor_scalar(
+                out=dst[:, lo:hi, :],
+                in0=src[:, :, lo:hi].rearrange("p q n -> p n q"),
+                scalar1=1.0,
+                scalar2=-0.0,
+                op0=ALU.mult,
+                op1=ALU.add,
+            )
+
+        def d_inter_pool(c, hi):
+            inter_pool(d_tile(c, "d_gr", [P, CH, 4], BF16), ds[(c, "d32")], 0, hi)
+            if hi < CH:
+                d_inter(c, hi, CH)
 
         def d_inter(c, lo=0, hi=CH, on_vector=False):
             inter(d_tile(c, "d_gr", [P, CH, 4], BF16), ds[(c, "d32")], lo, hi, on_vector)
@@ -322,6 +333,40 @@ def tile_ordinaldepththresholdfeaturegradient_x1_kernel(tc, x, g, w, s, b, y, t,
             )
             free.append(banks[(c, dh, tp, lo)][1])
 
+        turned = {}
+
+        def mm2_turned(c, j):
+            o, bank = take_bank([P, CH])
+            cols = slice(D - 256 + j * P, D - 256 + (j + 1) * P)
+            nc.tensor.matmul_mx(
+                out=o[:],
+                lhsT=wt_codes[:, cols].bitcast(FP8X4),
+                lhsT_scale=wt_scales[:, cols],
+                rhs=ds[(c, "d_codes")][:].bitcast(FP8X4),
+                rhs_scale=ds[(c, "d_scales")][:],
+                start=True,
+                stop=True,
+            )
+            turned[(c, j)] = (o, bank)
+
+        def scale_turned(c, j):
+            o, bank = turned[(c, j)]
+            ot = work.tile([P, 4, P], F32, align_bytes=64, name="o_turned")
+            nc.scalar.activation(out=ot[:].rearrange("p t m -> p (t m)"), in_=o[:], func=ACT.Copy, scale=g_rows[:, j : j + 1])
+            free.append(bank)
+            turned[(c, j)] = ot
+
+        def turn_back(c, j):
+            o, bank = take_bank([P, 4, P])
+            for tt in range(4):
+                nc.tensor.transpose(o[:, tt, :], turned[(c, j)][:, tt, :], id32[:])
+            turned[(c, j)] = (o, bank)
+
+        def copy_back(c, j):
+            o, bank = turned[(c, j)]
+            nc.scalar.copy(out=outp[(c, 1)]["o"][:, :, 256 + j * P : 256 + (j + 1) * P], in_=o[:])
+            free.append(bank)
+
         def o_store(c, dh, t0, t1, lo=0, hi=512):
             nc.sync.dma_start(
                 out=out_0[c * CH : (c + 1) * CH, dh * 512 + lo : dh * 512 + hi].rearrange("(p t) d -> p t d", t=4)[:, t0:t1, :],
@@ -330,6 +375,9 @@ def tile_ordinaldepththresholdfeaturegradient_x1_kernel(tc, x, g, w, s, b, y, t,
 
         def o_inter(c, dh, lo=0, hi=512, on_vector=False):
             inter(outp[(c, dh)]["gr"], outp[(c, dh)]["o"], lo, hi, on_vector)
+
+        def o_inter_pool(c, dh, lo, hi):
+            inter_pool(outp[(c, dh)]["gr"], outp[(c, dh)]["o"], lo, hi)
 
         def o_quant(c, dh, lo=0, hi=512):
             e = outp[(c, dh)]
@@ -352,7 +400,7 @@ def tile_ordinaldepththresholdfeaturegradient_x1_kernel(tc, x, g, w, s, b, y, t,
             )
 
         LAST_FIRST = (3, 2, 1, 0)
-        POOL_COLS = 384
+        POOL_COLS = 256
 
 
         def x_turns(c, parts=range(4)):
@@ -388,19 +436,44 @@ def tile_ordinaldepththresholdfeaturegradient_x1_kernel(tc, x, g, w, s, b, y, t,
                     o_store(c, dh, tt, tt + 2)
 
 
-        def d_scales(c):
-            for q in (2, 3, 1, 0):
-                d_scale(c, q, POOL_COLS)
+        def o_inter_shared(c, dh):
+            o_inter_pool(c, dh, 0, POOL_COLS)
+            o_inter(c, dh, POOL_COLS, 512)
 
 
-        def d_pool(c):
-            for lo in range(0, POOL_COLS, P):
-                d_sub_pool(c, lo, lo + P)
+        def turned_products(c):
+            o_alloc(c, 1)
+            for j in range(2):
+                mm2_turned(c, j)
+
+
+        def turned_scale(c):
+            for j in (1, 0):
+                scale_turned(c, j)
+
+
+        def turned_back(c):
+            for j in (1, 0):
+                turn_back(c, j)
+            for j in (0, 1):
+                copy_back(c, j)
+            o_store(c, 1, 0, 4, 256, 512)
+
+
+        def pair_products(c):
+            for tp in range(2):
+                mm2_pair(c, 1, tp, 0)
+
+
+        def pair_muls(c):
+            for tp in (1, 0):
+                o_mul_pair(c, 1, tp, 0)
+            o_store(c, 1, 0, 4, 0, 256)
 
 
         def d_subs(c):
             for q in (2, 3, 1, 0):
-                d_sub(c, q, POOL_COLS, CH)
+                d_sub(c, q)
 
 
         def o_pack(c, dh):
@@ -458,81 +531,79 @@ def tile_ordinaldepththresholdfeaturegradient_x1_kernel(tc, x, g, w, s, b, y, t,
         x_turns(3, (0, 1))
         for q in (2, 1, 0, 3):
             d_sub(0, q)
-        sigms(1, (1, 0))
-        d_inter(0)
+        d_inter_pool(0, POOL_COLS)
         x_muls(2)
         mm1s(1, (2, 3))
-        sigms(1, (3, 2))
+        sigms(1)
         x_turns(3, (2, 3))
+        g_turn()
         for q in LAST_FIRST:
             labels(q, 1024, 2048)
         d_quant(0)
+        turned_products(0)
+        turned_scale(0)
+        turned_back(0)
         mm2s(0, 0)
         x_quant(2)
         d_subs(1)
-        d_scales(1)
-        d_inter(1, POOL_COLS, CH)
-        d_pool(1)
+        d_inter_pool(1, POOL_COLS)
         x_muls(3)
         mm1s(2)
         sigms(2)
-        d_scales(2)
         o_muls(0, 0)
-        mm2s(0, 1)
+        pair_products(0)
         o_inter(0, 0)
         x_quant(3)
         mm1s(3, (0, 1))
-        d_subs(2)
         d_quant(1)
-        d_pool(2)
-        o_alloc(1, 0)
-        mm2(1, 0, 0)
-        mm2(1, 0, 1)
-        o_muls(0, 1)
-        mm2(1, 0, 2)
-        mm2(1, 0, 3)
+        mm2s(1, 0)
+        d_subs(2)
+        d_inter_pool(2, 384)
+        pair_muls(0)
+        turned_products(1)
+        sigms(3, (1, 0))
         mm1s(3, (2, 3))
-        d_inter(2, POOL_COLS, CH)
-        sigms(3)
-        d_scales(3)
-        o_inter(0, 1)
+        turned_scale(1)
+        sigms(3, (3, 2))
         o_muls(1, 0)
-        mm2s(1, 1)
-        d_subs(3)
-        o_pack(0, 0)
+        turned_back(1)
+        pair_products(1)
+        o_inter(0, 1)
         d_quant(2)
-        d_pool(3)
         mm2s(2, 0)
-        d_inter(3, POOL_COLS, CH)
+        o_pack(0, 0)
+        d_subs(3)
+        d_inter_pool(3, 384)
         o_inter(1, 0)
-        o_muls(1, 1)
+        pair_muls(1)
+        o_muls(2, 0)
         mm2s(2, 1)
         o_inter(1, 1)
-        o_muls(2, 0)
         o_inter(2, 0)
-        o_pack(0, 1)
-        o_pack(1, 0)
         d_quant(3)
+        o_pack(0, 1)
         c = NCH - 1
         o_alloc(c, 0)
         o_alloc(c, 1)
         for i in range(4):
             mm2_pair(c, 0, i % 2, 256 * (i // 2))
+        o_pack(1, 0)
         o_muls(2, 1)
         for i in range(4):
             mm2_pair(c, 1, i % 2, 256 * (i // 2))
-        o_inter(2, 1)
-        o_pack(1, 1)
+        o_inter_shared(2, 1)
         for dh in range(2):
             for lo in (256, 0):
                 for tp in (1, 0):
                     o_mul_pair(c, dh, tp, lo)
                 o_store(c, dh, 0, 4, lo, lo + 256)
-                if dh == 0:
+                if (dh, lo) == (0, 0):
+                    o_inter_pool(c, dh, lo, lo + 256)
+                else:
                     o_inter(c, dh, lo, lo + 256)
-            o_pack(c - 1, dh)
-        o_inter(c, 1, 384, 512)
-        o_inter(c, 1, 0, 384, True)
+        o_pack(1, 1)
+        o_pack(2, 0)
+        o_pack(2, 1)
         o_pack(c, 0)
         o_pack(c, 1)
         for qd in range(4):

@@ -19,6 +19,15 @@ P = 128
 CH = 512
 NCH = N // CH
 NH = D // 512
+HALF = 256
+TURNED = D - HALF
+LAST_FIRST = (3, 2, 1, 0)
+
+RUN = 4
+D_POOL_SHORT = 320
+D_POOL_LONG = 448
+O_POOL = 192
+O_GR_BUFS = 7
 
 
 def tile_ordinaldepththresholdfeaturegradient_x1_kernel(tc, x, g, w, s, b, y, t, out_0, out_1, out_2):
@@ -27,7 +36,7 @@ def tile_ordinaldepththresholdfeaturegradient_x1_kernel(tc, x, g, w, s, b, y, t,
         keep = ctx.enter_context(tc.tile_pool(name="keep", bufs=1))
         work = ctx.enter_context(tc.tile_pool(name="work", bufs=2))
         big = ctx.enter_context(tc.tile_pool(name="big", bufs=8))
-        outs = ctx.enter_context(tc.tile_pool(name="outs", bufs=6))
+        outs = ctx.enter_context(tc.tile_pool(name="outs", bufs=O_GR_BUFS))
         psum = ctx.enter_context(tc.psum_pool(name="psum", bufs=1))
         ctx.enter_context(tc.manual_schedule())
 
@@ -38,22 +47,21 @@ def tile_ordinaldepththresholdfeaturegradient_x1_kernel(tc, x, g, w, s, b, y, t,
             return psum.tile(shape, dtype, name="bank%d" % i), i
 
         x_raw = {}
-
-        def x_load(c, tp0, tp1, h0=0, h1=NH):
-            nt, nd = 2 * (tp1 - tp0), 512 * (h1 - h0)
-            xr = keep.tile([P, nt, nd], BF16, align_bytes=64, name="xr%d%d%d" % (c, tp0, h0))
-            xv = x[c * CH : (c + 1) * CH, :].rearrange("(p t) d -> p t d", t=4)
-            nc.sync.dma_start(out=xr[:], in_=xv[:, 2 * tp0 : 2 * tp1, 512 * h0 : 512 * h1])
-            for tp in range(tp0, tp1):
-                for h in range(h0, h1):
-                    x_raw[(c, tp, h)] = xr[:].bitcast(F32)[:, 2 * (tp - tp0) : 2 * (tp - tp0 + 1), 256 * (h - h0) : 256 * (h - h0 + 1)]
-
         w_raw = {}
 
+        def x_load(c, tp0, tp1):
+            xr = keep.tile([P, 2 * (tp1 - tp0), D], BF16, align_bytes=64, name="xr%d%d" % (c, tp0))
+            xv = x[c * CH : (c + 1) * CH, :].rearrange("(p t) d -> p t d", t=4)
+            nc.sync.dma_start(out=xr[:], in_=xv[:, 2 * tp0 : 2 * tp1, :])
+            for tp in range(tp0, tp1):
+                x_raw[(c, tp)] = xr[:].bitcast(F32)[:, 2 * (tp - tp0) : 2 * (tp - tp0 + 1), :]
+
         def w_load(h):
-            wr = keep.tile([P, 4 * K], BF16, align_bytes=64, name="wr%d" % h)
-            nc.sync.dma_start(out=wr[:], in_=w[h * 512 : (h + 1) * 512, :].rearrange("(p j) k -> p (j k)", j=4))
-            w_raw[h] = wr
+            w_raw[h] = keep.tile([P, 4 * K], BF16, align_bytes=64, name="wr%d" % h)
+            nc.sync.dma_start(out=w_raw[h][:], in_=w[h * 512 : (h + 1) * 512, :].rearrange("(p j) k -> p (j k)", j=4))
+
+        def col_load(dst, v):
+            nc.scalar.dma_start(out=dst, in_=v.rearrange("(a p i) -> p a i", p=P, i=4))
 
         g_col = keep.tile([P, NH, 4], BF16, align_bytes=64, name="g_col")
         y_col = keep.tile([P, NCH, 4], BF16, align_bytes=64, name="y_col")
@@ -61,39 +69,21 @@ def tile_ordinaldepththresholdfeaturegradient_x1_kernel(tc, x, g, w, s, b, y, t,
         s_col = keep.tile([P, 4], BF16, align_bytes=64, name="s_col")
         b_col = keep.tile([P, 4], BF16, align_bytes=64, name="b_col")
         s32 = keep.tile([P, 4], F32, align_bytes=64, name="s32")
-
-        def col_load(dst, v):
-            nc.scalar.dma_start(out=dst, in_=v.rearrange("(a p i) -> p a i", p=P, i=4))
-
-        def s_widen():
-            nc.scalar.copy(out=s32[:], in_=s_col[:])
-
+        t32 = keep.tile([P, 4], F32, align_bytes=64, name="t32")
         warm = keep.tile([P, 1], F32, name="warm")
         warm2 = keep.tile([P, 1], F32, name="warm2")
-
-        def warm_up():
-            nc.vector.memset(warm[:], 0.0)
-            nc.scalar.activation(out=warm2[:], in_=warm[:], func=ACT.Sigmoid)
-
         id32 = keep.tile([P, P], F32, align_bytes=64, name="id32")
         id16 = keep.tile([P, P], BF16, align_bytes=64, name="id16")
-
-        def identities():
-            make_identity(nc, id32[:])
-            make_identity(nc, id16[:])
-
         g4 = g_col[:].rearrange("p h (u e) -> p h u e", u=2)
 
         y_bc = keep.tile([P, N], BF16, align_bytes=64, name="y_bc")
-
         ys = {}
 
         def y_spread(hf):
-            yp, bank = take_bank([P, N // 2], BF16)
+            ys[hf] = take_bank([P, N // 2], BF16)
             for i in range(8):
-                j = hf * 8 + i
-                nc.tensor.transpose(yp[:, i * P : (i + 1) * P], y_col[:, j // 4, j % 4 : j % 4 + 1].to_broadcast([P, P]), id16[:])
-            ys[hf] = (yp, bank)
+                c, tt = 2 * hf + i // 4, i % 4
+                nc.tensor.transpose(ys[hf][0][:, i * P : (i + 1) * P], y_col[:, c, tt : tt + 1].to_broadcast([P, P]), id16[:])
 
         def y_copy(hf):
             nc.scalar.copy(out=y_bc[:, hf * N // 2 : (hf + 1) * N // 2], in_=ys[hf][0][:])
@@ -103,180 +93,159 @@ def tile_ordinaldepththresholdfeaturegradient_x1_kernel(tc, x, g, w, s, b, y, t,
         w_codes = keep.tile([P, NH, K], U32, align_bytes=64, name="w_codes")
         w_scales = keep.tile([P, NH, K], U8, align_bytes=64, name="w_scales")
 
-        def w_inter(h, on_vector, lo=0, hi=64):
-            dst = w_gr[:, h].rearrange("p (q a m) j -> p a q m j", q=4, m=2)[:, lo:hi]
-            src = w_raw[h][:].rearrange("p (j a m q) -> p a q m j", j=4, m=2, q=4)[:, lo:hi]
-            if on_vector:
-                nc.vector.tensor_copy(out=dst, in_=src)
-            else:
-                nc.scalar.copy(out=dst, in_=src)
+        def w_views(h):
+            dst = w_gr[:, h].rearrange("p (q a m) j -> p a q m j", q=4, m=2)
+            return dst, w_raw[h][:].rearrange("p (j a m q) -> p a q m j", j=4, m=2, q=4)
 
-        def w_quant(h0, h1):
-            nc.vector.quantize_mx(
-                out=w_codes[:, h0:h1].rearrange("p h k -> p (h k)").bitcast(FP8X4),
-                scales=w_scales[:, h0:h1].rearrange("p h k -> p (h k)"),
-                in_=w_gr[:, h0:h1].rearrange("p h k j -> p (h k j)"),
-            )
+        def quantise(codes, scales, src):
+            nc.vector.quantize_mx(out=codes.bitcast(FP8X4), scales=scales, in_=src)
 
-        xs = {}
+        x_gr = {}
+        x_q = {}
         xts = {}
 
-        def x_alloc(c):
-            xs[c] = [big.tile([P, NH, CH, 4], BF16, align_bytes=64, name="big")]
+        def x_turns(c, parts=range(4)):
+            for i in parts:
+                tp, h = i // 2, i % 2
+                xts[(c, i)] = take_bank([P, 2, HALF])
+                for tt in range(2):
+                    for u in range(2):
+                        nc.tensor.transpose(
+                            xts[(c, i)][0][:, u, tt * P : (tt + 1) * P],
+                            x_raw[(c, tp)][:, tt, HALF * h + u : HALF * (h + 1) : 2],
+                            id32[:],
+                        )
 
-        def x_turn(c, tp, h):
-            words = x_raw[(c, tp, h)]
-            xt, bank = take_bank([P, 2, 256])
-            for tt in range(2):
-                for u in range(2):
-                    nc.tensor.transpose(xt[:, u, tt * P : (tt + 1) * P], words[:, tt, u:256:2], id32[:])
-            xts[(c, tp, h)] = (xt, bank)
+        def x_muls(c, parts=LAST_FIRST):
+            for i in parts:
+                tp, h = i // 2, i % 2
+                nc.vector.tensor_tensor(
+                    out=x_gr[c][:, h, HALF * tp : HALF * (tp + 1), :].rearrange("p n (u e) -> p n u e", u=2),
+                    in0=xts[(c, i)][0][:].bitcast(BF16).rearrange("p u (n e) -> p n u e", e=2),
+                    in1=g4[:, h].unsqueeze(1).to_broadcast([P, HALF, 2, 2]),
+                    op=ALU.mult,
+                )
+                free.append(xts[(c, i)][1])
 
-        def x_mul(c, tp, h):
-            nc.vector.tensor_tensor(
-                out=xs[c][0][:, h, 256 * tp : 256 * (tp + 1), :].rearrange("p n (u e) -> p n u e", u=2),
-                in0=xts[(c, tp, h)][0][:].bitcast(BF16).rearrange("p u (n e) -> p n u e", e=2),
-                in1=g4[:, h].unsqueeze(1).to_broadcast([P, 256, 2, 2]),
-                op=ALU.mult,
-            )
-            free.append(xts[(c, tp, h)][1])
-
-        def x_quant(c, h0=0, h1=NH):
-            if h0 == 0:
-                xs[c].append(work.tile([P, NH, CH], U32, align_bytes=64, name="x_codes"))
-                xs[c].append(work.tile([P, NH, CH], U8, align_bytes=64, name="x_scales"))
-            gr, codes, scales = xs[c]
-            nc.vector.quantize_mx(
-                out=codes[:, h0:h1].rearrange("p h n -> p (h n)").bitcast(FP8X4),
-                scales=scales[:, h0:h1].rearrange("p h n -> p (h n)"),
-                in_=gr[:, h0:h1].rearrange("p h n j -> p (h n j)"),
+        def x_quant(c):
+            codes = work.tile([P, NH, CH], U32, align_bytes=64, name="x_codes")
+            scales = work.tile([P, NH, CH], U8, align_bytes=64, name="x_scales")
+            x_q[c] = (codes, scales)
+            quantise(
+                codes[:].rearrange("p h n -> p (h n)"),
+                scales[:].rearrange("p h n -> p (h n)"),
+                x_gr[c][:].rearrange("p h n j -> p (h n j)"),
             )
 
         wt_gr = big.tile([P, D, 4], BF16, align_bytes=64, name="big")
         wt_codes = keep.tile([P, D], U32, align_bytes=64, name="wt_codes")
         wt_scales = keep.tile([P, D], U8, align_bytes=64, name="wt_scales")
-
         wts = {}
 
         def wt_turn(h, jp):
             words = w_raw[h][:].bitcast(F32).rearrange("p (j k) -> p j k", j=4)
-            wt, bank = take_bank([P, 2, 2, P])
+            wts[(h, jp)] = take_bank([P, 2, 2, P])
             for jj in range(2):
                 for u in range(2):
-                    nc.tensor.transpose(wt[:, jj, u, :], words[:, 2 * jp + jj, u : 256 : 2], id32[:])
-            wts[(h, jp)] = (wt, bank)
+                    nc.tensor.transpose(wts[(h, jp)][0][:, jj, u, :], words[:, 2 * jp + jj, u:HALF:2], id32[:])
 
         def wt_copy(h, jp):
             dst = wt_gr[:].rearrange("p d e -> p (d e)").bitcast(F32).rearrange("p (h m j u) -> p h m j u", h=NH, j=4, u=2)
             nc.scalar.copy(out=dst[:, h, :, 2 * jp : 2 * jp + 2, :], in_=wts[(h, jp)][0][:].rearrange("p j u m -> p m j u"))
             free.append(wts[(h, jp)][1])
 
-        def wt_quant(h0, h1):
-            nc.vector.quantize_mx(
-                out=wt_codes[:, h0 * 512 : h1 * 512].bitcast(FP8X4),
-                scales=wt_scales[:, h0 * 512 : h1 * 512],
-                in_=wt_gr[:, h0 * 512 : h1 * 512, :].rearrange("p d j -> p (d j)"),
-            )
-
         g_bc = keep.tile([P, D], BF16, align_bytes=64, name="g_bc")
-
-        def g_spread():
-            nc.sync.dma_start(out=g_bc[:], in_=g.partition_broadcast(P))
-
         g_rows = keep.tile([P, 2], F32, align_bytes=64, name="g_rows")
 
         def g_turn():
-            bank_tile, bank = take_bank([P, 2, P], BF16)
+            turned_g, bank = take_bank([P, 2, P], BF16)
             for j in range(2):
-                nc.tensor.transpose(bank_tile[:, j, :], g_bc[:, D - 256 + j * P : D - 256 + (j + 1) * P], id16[:])
-            nc.scalar.copy(out=g_rows[:], in_=bank_tile[:, :, 0])
+                nc.tensor.transpose(turned_g[:, j, :], g_bc[:, TURNED + j * P : TURNED + (j + 1) * P], id16[:])
+            nc.scalar.copy(out=g_rows[:], in_=turned_g[:, :, 0])
             free.append(bank)
 
         ls = keep.tile([P, 4, N], BF16, align_bytes=64, name="ls")
-
-        def labels(q, lo=0, hi=N):
-            nc.vector.tensor_scalar(
-                out=ls[:, q, lo:hi],
-                in0=y_bc[:, lo:hi],
-                scalar1=t_col[:, q : q + 1],
-                scalar2=s_col[:, q : q + 1],
-                op0=ALU.is_gt,
-                op1=ALU.mult,
-            )
-
         ds = {}
         zs = {}
+
+        def labels(hf):
+            cols = slice(hf * N // 2, (hf + 1) * N // 2)
+            for q in LAST_FIRST:
+                nc.vector.tensor_scalar(
+                    out=ls[:, q, cols],
+                    in0=y_bc[:, cols],
+                    scalar1=t32[:, q : q + 1],
+                    scalar2=s32[:, q : q + 1],
+                    op0=ALU.is_gt,
+                    op1=ALU.mult,
+                )
 
         def d_tile(c, name, shape, dtype):
             if (c, name) not in ds:
                 ds[(c, name)] = work.tile(shape, dtype, align_bytes=64, name=name)
             return ds[(c, name)]
 
-        def mm1(c, q, passes=range(NH)):
-            if (c, q) not in zs:
+        def mm1s(c, qs=range(4)):
+            for q in qs:
                 zs[(c, q)] = take_bank([P, CH])
-            for h in passes:
-                nc.tensor.matmul_mx(
-                    out=zs[(c, q)][0][:],
-                    lhsT=w_codes[:, h, q * P : (q + 1) * P].bitcast(FP8X4),
-                    lhsT_scale=w_scales[:, h, q * P : (q + 1) * P],
-                    rhs=xs[c][1][:, h].bitcast(FP8X4),
-                    rhs_scale=xs[c][2][:, h],
-                    start=(h == 0),
-                    stop=(h == NH - 1),
+                for h in range(NH):
+                    nc.tensor.matmul_mx(
+                        out=zs[(c, q)][0][:],
+                        lhsT=w_codes[:, h, q * P : (q + 1) * P].bitcast(FP8X4),
+                        lhsT_scale=w_scales[:, h, q * P : (q + 1) * P],
+                        rhs=x_q[c][0][:, h].bitcast(FP8X4),
+                        rhs_scale=x_q[c][1][:, h],
+                        start=(h == 0),
+                        stop=(h == NH - 1),
+                    )
+
+        def sigms(c, qs=(1, 0, 3, 2)):
+            for q in qs:
+                nc.scalar.activation(
+                    out=d_tile(c, "sig", [P, 4, CH], F32)[:, q, :],
+                    in_=zs[(c, q)][0][:],
+                    func=ACT.Sigmoid,
+                    bias=b_col[:, q : q + 1],
+                    scale=s32[:, q : q + 1],
+                )
+                free.append(zs[(c, q)][1])
+
+        def d_subs(c, qs=(2, 3, 1, 0)):
+            for q in qs:
+                nc.vector.scalar_tensor_tensor(
+                    out=d_tile(c, "d16", [P, 4, CH], BF16)[:, q, :],
+                    in0=ds[(c, "sig")][:, q, :],
+                    scalar=s32[:, q : q + 1],
+                    in1=ls[:, q, c * CH : (c + 1) * CH],
+                    op0=ALU.mult,
+                    op1=ALU.subtract,
                 )
 
-        def sigm(c, q, lo=0, hi=CH):
-            nc.scalar.activation(
-                out=d_tile(c, "sig", [P, 4, CH], F32)[:, q, lo:hi],
-                in_=zs[(c, q)][0][:],
-                func=ACT.Sigmoid,
-                bias=b_col[:, q : q + 1],
-                scale=s32[:, q : q + 1],
-            )
-            free.append(zs[(c, q)][1])
-
-        def d_sub(c, q, lo=0, hi=CH):
-            nc.vector.scalar_tensor_tensor(
-                out=d_tile(c, "d32", [P, 4, CH], F32)[:, q, lo:hi],
-                in0=ds[(c, "sig")][:, q, lo:hi],
-                scalar=s_col[:, q : q + 1],
-                in1=ls[:, q, c * CH + lo : c * CH + hi],
-                op0=ALU.mult,
-                op1=ALU.subtract,
+        def inter(dst, src, lo, hi):
+            nc.scalar.copy(
+                out=dst[:, lo:hi, :].rearrange("p (a i) q -> p a q i", i=RUN),
+                in_=src[:, :, lo:hi].rearrange("p q (a i) -> p a q i", i=RUN),
             )
 
-        def inter(dst, src, lo, hi, on_vector):
-            o = dst[:, lo:hi, :].rearrange("p (a i) q -> p a q i", i=4)
-            i_ = src[:, :, lo:hi].rearrange("p q (a i) -> p a q i", i=4)
-            if on_vector:
-                nc.vector.tensor_copy(out=o, in_=i_)
-            else:
-                nc.scalar.copy(out=o, in_=i_)
-
-        def inter_pool(dst, src, lo, hi):
+        def inter_shared(dst, src, lo, mid, hi):
             nc.gpsimd.tensor_scalar(
-                out=dst[:, lo:hi, :],
-                in0=src[:, :, lo:hi].rearrange("p q n -> p n q"),
+                out=dst[:, lo:mid, :],
+                in0=src[:, :, lo:mid].rearrange("p q n -> p n q"),
                 scalar1=1.0,
                 scalar2=-0.0,
                 op0=ALU.mult,
                 op1=ALU.add,
             )
+            inter(dst, src, mid, hi)
 
-        def d_inter_pool(c, hi):
-            inter_pool(d_tile(c, "d_gr", [P, CH, 4], BF16), ds[(c, "d32")], 0, hi)
-            if hi < CH:
-                d_inter(c, hi, CH)
+        def d_inter(c, pool_rows):
+            inter_shared(d_tile(c, "d_gr", [P, CH, 4], BF16), ds[(c, "d16")], 0, pool_rows, CH)
 
-        def d_inter(c, lo=0, hi=CH, on_vector=False):
-            inter(d_tile(c, "d_gr", [P, CH, 4], BF16), ds[(c, "d32")], lo, hi, on_vector)
-
-        def d_quant(c, lo=0, hi=CH):
-            nc.vector.quantize_mx(
-                out=d_tile(c, "d_codes", [P, CH], U32)[:, lo:hi].bitcast(FP8X4),
-                scales=d_tile(c, "d_scales", [P, CH], U8)[:, lo:hi],
-                in_=ds[(c, "d_gr")][:, lo:hi, :].rearrange("p n j -> p (n j)"),
+        def d_quant(c):
+            quantise(
+                d_tile(c, "d_codes", [P, CH], U32)[:],
+                d_tile(c, "d_scales", [P, CH], U8)[:],
+                ds[(c, "d_gr")][:].rearrange("p n j -> p (n j)"),
             )
 
         outp = {}
@@ -290,196 +259,117 @@ def tile_ordinaldepththresholdfeaturegradient_x1_kernel(tc, x, g, w, s, b, y, t,
                 codes=keep.tile([P, 512], U32, align_bytes=64, name="o_codes%d%d" % (c, dh)),
             )
 
-        def mm2(c, dh, tt, lo=0, hi=512):
-            o, bank = take_bank([P, hi - lo])
+        def mm2(out, c, tt, d0, d1):
             nc.tensor.matmul_mx(
-                out=o[:],
+                out=out,
                 lhsT=ds[(c, "d_codes")][:, tt * P : (tt + 1) * P].bitcast(FP8X4),
                 lhsT_scale=ds[(c, "d_scales")][:, tt * P : (tt + 1) * P],
-                rhs=wt_codes[:, dh * 512 + lo : dh * 512 + hi].bitcast(FP8X4),
-                rhs_scale=wt_scales[:, dh * 512 + lo : dh * 512 + hi],
+                rhs=wt_codes[:, d0:d1].bitcast(FP8X4),
+                rhs_scale=wt_scales[:, d0:d1],
                 start=True,
                 stop=True,
             )
-            banks[(c, dh, tt, lo)] = (o, bank)
 
-        def o_mul(c, dh, tt, lo=0, hi=512):
-            nc.vector.tensor_tensor(
-                out=outp[(c, dh)]["o"][:, tt, lo:hi], in0=banks[(c, dh, tt, lo)][0][:], in1=g_bc[:, dh * 512 + lo : dh * 512 + hi], op=ALU.mult
-            )
-            free.append(banks[(c, dh, tt, lo)][1])
-
-        def mm2_pair(c, dh, tp, lo):
-            o, bank = take_bank([P, 2, 256])
-            for tt in range(2):
-                cols = slice((2 * tp + tt) * P, (2 * tp + tt + 1) * P)
-                nc.tensor.matmul_mx(
-                    out=o[:, tt, :],
-                    lhsT=ds[(c, "d_codes")][:, cols].bitcast(FP8X4),
-                    lhsT_scale=ds[(c, "d_scales")][:, cols],
-                    rhs=wt_codes[:, dh * 512 + lo : dh * 512 + lo + 256].bitcast(FP8X4),
-                    rhs_scale=wt_scales[:, dh * 512 + lo : dh * 512 + lo + 256],
-                    start=True,
-                    stop=True,
-                )
-            banks[(c, dh, tp, lo)] = (o, bank)
-
-        def o_mul_pair(c, dh, tp, lo):
-            nc.vector.tensor_tensor(
-                out=outp[(c, dh)]["o"][:, 2 * tp : 2 * tp + 2, lo : lo + 256],
-                in0=banks[(c, dh, tp, lo)][0][:],
-                in1=g_bc[:, dh * 512 + lo : dh * 512 + lo + 256].unsqueeze(1).to_broadcast([P, 2, 256]),
-                op=ALU.mult,
-            )
-            free.append(banks[(c, dh, tp, lo)][1])
-
-        turned = {}
-
-        def mm2_turned(c, j):
-            o, bank = take_bank([P, CH])
-            cols = slice(D - 256 + j * P, D - 256 + (j + 1) * P)
-            nc.tensor.matmul_mx(
-                out=o[:],
-                lhsT=wt_codes[:, cols].bitcast(FP8X4),
-                lhsT_scale=wt_scales[:, cols],
-                rhs=ds[(c, "d_codes")][:].bitcast(FP8X4),
-                rhs_scale=ds[(c, "d_scales")][:],
-                start=True,
-                stop=True,
-            )
-            turned[(c, j)] = (o, bank)
-
-        def scale_turned(c, j):
-            o, bank = turned[(c, j)]
-            ot = work.tile([P, 4, P], F32, align_bytes=64, name="o_turned")
-            nc.scalar.activation(out=ot[:].rearrange("p t m -> p (t m)"), in_=o[:], func=ACT.Copy, scale=g_rows[:, j : j + 1])
-            free.append(bank)
-            turned[(c, j)] = ot
-
-        def turn_back(c, j):
-            o, bank = take_bank([P, 4, P])
+        def mm2s(c, dh):
+            o_alloc(c, dh)
             for tt in range(4):
-                nc.tensor.transpose(o[:, tt, :], turned[(c, j)][:, tt, :], id32[:])
-            turned[(c, j)] = (o, bank)
+                banks[(c, dh, tt)] = take_bank([P, 512])
+                mm2(banks[(c, dh, tt)][0][:], c, tt, dh * 512, (dh + 1) * 512)
 
-        def copy_back(c, j):
-            o, bank = turned[(c, j)]
-            nc.scalar.copy(out=outp[(c, 1)]["o"][:, :, 256 + j * P : 256 + (j + 1) * P], in_=o[:])
-            free.append(bank)
-
-        def o_store(c, dh, t0, t1, lo=0, hi=512):
+        def o_store(c, dh, t0, t1, lo, hi):
             nc.sync.dma_start(
                 out=out_0[c * CH : (c + 1) * CH, dh * 512 + lo : dh * 512 + hi].rearrange("(p t) d -> p t d", t=4)[:, t0:t1, :],
                 in_=outp[(c, dh)]["o"][:, t0:t1, lo:hi],
             )
 
-        def o_inter(c, dh, lo=0, hi=512, on_vector=False):
-            inter(outp[(c, dh)]["gr"], outp[(c, dh)]["o"], lo, hi, on_vector)
-
-        def o_inter_pool(c, dh, lo, hi):
-            inter_pool(outp[(c, dh)]["gr"], outp[(c, dh)]["o"], lo, hi)
-
-        def o_quant(c, dh, lo=0, hi=512):
-            e = outp[(c, dh)]
-            nc.vector.quantize_mx(
-                out=e["codes"][:, lo:hi].bitcast(FP8X4),
-                scales=o_scales[4 * c : P, dh * 512 + lo : dh * 512 + hi],
-                in_=e["gr"][:, lo:hi, :].rearrange("p d j -> p (d j)"),
-            )
-
-        def code_store(c, dh, lo=0, hi=512):
-            nc.sync.dma_start(
-                out=out_1[c, :, dh * 512 + lo : dh * 512 + hi, :].rearrange("p m t -> p (m t)").bitcast(I32),
-                in_=outp[(c, dh)]["codes"][:, lo:hi].bitcast(I32),
-            )
-
-        def scale_store(qd, queue):
-            queue.dma_start(
-                out=out_2[:, 4 * qd : 4 * qd + 4, :].bitcast(I32),
-                in_=o_scales[32 * qd : 32 * qd + 16, :].bitcast(I32),
-            )
-
-        LAST_FIRST = (3, 2, 1, 0)
-        POOL_COLS = 256
-
-
-        def x_turns(c, parts=range(4)):
-            for i in parts:
-                x_turn(c, i // 2, i % 2)
-
-
-        def x_muls(c):
-            for i in LAST_FIRST:
-                x_mul(c, i // 2, i % 2)
-
-
-        def mm1s(c, qs=range(4)):
-            for q in qs:
-                mm1(c, q)
-
-
-        def sigms(c, qs=(1, 0, 3, 2)):
-            for q in qs:
-                sigm(c, q)
-
-
-        def mm2s(c, dh):
-            o_alloc(c, dh)
-            for tt in range(4):
-                mm2(c, dh, tt)
-
-
         def o_muls(c, dh):
             for tt in LAST_FIRST:
-                o_mul(c, dh, tt)
+                nc.vector.tensor_tensor(
+                    out=outp[(c, dh)]["o"][:, tt, :],
+                    in0=banks[(c, dh, tt)][0][:],
+                    in1=g_bc[:, dh * 512 : (dh + 1) * 512],
+                    op=ALU.mult,
+                )
+                free.append(banks[(c, dh, tt)][1])
                 if tt % 2 == 0:
-                    o_store(c, dh, tt, tt + 2)
+                    o_store(c, dh, tt, tt + 2, 0, 512)
 
+        def pair_products(c, dh, lo):
+            for tp in range(2):
+                banks[(c, dh, tp, lo)] = take_bank([P, 2, HALF])
+                for tt in range(2):
+                    mm2(banks[(c, dh, tp, lo)][0][:, tt, :], c, 2 * tp + tt, dh * 512 + lo, dh * 512 + lo + HALF)
 
-        def o_inter_shared(c, dh):
-            o_inter_pool(c, dh, 0, POOL_COLS)
-            o_inter(c, dh, POOL_COLS, 512)
+        def pair_muls(c, dh, lo):
+            for tp in (1, 0):
+                nc.vector.tensor_tensor(
+                    out=outp[(c, dh)]["o"][:, 2 * tp : 2 * tp + 2, lo : lo + HALF],
+                    in0=banks[(c, dh, tp, lo)][0][:],
+                    in1=g_bc[:, dh * 512 + lo : dh * 512 + lo + HALF].unsqueeze(1).to_broadcast([P, 2, HALF]),
+                    op=ALU.mult,
+                )
+                free.append(banks[(c, dh, tp, lo)][1])
+            o_store(c, dh, 0, 4, lo, lo + HALF)
 
+        turned = {}
 
         def turned_products(c):
             o_alloc(c, 1)
             for j in range(2):
-                mm2_turned(c, j)
-
+                turned[(c, j)] = take_bank([P, CH])
+                cols = slice(TURNED + j * P, TURNED + (j + 1) * P)
+                nc.tensor.matmul_mx(
+                    out=turned[(c, j)][0][:],
+                    lhsT=wt_codes[:, cols].bitcast(FP8X4),
+                    lhsT_scale=wt_scales[:, cols],
+                    rhs=ds[(c, "d_codes")][:].bitcast(FP8X4),
+                    rhs_scale=ds[(c, "d_scales")][:],
+                    start=True,
+                    stop=True,
+                )
 
         def turned_scale(c):
             for j in (1, 0):
-                scale_turned(c, j)
-
+                o, bank = turned[(c, j)]
+                ot = work.tile([P, 4, P], F32, align_bytes=64, name="o_turned")
+                nc.scalar.activation(out=ot[:].rearrange("p t m -> p (t m)"), in_=o[:], func=ACT.Copy, scale=g_rows[:, j : j + 1])
+                free.append(bank)
+                turned[(c, j)] = ot
 
         def turned_back(c):
+            back = {}
             for j in (1, 0):
-                turn_back(c, j)
+                back[j] = take_bank([P, 4, P])
+                for tt in range(4):
+                    nc.tensor.transpose(back[j][0][:, tt, :], turned[(c, j)][:, tt, :], id32[:])
             for j in (0, 1):
-                copy_back(c, j)
-            o_store(c, 1, 0, 4, 256, 512)
+                nc.scalar.copy(out=outp[(c, 1)]["o"][:, :, HALF + j * P : HALF + (j + 1) * P], in_=back[j][0][:])
+                free.append(back[j][1])
+            o_store(c, 1, 0, 4, HALF, 512)
 
+        def o_inter(c, dh, lo=0, hi=512):
+            inter(outp[(c, dh)]["gr"], outp[(c, dh)]["o"], lo, hi)
 
-        def pair_products(c):
-            for tp in range(2):
-                mm2_pair(c, 1, tp, 0)
+        def o_inter_shared(c, dh, hi):
+            inter_shared(outp[(c, dh)]["gr"], outp[(c, dh)]["o"], 0, O_POOL, hi)
 
+        def o_quant(c, dh, lo=0, hi=512):
+            e = outp[(c, dh)]
+            quantise(
+                e["codes"][:, lo:hi],
+                o_scales[4 * c : P, dh * 512 + lo : dh * 512 + hi],
+                e["gr"][:, lo:hi, :].rearrange("p d j -> p (d j)"),
+            )
 
-        def pair_muls(c):
-            for tp in (1, 0):
-                o_mul_pair(c, 1, tp, 0)
-            o_store(c, 1, 0, 4, 0, 256)
-
-
-        def d_subs(c):
-            for q in (2, 3, 1, 0):
-                d_sub(c, q)
-
+        def code_store(c, dh):
+            nc.sync.dma_start(
+                out=out_1[c, :, dh * 512 : (dh + 1) * 512, :].rearrange("p m t -> p (m t)").bitcast(I32),
+                in_=outp[(c, dh)]["codes"][:].bitcast(I32),
+            )
 
         def o_pack(c, dh):
             o_quant(c, dh)
             code_store(c, dh)
-
 
         x_load(0, 0, 1)
         col_load(g_col[:], g)
@@ -493,52 +383,59 @@ def tile_ordinaldepththresholdfeaturegradient_x1_kernel(tc, x, g, w, s, b, y, t,
         col_load(b_col[:].unsqueeze(1), b)
         for c in range(2, NCH):
             x_load(c, 0, 2)
-        g_spread()
-        warm_up()
-        identities()
+        nc.sync.dma_start(out=g_bc[:], in_=g.partition_broadcast(P))
+        nc.vector.memset(warm[:], 0.0)
+        nc.scalar.activation(out=warm2[:], in_=warm[:], func=ACT.Sigmoid)
+        make_identity(nc, id32[:])
+        make_identity(nc, id16[:])
         for c in range(NCH):
-            x_alloc(c)
+            x_gr[c] = big.tile([P, NH, CH, 4], BF16, align_bytes=64, name="big")
+
         x_turns(0)
-        for i in (0, 1, 3, 2):
-            x_mul(0, i // 2, i % 2)
-        s_widen()
-        w_inter(0, False)
-        wt_turn(0, 0)
-        wt_turn(0, 1)
-        y_spread(0)
-        wt_turn(1, 0)
-        wt_turn(1, 1)
-        y_spread(1)
+        x_muls(0, (0, 1, 3, 2))
+        nc.scalar.copy(out=s32[:], in_=s_col[:])
+        nc.scalar.copy(out=t32[:], in_=t_col[:])
+        dst, src = w_views(0)
+        nc.scalar.copy(out=dst, in_=src)
+        for h in range(NH):
+            wt_turn(h, 0)
+            wt_turn(h, 1)
+            y_spread(h)
         y_copy(0)
-        for i in (1, 0, 3, 2):
-            wt_copy(i // 2, i % 2)
+        for h in range(NH):
+            wt_copy(h, 1)
+            wt_copy(h, 0)
         y_copy(1)
-        w_inter(1, True)
+        dst, src = w_views(1)
+        nc.vector.tensor_copy(out=dst, in_=src)
         x_turns(1)
         x_quant(0)
-        w_quant(0, 2)
+        quantise(
+            w_codes[:].rearrange("p h k -> p (h k)"),
+            w_scales[:].rearrange("p h k -> p (h k)"),
+            w_gr[:].rearrange("p h k j -> p (h k j)"),
+        )
+
         mm1s(0, (0, 1, 2))
-        for q in LAST_FIRST:
-            labels(q, 0, 1024)
+        labels(0)
         x_muls(1)
         x_turns(2, (0, 1))
         mm1s(0, (3,))
         x_turns(2, (2, 3))
         sigms(0, range(4))
-        wt_quant(0, 2)
+        quantise(wt_codes[:], wt_scales[:], wt_gr[:].rearrange("p d j -> p (d j)"))
         x_quant(1)
         mm1s(1, (0, 1))
         x_turns(3, (0, 1))
-        for q in (2, 1, 0, 3):
-            d_sub(0, q)
-        d_inter_pool(0, POOL_COLS)
+        d_subs(0, (2, 1, 0, 3))
+        d_inter(0, D_POOL_SHORT)
         x_muls(2)
         mm1s(1, (2, 3))
         sigms(1)
         x_turns(3, (2, 3))
         g_turn()
-        for q in LAST_FIRST:
-            labels(q, 1024, 2048)
+        labels(1)
+
         d_quant(0)
         turned_products(0)
         turned_scale(0)
@@ -546,20 +443,21 @@ def tile_ordinaldepththresholdfeaturegradient_x1_kernel(tc, x, g, w, s, b, y, t,
         mm2s(0, 0)
         x_quant(2)
         d_subs(1)
-        d_inter_pool(1, POOL_COLS)
+        d_inter(1, D_POOL_SHORT)
         x_muls(3)
         mm1s(2)
         sigms(2)
         o_muls(0, 0)
-        pair_products(0)
+        pair_products(0, 1, 0)
         o_inter(0, 0)
         x_quant(3)
         mm1s(3, (0, 1))
         d_quant(1)
         mm2s(1, 0)
         d_subs(2)
-        d_inter_pool(2, 384)
-        pair_muls(0)
+        d_inter(2, D_POOL_LONG)
+        pair_muls(0, 1, 0)
+
         turned_products(1)
         sigms(3, (1, 0))
         mm1s(3, (2, 3))
@@ -567,44 +465,47 @@ def tile_ordinaldepththresholdfeaturegradient_x1_kernel(tc, x, g, w, s, b, y, t,
         sigms(3, (3, 2))
         o_muls(1, 0)
         turned_back(1)
-        pair_products(1)
+        pair_products(1, 1, 0)
         o_inter(0, 1)
         d_quant(2)
         mm2s(2, 0)
         o_pack(0, 0)
         d_subs(3)
-        d_inter_pool(3, 384)
+        d_inter(3, D_POOL_LONG)
         o_inter(1, 0)
-        pair_muls(1)
+        pair_muls(1, 1, 0)
+
         o_muls(2, 0)
         mm2s(2, 1)
         o_inter(1, 1)
         o_inter(2, 0)
         d_quant(3)
         o_pack(0, 1)
-        c = NCH - 1
-        o_alloc(c, 0)
-        o_alloc(c, 1)
-        for i in range(4):
-            mm2_pair(c, 0, i % 2, 256 * (i // 2))
+        o_alloc(3, 0)
+        o_alloc(3, 1)
+        for lo in (0, HALF):
+            pair_products(3, 0, lo)
         o_pack(1, 0)
         o_muls(2, 1)
-        for i in range(4):
-            mm2_pair(c, 1, i % 2, 256 * (i // 2))
-        o_inter_shared(2, 1)
+        for lo in (0, HALF):
+            pair_products(3, 1, lo)
+        o_inter_shared(2, 1, 512)
         for dh in range(2):
-            for lo in (256, 0):
-                for tp in (1, 0):
-                    o_mul_pair(c, dh, tp, lo)
-                o_store(c, dh, 0, 4, lo, lo + 256)
-                if (dh, lo) == (0, 0):
-                    o_inter_pool(c, dh, lo, lo + 256)
-                else:
-                    o_inter(c, dh, lo, lo + 256)
-        o_pack(1, 1)
-        o_pack(2, 0)
-        o_pack(2, 1)
-        o_pack(c, 0)
-        o_pack(c, 1)
+            pair_muls(3, dh, HALF)
+            o_inter(3, dh, HALF, 512)
+            pair_muls(3, dh, 0)
+            if dh == 0:
+                o_inter_shared(3, 0, HALF)
+            else:
+                o_inter(3, 1, 0, HALF)
+        for c, dh in ((1, 1), (2, 0), (2, 1), (3, 0)):
+            o_pack(c, dh)
+        o_quant(3, 1, HALF, 512)
+        o_quant(3, 1, 0, HALF)
+        code_store(3, 1)
         for qd in range(4):
-            scale_store(qd, nc.scalar if qd % 2 else nc.sync)
+            queue = nc.scalar if qd % 2 else nc.sync
+            queue.dma_start(
+                out=out_2[:, 4 * qd : 4 * qd + 4, :].bitcast(I32),
+                in_=o_scales[32 * qd : 32 * qd + 16, :].bitcast(I32),
+            )

@@ -24,8 +24,11 @@ TURNED = D - HALF
 LAST_FIRST = (3, 2, 1, 0)
 
 RUN = 4
-D_POOL_SHORT = 320
-D_POOL_LONG = 448
+D_POOL_FIRST = 224
+D_POOL_MID = 368
+D_POOL_LAST = 416
+O_POOL_LAST = 32
+D_POOL_LONG = 416
 O_POOL = 192
 O_GR_BUFS = 7
 
@@ -60,8 +63,8 @@ def tile_ordinaldepththresholdfeaturegradient_x1_kernel(tc, x, g, w, s, b, y, t,
             w_raw[h] = keep.tile([P, 4 * K], BF16, align_bytes=64, name="wr%d" % h)
             nc.sync.dma_start(out=w_raw[h][:], in_=w[h * 512 : (h + 1) * 512, :].rearrange("(p j) k -> p (j k)", j=4))
 
-        def col_load(dst, v):
-            nc.scalar.dma_start(out=dst, in_=v.rearrange("(a p i) -> p a i", p=P, i=4))
+        def col_load(queue, dst, v):
+            queue.dma_start(out=dst, in_=v.rearrange("(a p i) -> p a i", p=P, i=4))
 
         g_col = keep.tile([P, NH, 4], BF16, align_bytes=64, name="g_col")
         y_col = keep.tile([P, NCH, 4], BF16, align_bytes=64, name="y_col")
@@ -127,10 +130,19 @@ def tile_ordinaldepththresholdfeaturegradient_x1_kernel(tc, x, g, w, s, b, y, t,
                 )
                 free.append(xts[(c, i)][1])
 
-        def x_quant(c):
+        def x_planes(c):
             codes = work.tile([P, NH, CH], U32, align_bytes=64, name="x_codes")
             scales = work.tile([P, NH, CH], U8, align_bytes=64, name="x_scales")
             x_q[c] = (codes, scales)
+            return codes, scales
+
+        def x_quant_part(c, i):
+            tp, h = i // 2, i % 2
+            rows = slice(HALF * tp, HALF * (tp + 1))
+            quantise(x_q[c][0][:, h, rows], x_q[c][1][:, h, rows], x_gr[c][:, h, rows, :].rearrange("p n j -> p (n j)"))
+
+        def x_quant(c):
+            codes, scales = x_planes(c)
             quantise(
                 codes[:].rearrange("p h n -> p (h n)"),
                 scales[:].rearrange("p h n -> p (h n)"),
@@ -155,12 +167,12 @@ def tile_ordinaldepththresholdfeaturegradient_x1_kernel(tc, x, g, w, s, b, y, t,
             free.append(wts[(h, jp)][1])
 
         g_bc = keep.tile([P, D], BF16, align_bytes=64, name="g_bc")
-        g_rows = keep.tile([P, 2], F32, align_bytes=64, name="g_rows")
+        g_rows = keep.tile([P, 4], F32, align_bytes=64, name="g_rows")
 
         def g_turn():
-            turned_g, bank = take_bank([P, 2, P], BF16)
-            for j in range(2):
-                nc.tensor.transpose(turned_g[:, j, :], g_bc[:, TURNED + j * P : TURNED + (j + 1) * P], id16[:])
+            turned_g, bank = take_bank([P, 4, P], BF16)
+            for j in range(4):
+                nc.tensor.transpose(turned_g[:, j, :], g_bc[:, 512 + j * P : 512 + (j + 1) * P], id16[:])
             nc.scalar.copy(out=g_rows[:], in_=turned_g[:, :, 0])
             free.append(bank)
 
@@ -168,8 +180,8 @@ def tile_ordinaldepththresholdfeaturegradient_x1_kernel(tc, x, g, w, s, b, y, t,
         ds = {}
         zs = {}
 
-        def labels(hf):
-            cols = slice(hf * N // 2, (hf + 1) * N // 2)
+        def labels(c0, c1):
+            cols = slice(c0 * CH, c1 * CH)
             for q in LAST_FIRST:
                 nc.vector.tensor_scalar(
                     out=ls[:, q, cols],
@@ -185,10 +197,11 @@ def tile_ordinaldepththresholdfeaturegradient_x1_kernel(tc, x, g, w, s, b, y, t,
                 ds[(c, name)] = work.tile(shape, dtype, align_bytes=64, name=name)
             return ds[(c, name)]
 
-        def mm1s(c, qs=range(4)):
+        def mm1s(c, qs=range(4), hs=range(NH)):
             for q in qs:
-                zs[(c, q)] = take_bank([P, CH])
-                for h in range(NH):
+                for h in hs:
+                    if h == 0:
+                        zs[(c, q)] = take_bank([P, CH])
                     nc.tensor.matmul_mx(
                         out=zs[(c, q)][0][:],
                         lhsT=w_codes[:, h, q * P : (q + 1) * P].bitcast(FP8X4),
@@ -236,7 +249,8 @@ def tile_ordinaldepththresholdfeaturegradient_x1_kernel(tc, x, g, w, s, b, y, t,
                 op0=ALU.mult,
                 op1=ALU.add,
             )
-            inter(dst, src, mid, hi)
+            if mid < hi:
+                inter(dst, src, mid, hi)
 
         def d_inter(c, pool_rows):
             inter_shared(d_tile(c, "d_gr", [P, CH, 4], BF16), ds[(c, "d16")], 0, pool_rows, CH)
@@ -250,13 +264,13 @@ def tile_ordinaldepththresholdfeaturegradient_x1_kernel(tc, x, g, w, s, b, y, t,
 
         outp = {}
         banks = {}
+        o_codes = keep.tile([P, NCH, D], U32, align_bytes=64, name="o_codes")
         o_scales = keep.tile([P, D], U8, align_bytes=64, name="o_scales")
 
         def o_alloc(c, dh):
             outp[(c, dh)] = dict(
                 o=big.tile([P, 4, 512], F32, align_bytes=64, name="big"),
                 gr=outs.tile([P, 512, 4], BF16, align_bytes=64, name="o_gr"),
-                codes=keep.tile([P, 512], U32, align_bytes=64, name="o_codes%d%d" % (c, dh)),
             )
 
         def mm2(out, c, tt, d0, d1):
@@ -300,8 +314,8 @@ def tile_ordinaldepththresholdfeaturegradient_x1_kernel(tc, x, g, w, s, b, y, t,
                 for tt in range(2):
                     mm2(banks[(c, dh, tp, lo)][0][:, tt, :], c, 2 * tp + tt, dh * 512 + lo, dh * 512 + lo + HALF)
 
-        def pair_muls(c, dh, lo):
-            for tp in (1, 0):
+        def pair_muls(c, dh, lo, tps=(1, 0)):
+            for tp in tps:
                 nc.vector.tensor_tensor(
                     out=outp[(c, dh)]["o"][:, 2 * tp : 2 * tp + 2, lo : lo + HALF],
                     in0=banks[(c, dh, tp, lo)][0][:],
@@ -309,15 +323,16 @@ def tile_ordinaldepththresholdfeaturegradient_x1_kernel(tc, x, g, w, s, b, y, t,
                     op=ALU.mult,
                 )
                 free.append(banks[(c, dh, tp, lo)][1])
-            o_store(c, dh, 0, 4, lo, lo + HALF)
+            if len(tps) == 2 or 0 in tps:
+                o_store(c, dh, 0, 4, lo, lo + HALF)
 
         turned = {}
+        back = {}
 
-        def turned_products(c):
-            o_alloc(c, 1)
-            for j in range(2):
+        def turned_products(c, js):
+            for j in js:
                 turned[(c, j)] = take_bank([P, CH])
-                cols = slice(TURNED + j * P, TURNED + (j + 1) * P)
+                cols = slice(512 + j * P, 512 + (j + 1) * P)
                 nc.tensor.matmul_mx(
                     out=turned[(c, j)][0][:],
                     lhsT=wt_codes[:, cols].bitcast(FP8X4),
@@ -328,62 +343,62 @@ def tile_ordinaldepththresholdfeaturegradient_x1_kernel(tc, x, g, w, s, b, y, t,
                     stop=True,
                 )
 
-        def turned_scale(c):
-            for j in (1, 0):
+        def turned_scale(c, js):
+            for j in js:
                 o, bank = turned[(c, j)]
-                ot = work.tile([P, 4, P], F32, align_bytes=64, name="o_turned")
+                ot = work.tile([P, 4, P], F32, align_bytes=64, name="o_turned", bufs=4)
                 nc.scalar.activation(out=ot[:].rearrange("p t m -> p (t m)"), in_=o[:], func=ACT.Copy, scale=g_rows[:, j : j + 1])
                 free.append(bank)
                 turned[(c, j)] = ot
 
-        def turned_back(c):
-            back = {}
-            for j in (1, 0):
-                back[j] = take_bank([P, 4, P])
+        def turn_back(c, js):
+            for j in js:
+                back[(c, j)] = take_bank([P, 4, P])
                 for tt in range(4):
-                    nc.tensor.transpose(back[j][0][:, tt, :], turned[(c, j)][:, tt, :], id32[:])
-            for j in (0, 1):
-                nc.scalar.copy(out=outp[(c, 1)]["o"][:, :, HALF + j * P : HALF + (j + 1) * P], in_=back[j][0][:])
-                free.append(back[j][1])
-            o_store(c, 1, 0, 4, HALF, 512)
+                    nc.tensor.transpose(back[(c, j)][0][:, tt, :], turned[(c, j)][:, tt, :], id32[:])
+
+        def back_copies(c, js):
+            for j in js:
+                cols = slice(j * P, (j + 1) * P)
+                nc.scalar.copy(out=outp[(c, 1)]["o"][:, :, cols], in_=back[(c, j)][0][:])
+                nc.scalar.copy(out=outp[(c, 1)]["gr"][:, cols, :], in_=back[(c, j)][0][:].rearrange("p t m -> p m t"))
+                free.append(back[(c, j)][1])
+            o_store(c, 1, 0, 4, min(js) * P, (max(js) + 1) * P)
 
         def o_inter(c, dh, lo=0, hi=512):
             inter(outp[(c, dh)]["gr"], outp[(c, dh)]["o"], lo, hi)
 
-        def o_inter_shared(c, dh, hi):
-            inter_shared(outp[(c, dh)]["gr"], outp[(c, dh)]["o"], 0, O_POOL, hi)
+        def o_inter_shared(c, dh, lo, mid, hi):
+            inter_shared(outp[(c, dh)]["gr"], outp[(c, dh)]["o"], lo, mid, hi)
 
         def o_quant(c, dh, lo=0, hi=512):
             e = outp[(c, dh)]
             quantise(
-                e["codes"][:, lo:hi],
+                o_codes[:, c, dh * 512 + lo : dh * 512 + hi],
                 o_scales[4 * c : P, dh * 512 + lo : dh * 512 + hi],
                 e["gr"][:, lo:hi, :].rearrange("p d j -> p (d j)"),
             )
 
-        def code_store(c, dh):
+        def code_store(c, lo=0, hi=D):
             nc.sync.dma_start(
-                out=out_1[c, :, dh * 512 : (dh + 1) * 512, :].rearrange("p m t -> p (m t)").bitcast(I32),
-                in_=outp[(c, dh)]["codes"][:].bitcast(I32),
+                out=out_1[c, :, lo:hi, :].rearrange("p m t -> p (m t)").bitcast(I32),
+                in_=o_codes[:, c, lo:hi].bitcast(I32),
             )
 
-        def o_pack(c, dh):
-            o_quant(c, dh)
-            code_store(c, dh)
-
-        x_load(0, 0, 1)
-        col_load(g_col[:], g)
-        x_load(0, 1, 2)
-        col_load(t_col[:].unsqueeze(1), t)
         w_load(0)
-        col_load(s_col[:].unsqueeze(1), s)
+        col_load(nc.scalar, g_col[:], g)
+        x_load(0, 0, 1)
+        x_load(0, 1, 2)
         w_load(1)
-        col_load(y_col[:], y)
-        x_load(1, 0, 2)
-        col_load(b_col[:].unsqueeze(1), b)
-        for c in range(2, NCH):
-            x_load(c, 0, 2)
+        x_load(1, 0, 1)
+        col_load(nc.sync, y_col[:], y)
+        col_load(nc.sync, s_col[:].unsqueeze(1), s)
+        col_load(nc.sync, b_col[:].unsqueeze(1), b)
+        col_load(nc.sync, t_col[:].unsqueeze(1), t)
+        x_load(1, 1, 2)
+        x_load(2, 0, 2)
         nc.sync.dma_start(out=g_bc[:], in_=g.partition_broadcast(P))
+        x_load(3, 0, 2)
         nc.vector.memset(warm[:], 0.0)
         nc.scalar.activation(out=warm2[:], in_=warm[:], func=ACT.Sigmoid)
         make_identity(nc, id32[:])
@@ -391,118 +406,145 @@ def tile_ordinaldepththresholdfeaturegradient_x1_kernel(tc, x, g, w, s, b, y, t,
         for c in range(NCH):
             x_gr[c] = big.tile([P, NH, CH, 4], BF16, align_bytes=64, name="big")
 
+        def w_quant(h):
+            quantise(w_codes[:, h], w_scales[:, h], w_gr[:, h].rearrange("p k j -> p (k j)"))
+
+        def wt_quant():
+            quantise(wt_codes[:], wt_scales[:], wt_gr[:].rearrange("p d j -> p (d j)"))
+
+        wt_turn(0, 0)
+        wt_turn(0, 1)
+        dst, src = w_views(0)
+        nc.vector.tensor_copy(out=dst, in_=src)
         x_turns(0)
-        x_muls(0, (0, 1, 3, 2))
+        wt_copy(0, 0)
+        wt_copy(0, 1)
+        w_quant(0)
+        wt_turn(1, 0)
+        wt_turn(1, 1)
+        x_planes(0)
+        for tp in range(2):
+            x_muls(0, (2 * tp, 2 * tp + 1))
+            x_quant_part(0, 2 * tp)
+            x_quant_part(0, 2 * tp + 1)
+        dst, src = w_views(1)
+        nc.scalar.copy(out=dst, in_=src)
+        x_turns(1, (0, 1))
+        y_spread(0)
+        y_spread(1)
+        mm1s(0, (0, 1), (0,))
+        wt_copy(1, 1)
+        wt_copy(1, 0)
+        x_muls(1, (1, 0))
+        x_turns(1, (2, 3))
+        w_quant(1)
         nc.scalar.copy(out=s32[:], in_=s_col[:])
         nc.scalar.copy(out=t32[:], in_=t_col[:])
-        dst, src = w_views(0)
-        nc.scalar.copy(out=dst, in_=src)
-        for h in range(NH):
-            wt_turn(h, 0)
-            wt_turn(h, 1)
-            y_spread(h)
         y_copy(0)
-        for h in range(NH):
-            wt_copy(h, 1)
-            wt_copy(h, 0)
         y_copy(1)
-        dst, src = w_views(1)
-        nc.vector.tensor_copy(out=dst, in_=src)
-        x_turns(1)
-        x_quant(0)
-        quantise(
-            w_codes[:].rearrange("p h k -> p (h k)"),
-            w_scales[:].rearrange("p h k -> p (h k)"),
-            w_gr[:].rearrange("p h k j -> p (h k j)"),
-        )
-
-        mm1s(0, (0, 1, 2))
-        labels(0)
-        x_muls(1)
-        x_turns(2, (0, 1))
-        mm1s(0, (3,))
-        x_turns(2, (2, 3))
+        mm1s(0, (0, 1), (1,))
+        mm1s(0, (2, 3))
+        wt_quant()
+        labels(0, 1)
+        x_muls(1, (3, 2))
         sigms(0, range(4))
-        quantise(wt_codes[:], wt_scales[:], wt_gr[:].rearrange("p d j -> p (d j)"))
-        x_quant(1)
-        mm1s(1, (0, 1))
-        x_turns(3, (0, 1))
-        d_subs(0, (2, 1, 0, 3))
-        d_inter(0, D_POOL_SHORT)
-        x_muls(2)
-        mm1s(1, (2, 3))
-        sigms(1)
-        x_turns(3, (2, 3))
+        x_turns(2)
         g_turn()
-        labels(1)
+        labels(1, 2)
+        x_quant(1)
+        mm1s(1)
+        d_subs(0, (3, 2, 1, 0))
+        d_inter(0, D_POOL_FIRST)
+        x_muls(2)
+        sigms(1)
 
+        T = (2, 3)
         d_quant(0)
-        turned_products(0)
-        turned_scale(0)
-        turned_back(0)
+        o_alloc(0, 1)
+        turned_products(0, T)
         mm2s(0, 0)
+        turned_scale(0, T)
         x_quant(2)
+        turn_back(0, T)
+        mm1s(2, (0, 1))
         d_subs(1)
-        d_inter(1, D_POOL_SHORT)
-        x_muls(3)
-        mm1s(2)
-        sigms(2)
         o_muls(0, 0)
         pair_products(0, 1, 0)
+        back_copies(0, T)
+        d_inter(1, D_POOL_LONG)
+        mm1s(2, (2, 3))
+        sigms(2)
+        pair_muls(0, 1, 0)
+        x_turns(3, (0, 1))
+
+        d_quant(1)
+        o_alloc(1, 1)
+        turned_products(1, T)
+        x_turns(3, (2, 3))
+        pair_products(1, 1, 0)
+        labels(2, 4)
+        turned_scale(1, T)
         o_inter(0, 0)
+        d_subs(2)
+        d_inter(2, D_POOL_MID)
+        turn_back(1, T)
+        x_muls(3)
+        pair_muls(1, 1, 0, (1,))
+        back_copies(1, T)
+        mm2s(1, 0)
+        o_inter(0, 1, 0, HALF)
         x_quant(3)
         mm1s(3, (0, 1))
-        d_quant(1)
-        mm2s(1, 0)
-        d_subs(2)
-        d_inter(2, D_POOL_LONG)
-        pair_muls(0, 1, 0)
-
-        turned_products(1)
+        d_quant(2)
+        o_quant(0, 0)
+        pair_muls(1, 1, 0, (0,))
         sigms(3, (1, 0))
         mm1s(3, (2, 3))
-        turned_scale(1)
         sigms(3, (3, 2))
+        o_inter_shared(1, 1, 0, O_POOL, HALF)
         o_muls(1, 0)
-        turned_back(1)
-        pair_products(1, 1, 0)
-        o_inter(0, 1)
-        d_quant(2)
-        mm2s(2, 0)
-        o_pack(0, 0)
-        d_subs(3)
-        d_inter(3, D_POOL_LONG)
-        o_inter(1, 0)
-        pair_muls(1, 1, 0)
 
+        o_alloc(2, 1)
+        turned_products(2, T)
+        mm2s(2, 0)
+        turned_scale(2, T)
+        pair_products(2, 1, 0)
+        o_quant(0, 1)
+        code_store(0)
+        o_inter(1, 0)
+        d_subs(3)
+        d_inter(3, D_POOL_LAST)
+        turn_back(2, T)
+        pair_muls(2, 1, 0)
         o_muls(2, 0)
-        mm2s(2, 1)
-        o_inter(1, 1)
+        back_copies(2, T)
+        o_inter(2, 1, 0, HALF)
         o_inter(2, 0)
         d_quant(3)
-        o_pack(0, 1)
         o_alloc(3, 0)
         o_alloc(3, 1)
-        for lo in (0, HALF):
-            pair_products(3, 0, lo)
-        o_pack(1, 0)
-        o_muls(2, 1)
-        for lo in (0, HALF):
-            pair_products(3, 1, lo)
-        o_inter_shared(2, 1, 512)
         for dh in range(2):
-            pair_muls(3, dh, HALF)
-            o_inter(3, dh, HALF, 512)
-            pair_muls(3, dh, 0)
-            if dh == 0:
-                o_inter_shared(3, 0, HALF)
-            else:
-                o_inter(3, 1, 0, HALF)
-        for c, dh in ((1, 1), (2, 0), (2, 1), (3, 0)):
-            o_pack(c, dh)
-        o_quant(3, 1, HALF, 512)
+            for lo in (0, HALF):
+                pair_products(3, dh, lo)
+        o_quant(1, 1)
+        o_quant(1, 0)
+        code_store(1)
+        pair_muls(3, 0, 0, (0, 1))
+        o_inter_shared(3, 0, 0, HALF, HALF)
+        pair_muls(3, 0, HALF)
+        o_inter_shared(3, 0, HALF, HALF + O_POOL_LAST, 512)
+        pair_muls(3, 1, 0)
+        o_inter(3, 1, 0, HALF)
+        pair_muls(3, 1, HALF)
+        o_inter(3, 1, HALF, 512)
+        o_quant(2, 0)
+        o_quant(2, 1)
+        code_store(2)
+        o_quant(3, 0)
         o_quant(3, 1, 0, HALF)
-        code_store(3, 1)
+        code_store(3, 0, D - HALF)
+        o_quant(3, 1, HALF, 512)
+        code_store(3, D - HALF, D)
         for qd in range(4):
             queue = nc.scalar if qd % 2 else nc.sync
             queue.dma_start(

@@ -25,9 +25,8 @@ LAST_FIRST = (3, 2, 1, 0)
 
 RUN = 4
 D_POOL_FIRST = 224
-D_POOL_MID = 368
+D_POOL_MID = 336
 D_POOL_LAST = 416
-O_POOL_LAST = 32
 D_POOL_LONG = 416
 O_POOL = 192
 O_GR_BUFS = 7
@@ -45,8 +44,8 @@ def tile_ordinaldepththresholdfeaturegradient_x1_kernel(tc, x, g, w, s, b, y, t,
 
         free = list(range(8))
 
-        def take_bank(shape, dtype=F32):
-            i = free.pop(0)
+        def take_bank(shape, dtype=F32, skip=0):
+            i = free.pop(skip)
             return psum.tile(shape, dtype, name="bank%d" % i), i
 
         x_raw = {}
@@ -83,13 +82,16 @@ def tile_ordinaldepththresholdfeaturegradient_x1_kernel(tc, x, g, w, s, b, y, t,
         ys = {}
 
         def y_spread(hf):
-            ys[hf] = take_bank([P, N // 2], BF16)
-            for i in range(8):
-                c, tt = 2 * hf + i // 4, i % 4
-                nc.tensor.transpose(ys[hf][0][:, i * P : (i + 1) * P], y_col[:, c, tt : tt + 1].to_broadcast([P, P]), id16[:])
+            ys[hf] = take_bank([P, 4, P])
+            words = y_col[:].rearrange("p c t -> p (c t)").bitcast(F32)
+            for i in range(4):
+                nc.tensor.transpose(ys[hf][0][:, i, :], words[:, 4 * hf + i : 4 * hf + i + 1].to_broadcast([P, P]), id32[:])
 
         def y_copy(hf):
-            nc.scalar.copy(out=y_bc[:, hf * N // 2 : (hf + 1) * N // 2], in_=ys[hf][0][:])
+            nc.scalar.copy(
+                out=y_bc[:, hf * N // 2 : (hf + 1) * N // 2].rearrange("p (i e m) -> p i e m", i=4, e=2),
+                in_=ys[hf][0][:].bitcast(BF16).rearrange("p i (m e) -> p i e m", e=2),
+            )
             free.append(ys[hf][1])
 
         w_gr = big.tile([P, NH, K, 4], BF16, align_bytes=64, name="big")
@@ -169,12 +171,16 @@ def tile_ordinaldepththresholdfeaturegradient_x1_kernel(tc, x, g, w, s, b, y, t,
         g_bc = keep.tile([P, D], BF16, align_bytes=64, name="g_bc")
         g_rows = keep.tile([P, 4], F32, align_bytes=64, name="g_rows")
 
+        gs = []
+
         def g_turn():
-            turned_g, bank = take_bank([P, 4, P], BF16)
+            gs.extend(take_bank([P, 4, P], BF16))
             for j in range(4):
-                nc.tensor.transpose(turned_g[:, j, :], g_bc[:, 512 + j * P : 512 + (j + 1) * P], id16[:])
-            nc.scalar.copy(out=g_rows[:], in_=turned_g[:, :, 0])
-            free.append(bank)
+                nc.tensor.transpose(gs[0][:, j, :], g_bc[:, 512 + j * P : 512 + (j + 1) * P], id16[:])
+
+        def g_copy():
+            nc.scalar.copy(out=g_rows[:], in_=gs[0][:, :, 0])
+            free.append(gs[1])
 
         ls = keep.tile([P, 4, N], BF16, align_bytes=64, name="ls")
         ds = {}
@@ -197,11 +203,11 @@ def tile_ordinaldepththresholdfeaturegradient_x1_kernel(tc, x, g, w, s, b, y, t,
                 ds[(c, name)] = work.tile(shape, dtype, align_bytes=64, name=name)
             return ds[(c, name)]
 
-        def mm1s(c, qs=range(4), hs=range(NH)):
+        def mm1s(c, qs=range(4), hs=range(NH), skip=0):
             for q in qs:
                 for h in hs:
                     if h == 0:
-                        zs[(c, q)] = take_bank([P, CH])
+                        zs[(c, q)] = take_bank([P, CH], skip=skip)
                     nc.tensor.matmul_mx(
                         out=zs[(c, q)][0][:],
                         lhsT=w_codes[:, h, q * P : (q + 1) * P].bitcast(FP8X4),
@@ -361,7 +367,7 @@ def tile_ordinaldepththresholdfeaturegradient_x1_kernel(tc, x, g, w, s, b, y, t,
             for j in js:
                 cols = slice(j * P, (j + 1) * P)
                 nc.scalar.copy(out=outp[(c, 1)]["o"][:, :, cols], in_=back[(c, j)][0][:])
-                nc.scalar.copy(out=outp[(c, 1)]["gr"][:, cols, :], in_=back[(c, j)][0][:].rearrange("p t m -> p m t"))
+                inter(outp[(c, 1)]["gr"][:, cols, :], back[(c, j)][0], 0, P)
                 free.append(back[(c, j)][1])
             o_store(c, 1, 0, 4, min(js) * P, (max(js) + 1) * P)
 
@@ -385,17 +391,17 @@ def tile_ordinaldepththresholdfeaturegradient_x1_kernel(tc, x, g, w, s, b, y, t,
                 in_=o_codes[:, c, lo:hi].bitcast(I32),
             )
 
-        w_load(0)
-        col_load(nc.scalar, g_col[:], g)
         x_load(0, 0, 1)
+        col_load(nc.scalar, g_col[:], g)
         x_load(0, 1, 2)
+        col_load(nc.scalar, y_col[:], y)
+        w_load(0)
+        col_load(nc.scalar, t_col[:].unsqueeze(1), t)
         w_load(1)
+        col_load(nc.scalar, s_col[:].unsqueeze(1), s)
         x_load(1, 0, 1)
-        col_load(nc.sync, y_col[:], y)
-        col_load(nc.sync, s_col[:].unsqueeze(1), s)
-        col_load(nc.sync, b_col[:].unsqueeze(1), b)
-        col_load(nc.sync, t_col[:].unsqueeze(1), t)
         x_load(1, 1, 2)
+        col_load(nc.sync, b_col[:].unsqueeze(1), b)
         x_load(2, 0, 2)
         nc.sync.dma_start(out=g_bc[:], in_=g.partition_broadcast(P))
         x_load(3, 0, 2)
@@ -406,57 +412,67 @@ def tile_ordinaldepththresholdfeaturegradient_x1_kernel(tc, x, g, w, s, b, y, t,
         for c in range(NCH):
             x_gr[c] = big.tile([P, NH, CH, 4], BF16, align_bytes=64, name="big")
 
-        def w_quant(h):
-            quantise(w_codes[:, h], w_scales[:, h], w_gr[:, h].rearrange("p k j -> p (k j)"))
+        def w_quant(h, lo=0, hi=K, held=None):
+            src = w_gr[:, h if held is None else held, lo:hi, :]
+            quantise(w_codes[:, h, lo:hi], w_scales[:, h, lo:hi], src.rearrange("p k j -> p (k j)"))
 
         def wt_quant():
             quantise(wt_codes[:], wt_scales[:], wt_gr[:].rearrange("p d j -> p (d j)"))
 
+        x_turns(0, (0, 1))
+        y_spread(0)
+        x_turns(0, (2, 3))
+        y_spread(1)
+        y_copy(0)
+        nc.scalar.copy(out=s32[:], in_=s_col[:])
+        nc.scalar.copy(out=t32[:], in_=t_col[:])
         wt_turn(0, 0)
         wt_turn(0, 1)
-        dst, src = w_views(0)
-        nc.vector.tensor_copy(out=dst, in_=src)
-        x_turns(0)
-        wt_copy(0, 0)
-        wt_copy(0, 1)
-        w_quant(0)
-        wt_turn(1, 0)
-        wt_turn(1, 1)
         x_planes(0)
         for tp in range(2):
             x_muls(0, (2 * tp, 2 * tp + 1))
             x_quant_part(0, 2 * tp)
             x_quant_part(0, 2 * tp + 1)
-        dst, src = w_views(1)
+        wt_turn(1, 0)
+        wt_turn(1, 1)
+        dst, src = w_views(0)
         nc.scalar.copy(out=dst, in_=src)
-        x_turns(1, (0, 1))
-        y_spread(0)
-        y_spread(1)
-        mm1s(0, (0, 1), (0,))
-        wt_copy(1, 1)
-        wt_copy(1, 0)
-        x_muls(1, (1, 0))
-        x_turns(1, (2, 3))
-        w_quant(1)
-        nc.scalar.copy(out=s32[:], in_=s_col[:])
-        nc.scalar.copy(out=t32[:], in_=t_col[:])
-        y_copy(0)
         y_copy(1)
-        mm1s(0, (0, 1), (1,))
-        mm1s(0, (2, 3))
-        wt_quant()
-        labels(0, 1)
-        x_muls(1, (3, 2))
-        sigms(0, range(4))
-        x_turns(2)
-        g_turn()
-        labels(1, 2)
+        dst, src = w_views(1)
+        nc.scalar.copy(out=dst[:, :, 0:2], in_=src[:, :, 0:2])
+        x_turns(1)
+        labels(0, 2)
+        w_quant(0)
+        nc.gpsimd.tensor_scalar(
+            out=w_gr[:, 0, HALF:K, :].rearrange("p (q m) j -> p m q j", q=2),
+            in0=w_raw[1][:].rearrange("p (j m q) -> p m q j", j=4, q=4)[:, :, 2:4, :],
+            scalar1=1.0,
+            scalar2=-0.0,
+            op0=ALU.mult,
+            op1=ALU.add,
+        )
+        x_muls(1, (1, 0, 3, 2))
+        mm1s(0, range(4), (0,))
+        for h in range(NH):
+            wt_copy(h, 1)
+            wt_copy(h, 0)
+        w_quant(1, 0, HALF)
+        w_quant(1, HALF, K, 0)
+        mm1s(0, range(4), (1,))
         x_quant(1)
-        mm1s(1)
-        d_subs(0, (3, 2, 1, 0))
+        x_turns(2, (0, 1))
+        mm1s(1, (0, 1))
+        sigms(0, range(4))
+        x_turns(2, (2, 3))
+        wt_quant()
+        g_turn()
+        sigms(1, (1, 0))
+        g_copy()
+        d_subs(0, (1, 0, 3, 2))
         d_inter(0, D_POOL_FIRST)
         x_muls(2)
-        sigms(1)
+        mm1s(1, (2, 3), skip=4)
+        sigms(1, (2, 3))
 
         T = (2, 3)
         d_quant(0)
@@ -467,7 +483,7 @@ def tile_ordinaldepththresholdfeaturegradient_x1_kernel(tc, x, g, w, s, b, y, t,
         x_quant(2)
         turn_back(0, T)
         mm1s(2, (0, 1))
-        d_subs(1)
+        d_subs(1, LAST_FIRST)
         o_muls(0, 0)
         pair_products(0, 1, 0)
         back_copies(0, T)
@@ -483,38 +499,38 @@ def tile_ordinaldepththresholdfeaturegradient_x1_kernel(tc, x, g, w, s, b, y, t,
         x_turns(3, (2, 3))
         pair_products(1, 1, 0)
         labels(2, 4)
-        turned_scale(1, T)
         o_inter(0, 0)
+        turned_scale(1, T)
         d_subs(2)
         d_inter(2, D_POOL_MID)
         turn_back(1, T)
         x_muls(3)
         pair_muls(1, 1, 0, (1,))
-        back_copies(1, T)
         mm2s(1, 0)
-        o_inter(0, 1, 0, HALF)
-        x_quant(3)
-        mm1s(3, (0, 1))
+        back_copies(1, T)
         d_quant(2)
-        o_quant(0, 0)
-        pair_muls(1, 1, 0, (0,))
-        sigms(3, (1, 0))
-        mm1s(3, (2, 3))
-        sigms(3, (3, 2))
-        o_inter_shared(1, 1, 0, O_POOL, HALF)
-        o_muls(1, 0)
-
         o_alloc(2, 1)
         turned_products(2, T)
+        x_quant(3)
+        o_inter(0, 1, 0, HALF)
+        turned_scale(2, (2,))
+        mm1s(3, (0, 1))
+        o_quant(0, 0)
+        pair_muls(1, 1, 0, (0,))
+        o_muls(1, 0)
+        mm1s(3, (2, 3))
+        sigms(3, range(4))
+
         mm2s(2, 0)
-        turned_scale(2, T)
         pair_products(2, 1, 0)
+        turned_scale(2, (3,))
+        turn_back(2, T)
+        o_inter_shared(1, 1, 0, O_POOL, HALF)
         o_quant(0, 1)
         code_store(0)
         o_inter(1, 0)
-        d_subs(3)
+        d_subs(3, LAST_FIRST)
         d_inter(3, D_POOL_LAST)
-        turn_back(2, T)
         pair_muls(2, 1, 0)
         o_muls(2, 0)
         back_copies(2, T)
@@ -532,7 +548,7 @@ def tile_ordinaldepththresholdfeaturegradient_x1_kernel(tc, x, g, w, s, b, y, t,
         pair_muls(3, 0, 0, (0, 1))
         o_inter_shared(3, 0, 0, HALF, HALF)
         pair_muls(3, 0, HALF)
-        o_inter_shared(3, 0, HALF, HALF + O_POOL_LAST, 512)
+        o_inter(3, 0, HALF, 512)
         pair_muls(3, 1, 0)
         o_inter(3, 1, 0, HALF)
         pair_muls(3, 1, HALF)

@@ -109,10 +109,10 @@ def tile_ordinaldepththresholdfeaturegradient_x1_kernel(tc, x, g, w, s, b, y, t,
         x_q = {}
         xts = {}
 
-        def x_turns(c, parts=range(4)):
+        def x_turns(c, parts=range(4), skip=0):
             for i in parts:
                 tp, h = i // 2, i % 2
-                xts[(c, i)] = take_bank([P, 2, HALF])
+                xts[(c, i)] = take_bank([P, 2, HALF], skip=skip)
                 for tt in range(2):
                     for u in range(2):
                         nc.tensor.transpose(
@@ -186,9 +186,9 @@ def tile_ordinaldepththresholdfeaturegradient_x1_kernel(tc, x, g, w, s, b, y, t,
         ds = {}
         zs = {}
 
-        def labels(c0, c1):
+        def labels(c0, c1, qs=LAST_FIRST):
             cols = slice(c0 * CH, c1 * CH)
-            for q in LAST_FIRST:
+            for q in qs:
                 nc.vector.tensor_scalar(
                     out=ls[:, q, cols],
                     in0=y_bc[:, cols],
@@ -290,10 +290,9 @@ def tile_ordinaldepththresholdfeaturegradient_x1_kernel(tc, x, g, w, s, b, y, t,
                 stop=True,
             )
 
-        def mm2s(c, dh):
-            o_alloc(c, dh)
-            for tt in range(4):
-                banks[(c, dh, tt)] = take_bank([P, 512])
+        def mm2s(c, dh, tts=range(4), skip=0):
+            for tt in tts:
+                banks[(c, dh, tt)] = take_bank([P, 512], skip=skip)
                 mm2(banks[(c, dh, tt)][0][:], c, tt, dh * 512, (dh + 1) * 512)
 
         def o_store(c, dh, t0, t1, lo, hi):
@@ -302,8 +301,8 @@ def tile_ordinaldepththresholdfeaturegradient_x1_kernel(tc, x, g, w, s, b, y, t,
                 in_=outp[(c, dh)]["o"][:, t0:t1, lo:hi],
             )
 
-        def o_muls(c, dh):
-            for tt in LAST_FIRST:
+        def o_muls(c, dh, tts=LAST_FIRST):
+            for tt in tts:
                 nc.vector.tensor_tensor(
                     out=outp[(c, dh)]["o"][:, tt, :],
                     in0=banks[(c, dh, tt)][0][:],
@@ -314,9 +313,9 @@ def tile_ordinaldepththresholdfeaturegradient_x1_kernel(tc, x, g, w, s, b, y, t,
                 if tt % 2 == 0:
                     o_store(c, dh, tt, tt + 2, 0, 512)
 
-        def pair_products(c, dh, lo):
+        def pair_products(c, dh, lo, skip=0):
             for tp in range(2):
-                banks[(c, dh, tp, lo)] = take_bank([P, 2, HALF])
+                banks[(c, dh, tp, lo)] = take_bank([P, 2, HALF], skip=skip)
                 for tt in range(2):
                     mm2(banks[(c, dh, tp, lo)][0][:, tt, :], c, 2 * tp + tt, dh * 512 + lo, dh * 512 + lo + HALF)
 
@@ -331,6 +330,20 @@ def tile_ordinaldepththresholdfeaturegradient_x1_kernel(tc, x, g, w, s, b, y, t,
                 free.append(banks[(c, dh, tp, lo)][1])
             if len(tps) == 2 or 0 in tps:
                 o_store(c, dh, 0, 4, lo, lo + HALF)
+
+        def quad_products(c, j):
+            banks[(c, j)] = take_bank([P, 4, P])
+            for tt in range(4):
+                mm2(banks[(c, j)][0][:, tt, :], c, tt, 512 + j * P, 512 + (j + 1) * P)
+
+        def quad_mul(c, j):
+            nc.vector.tensor_tensor(
+                out=outp[(c, 1)]["o"][:, :, j * P : (j + 1) * P],
+                in0=banks[(c, j)][0][:],
+                in1=g_bc[:, 512 + j * P : 512 + (j + 1) * P].unsqueeze(1).to_broadcast([P, 4, P]),
+                op=ALU.mult,
+            )
+            free.append(banks[(c, j)][1])
 
         turned = {}
         back = {}
@@ -369,7 +382,6 @@ def tile_ordinaldepththresholdfeaturegradient_x1_kernel(tc, x, g, w, s, b, y, t,
                 nc.scalar.copy(out=outp[(c, 1)]["o"][:, :, cols], in_=back[(c, j)][0][:])
                 inter(outp[(c, 1)]["gr"][:, cols, :], back[(c, j)][0], 0, P)
                 free.append(back[(c, j)][1])
-            o_store(c, 1, 0, 4, min(js) * P, (max(js) + 1) * P)
 
         def o_inter(c, dh, lo=0, hi=512):
             inter(outp[(c, dh)]["gr"], outp[(c, dh)]["o"], lo, hi)
@@ -422,10 +434,9 @@ def tile_ordinaldepththresholdfeaturegradient_x1_kernel(tc, x, g, w, s, b, y, t,
         x_turns(0, (0, 1))
         y_spread(0)
         x_turns(0, (2, 3))
-        y_spread(1)
         y_copy(0)
-        nc.scalar.copy(out=s32[:], in_=s_col[:])
-        nc.scalar.copy(out=t32[:], in_=t_col[:])
+        nc.gpsimd.tensor_copy(out=t32[:], in_=t_col[:])
+        nc.gpsimd.tensor_copy(out=s32[:], in_=s_col[:])
         wt_turn(0, 0)
         wt_turn(0, 1)
         x_planes(0)
@@ -437,7 +448,6 @@ def tile_ordinaldepththresholdfeaturegradient_x1_kernel(tc, x, g, w, s, b, y, t,
         wt_turn(1, 1)
         dst, src = w_views(0)
         nc.scalar.copy(out=dst, in_=src)
-        y_copy(1)
         dst, src = w_views(1)
         nc.scalar.copy(out=dst[:, :, 0:2], in_=src[:, :, 0:2])
         x_turns(1)
@@ -453,7 +463,7 @@ def tile_ordinaldepththresholdfeaturegradient_x1_kernel(tc, x, g, w, s, b, y, t,
         )
         x_muls(1, (1, 0, 3, 2))
         mm1s(0, range(4), (0,))
-        for h in range(NH):
+        for h in (1, 0):
             wt_copy(h, 1)
             wt_copy(h, 0)
         w_quant(1, 0, HALF)
@@ -461,80 +471,94 @@ def tile_ordinaldepththresholdfeaturegradient_x1_kernel(tc, x, g, w, s, b, y, t,
         mm1s(0, range(4), (1,))
         x_quant(1)
         x_turns(2, (0, 1))
+        sigms(0)
         mm1s(1, (0, 1))
-        sigms(0, range(4))
         x_turns(2, (2, 3))
         wt_quant()
-        g_turn()
         sigms(1, (1, 0))
-        g_copy()
-        d_subs(0, (1, 0, 3, 2))
+        g_turn()
+        y_spread(1)
+        mm1s(1, (2, 3))
+        d_subs(0, range(4))
         d_inter(0, D_POOL_FIRST)
         x_muls(2)
-        mm1s(1, (2, 3), skip=4)
-        sigms(1, (2, 3))
+        sigms(1, (3, 2))
+        g_copy()
+        y_copy(1)
 
         T = (2, 3)
+        TB = (3, 2)
         d_quant(0)
         o_alloc(0, 1)
+        o_alloc(0, 0)
         turned_products(0, T)
         mm2s(0, 0)
-        turned_scale(0, T)
         x_quant(2)
-        turn_back(0, T)
         mm1s(2, (0, 1))
-        d_subs(1, LAST_FIRST)
-        o_muls(0, 0)
-        pair_products(0, 1, 0)
-        back_copies(0, T)
+        turned_scale(0, TB)
+        turn_back(0, TB)
+        sigms(2, (1, 0))
+        d_subs(1)
         d_inter(1, D_POOL_LONG)
+        o_muls(0, 0)
+        pair_products(0, 1, 0, skip=2)
         mm1s(2, (2, 3))
-        sigms(2)
-        pair_muls(0, 1, 0)
         x_turns(3, (0, 1))
+        back_copies(0, (2,))
+        sigms(2, (3, 2))
+        back_copies(0, (3,))
+        pair_muls(0, 1, 0)
+        o_store(0, 1, 0, 4, HALF, 512)
 
         d_quant(1)
         o_alloc(1, 1)
+        o_alloc(1, 0)
         turned_products(1, T)
-        x_turns(3, (2, 3))
+        x_turns(3, (2, 3), skip=1)
         pair_products(1, 1, 0)
-        labels(2, 4)
+        labels(2, 3)
+        turned_scale(1, TB)
+        turn_back(1, TB)
         o_inter(0, 0)
-        turned_scale(1, T)
         d_subs(2)
-        d_inter(2, D_POOL_MID)
-        turn_back(1, T)
+        d_inter(2, CH)
         x_muls(3)
-        pair_muls(1, 1, 0, (1,))
-        mm2s(1, 0)
+        mm2s(1, 0, (3,))
+        pair_muls(1, 1, 0)
+        o_muls(1, 0, (3,))
+        mm2s(1, 0, (0, 1, 2), skip=3)
         back_copies(1, T)
-        d_quant(2)
-        o_alloc(2, 1)
-        turned_products(2, T)
-        x_quant(3)
+        o_store(1, 1, 0, 4, HALF, 512)
         o_inter(0, 1, 0, HALF)
-        turned_scale(2, (2,))
-        mm1s(3, (0, 1))
+        x_quant(3)
+        mm1s(3)
+        d_quant(2)
+        labels(3, 4, (0, 1, 3, 2))
         o_quant(0, 0)
-        pair_muls(1, 1, 0, (0,))
-        o_muls(1, 0)
-        mm1s(3, (2, 3))
-        sigms(3, range(4))
+        o_alloc(2, 1)
+        o_alloc(2, 0)
+        turned_products(2, (3,))
+        o_muls(1, 0, (2, 1, 0))
+        sigms(3)
+        turned_scale(2, (3,))
 
         mm2s(2, 0)
         pair_products(2, 1, 0)
-        turned_scale(2, (3,))
-        turn_back(2, T)
-        o_inter_shared(1, 1, 0, O_POOL, HALF)
+        quad_products(2, 2)
+        turn_back(2, (3,))
         o_quant(0, 1)
         code_store(0)
         o_inter(1, 0)
-        d_subs(3, LAST_FIRST)
-        d_inter(3, D_POOL_LAST)
+        o_inter(1, 1, 0, HALF)
+        d_subs(3)
+        d_inter(3, CH)
+        quad_mul(2, 2)
+        back_copies(2, (3,))
         pair_muls(2, 1, 0)
-        o_muls(2, 0)
-        back_copies(2, T)
-        o_inter(2, 1, 0, HALF)
+        o_inter(2, 1, 0, HALF + P)
+        o_muls(2, 0, (3, 2))
+        o_store(2, 1, 0, 4, HALF, 512)
+        o_muls(2, 0, (1, 0))
         o_inter(2, 0)
         d_quant(3)
         o_alloc(3, 0)

@@ -27,6 +27,7 @@ RUN = 4
 D_POOL_FIRST = 224
 D_POOL_MID = 336
 D_POOL_LAST = 416
+D_POOL_WIDE = 448
 D_POOL_LONG = 416
 O_POOL = 192
 O_GR_BUFS = 7
@@ -521,7 +522,7 @@ def tile_ordinaldepththresholdfeaturegradient_x1_kernel(tc, x, g, w, s, b, y, t,
         turn_back(1, TB)
         o_inter(0, 0)
         d_subs(2)
-        d_inter(2, CH)
+        d_inter(2, D_POOL_WIDE)
         x_muls(3)
         mm2s(1, 0, (3,))
         pair_muls(1, 1, 0)
@@ -551,7 +552,7 @@ def tile_ordinaldepththresholdfeaturegradient_x1_kernel(tc, x, g, w, s, b, y, t,
         o_inter(1, 0)
         o_inter(1, 1, 0, HALF)
         d_subs(3)
-        d_inter(3, CH)
+        d_inter(3, D_POOL_WIDE)
         quad_mul(2, 2)
         back_copies(2, (3,))
         pair_muls(2, 1, 0)

@@ -25,7 +25,7 @@ LAST_FIRST = (3, 2, 1, 0)
 
 RUN = 4
 D_POOL_FIRST = 224
-D_POOL_MID = 336
+D_POOL_MID = 288
 D_POOL_LAST = 416
 D_POOL_WIDE = 448
 D_POOL_LONG = 416
@@ -435,6 +435,7 @@ def tile_ordinaldepththresholdfeaturegradient_x1_kernel(tc, x, g, w, s, b, y, t,
         x_turns(0, (0, 1))
         y_spread(0)
         x_turns(0, (2, 3))
+        y_spread(1)
         y_copy(0)
         nc.gpsimd.tensor_copy(out=t32[:], in_=t_col[:])
         nc.gpsimd.tensor_copy(out=s32[:], in_=s_col[:])
@@ -449,6 +450,7 @@ def tile_ordinaldepththresholdfeaturegradient_x1_kernel(tc, x, g, w, s, b, y, t,
         wt_turn(1, 1)
         dst, src = w_views(0)
         nc.scalar.copy(out=dst, in_=src)
+        y_copy(1)
         dst, src = w_views(1)
         nc.scalar.copy(out=dst[:, :, 0:2], in_=src[:, :, 0:2])
         x_turns(1)
@@ -475,17 +477,16 @@ def tile_ordinaldepththresholdfeaturegradient_x1_kernel(tc, x, g, w, s, b, y, t,
         sigms(0)
         mm1s(1, (0, 1))
         x_turns(2, (2, 3))
+        labels(2, 3)
         wt_quant()
         sigms(1, (1, 0))
-        g_turn()
-        y_spread(1)
         mm1s(1, (2, 3))
+        g_turn()
         d_subs(0, range(4))
         d_inter(0, D_POOL_FIRST)
         x_muls(2)
-        sigms(1, (3, 2))
         g_copy()
-        y_copy(1)
+        sigms(1, (3, 2))
 
         T = (2, 3)
         TB = (3, 2)
@@ -493,38 +494,34 @@ def tile_ordinaldepththresholdfeaturegradient_x1_kernel(tc, x, g, w, s, b, y, t,
         o_alloc(0, 1)
         o_alloc(0, 0)
         turned_products(0, T)
+        pair_products(0, 1, 0)
         mm2s(0, 0)
         x_quant(2)
-        mm1s(2, (0, 1))
         turned_scale(0, TB)
         turn_back(0, TB)
-        sigms(2, (1, 0))
         d_subs(1)
-        d_inter(1, D_POOL_LONG)
         o_muls(0, 0)
-        pair_products(0, 1, 0, skip=2)
-        mm1s(2, (2, 3))
-        x_turns(3, (0, 1))
+        mm1s(2)
+        d_inter(1, D_POOL_LONG)
         back_copies(0, (2,))
-        sigms(2, (3, 2))
-        back_copies(0, (3,))
         pair_muls(0, 1, 0)
+        sigms(2)
+        x_turns(3)
+        back_copies(0, (3,))
         o_store(0, 1, 0, 4, HALF, 512)
 
         d_quant(1)
         o_alloc(1, 1)
         o_alloc(1, 0)
         turned_products(1, T)
-        x_turns(3, (2, 3), skip=1)
         pair_products(1, 1, 0)
-        labels(2, 3)
-        turned_scale(1, TB)
-        turn_back(1, TB)
         o_inter(0, 0)
-        d_subs(2)
+        turned_scale(1, TB)
+        d_subs(2, range(4))
         d_inter(2, D_POOL_WIDE)
         x_muls(3)
-        mm2s(1, 0, (3,))
+        mm2s(1, 0, (3,), skip=2)
+        turn_back(1, TB)
         pair_muls(1, 1, 0)
         o_muls(1, 0, (3,))
         mm2s(1, 0, (0, 1, 2), skip=3)
@@ -538,28 +535,28 @@ def tile_ordinaldepththresholdfeaturegradient_x1_kernel(tc, x, g, w, s, b, y, t,
         o_quant(0, 0)
         o_alloc(2, 1)
         o_alloc(2, 0)
-        turned_products(2, (3,))
         o_muls(1, 0, (2, 1, 0))
-        sigms(3)
+        pair_products(2, 1, 0)
+        quad_products(2, 2)
+        sigms(3, (1, 0))
+        turned_products(2, (3,))
+        sigms(3, (3, 2))
         turned_scale(2, (3,))
 
         mm2s(2, 0)
-        pair_products(2, 1, 0)
-        quad_products(2, 2)
         turn_back(2, (3,))
         o_quant(0, 1)
         code_store(0)
-        o_inter(1, 0)
-        o_inter(1, 1, 0, HALF)
-        d_subs(3)
-        d_inter(3, D_POOL_WIDE)
         quad_mul(2, 2)
-        back_copies(2, (3,))
         pair_muls(2, 1, 0)
-        o_inter(2, 1, 0, HALF + P)
-        o_muls(2, 0, (3, 2))
+        o_inter(1, 0)
+        back_copies(2, (3,))
         o_store(2, 1, 0, 4, HALF, 512)
-        o_muls(2, 0, (1, 0))
+        d_subs(3)
+        d_inter(3, D_POOL_MID)
+        o_inter(1, 1, 0, HALF)
+        o_inter(2, 1, 0, HALF + P)
+        o_muls(2, 0)
         o_inter(2, 0)
         d_quant(3)
         o_alloc(3, 0)
@@ -567,8 +564,8 @@ def tile_ordinaldepththresholdfeaturegradient_x1_kernel(tc, x, g, w, s, b, y, t,
         for dh in range(2):
             for lo in (0, HALF):
                 pair_products(3, dh, lo)
-        o_quant(1, 1)
         o_quant(1, 0)
+        o_quant(1, 1)
         code_store(1)
         pair_muls(3, 0, 0, (0, 1))
         o_inter_shared(3, 0, 0, HALF, HALF)

@@ -25,7 +25,7 @@ LAST_FIRST = (3, 2, 1, 0)
 
 RUN = 4
 D_POOL_FIRST = 224
-D_POOL_MID = 288
+D_POOL_MID = 384
 D_POOL_LAST = 416
 D_POOL_WIDE = 448
 D_POOL_LONG = 416
@@ -520,11 +520,9 @@ def tile_ordinaldepththresholdfeaturegradient_x1_kernel(tc, x, g, w, s, b, y, t,
         d_subs(2, range(4))
         d_inter(2, D_POOL_WIDE)
         x_muls(3)
-        mm2s(1, 0, (3,), skip=2)
+        mm2s(1, 0, skip=2)
         turn_back(1, TB)
         pair_muls(1, 1, 0)
-        o_muls(1, 0, (3,))
-        mm2s(1, 0, (0, 1, 2), skip=3)
         back_copies(1, T)
         o_store(1, 1, 0, 4, HALF, 512)
         o_inter(0, 1, 0, HALF)
@@ -535,7 +533,7 @@ def tile_ordinaldepththresholdfeaturegradient_x1_kernel(tc, x, g, w, s, b, y, t,
         o_quant(0, 0)
         o_alloc(2, 1)
         o_alloc(2, 0)
-        o_muls(1, 0, (2, 1, 0))
+        o_muls(1, 0)
         pair_products(2, 1, 0)
         quad_products(2, 2)
         sigms(3, (1, 0))
@@ -547,13 +545,13 @@ def tile_ordinaldepththresholdfeaturegradient_x1_kernel(tc, x, g, w, s, b, y, t,
         turn_back(2, (3,))
         o_quant(0, 1)
         code_store(0)
-        quad_mul(2, 2)
         pair_muls(2, 1, 0)
         o_inter(1, 0)
         back_copies(2, (3,))
-        o_store(2, 1, 0, 4, HALF, 512)
         d_subs(3)
         d_inter(3, D_POOL_MID)
+        quad_mul(2, 2)
+        o_store(2, 1, 0, 4, HALF, 512)
         o_inter(1, 1, 0, HALF)
         o_inter(2, 1, 0, HALF + P)
         o_muls(2, 0)
@@ -561,9 +559,8 @@ def tile_ordinaldepththresholdfeaturegradient_x1_kernel(tc, x, g, w, s, b, y, t,
         d_quant(3)
         o_alloc(3, 0)
         o_alloc(3, 1)
-        for dh in range(2):
-            for lo in (0, HALF):
-                pair_products(3, dh, lo)
+        for dh, lo in ((0, 0), (0, HALF), (1, HALF), (1, 0)):
+            pair_products(3, dh, lo)
         o_quant(1, 0)
         o_quant(1, 1)
         code_store(1)

@@ -346,6 +346,20 @@ def tile_ordinaldepththresholdfeaturegradient_x1_kernel(tc, x, g, w, s, b, y, t,
             )
             free.append(banks[(c, j)][1])
 
+        def warm_tensor(codes, scales, skip):
+            for _ in range(4):
+                acc, bank = take_bank([P, 512], skip=skip)
+                nc.tensor.matmul_mx(
+                    out=acc[:],
+                    lhsT=codes[:, 0:P].bitcast(FP8X4),
+                    lhsT_scale=scales[:, 0:P],
+                    rhs=codes.bitcast(FP8X4),
+                    rhs_scale=scales,
+                    start=True,
+                    stop=True,
+                )
+                free.append(bank)
+
         turned = {}
         back = {}
 
@@ -494,11 +508,11 @@ def tile_ordinaldepththresholdfeaturegradient_x1_kernel(tc, x, g, w, s, b, y, t,
         o_alloc(0, 1)
         o_alloc(0, 0)
         turned_products(0, T)
-        pair_products(0, 1, 0)
         mm2s(0, 0)
         x_quant(2)
         turned_scale(0, TB)
         turn_back(0, TB)
+        pair_products(0, 1, 0)
         d_subs(1)
         o_muls(0, 0)
         mm1s(2)
@@ -555,6 +569,7 @@ def tile_ordinaldepththresholdfeaturegradient_x1_kernel(tc, x, g, w, s, b, y, t,
         o_inter(1, 1, 0, HALF)
         o_inter(2, 1, 0, HALF + P)
         o_muls(2, 0)
+        warm_tensor(w_codes[:, 0], w_scales[:, 0], 4)
         o_inter(2, 0)
         d_quant(3)
         o_alloc(3, 0)
@@ -564,7 +579,7 @@ def tile_ordinaldepththresholdfeaturegradient_x1_kernel(tc, x, g, w, s, b, y, t,
         o_quant(1, 0)
         o_quant(1, 1)
         code_store(1)
-        pair_muls(3, 0, 0, (0, 1))
+        pair_muls(3, 0, 0)
         o_inter_shared(3, 0, 0, HALF, HALF)
         pair_muls(3, 0, HALF)
         o_inter(3, 0, HALF, 512)

@@ -170,14 +170,14 @@ def tile_ordinaldepththresholdfeaturegradient_x1_kernel(tc, x, g, w, s, b, y, t,
             free.append(wts[(h, jp)][1])
 
         g_bc = keep.tile([P, D], BF16, align_bytes=64, name="g_bc")
-        g_rows = keep.tile([P, 4], F32, align_bytes=64, name="g_rows")
+        g_rows = keep.tile([P, 2], F32, align_bytes=64, name="g_rows")
 
         gs = []
 
         def g_turn():
-            gs.extend(take_bank([P, 4, P], BF16))
-            for j in range(4):
-                nc.tensor.transpose(gs[0][:, j, :], g_bc[:, 512 + j * P : 512 + (j + 1) * P], id16[:])
+            gs.extend(take_bank([P, 2, P], BF16))
+            for j in range(2):
+                nc.tensor.transpose(gs[0][:, j, :], g_bc[:, TURNED + j * P : TURNED + (j + 1) * P], id16[:])
 
         def g_copy():
             nc.scalar.copy(out=g_rows[:], in_=gs[0][:, :, 0])
@@ -381,7 +381,7 @@ def tile_ordinaldepththresholdfeaturegradient_x1_kernel(tc, x, g, w, s, b, y, t,
             for j in js:
                 o, bank = turned[(c, j)]
                 ot = work.tile([P, 4, P], F32, align_bytes=64, name="o_turned", bufs=4)
-                nc.scalar.activation(out=ot[:].rearrange("p t m -> p (t m)"), in_=o[:], func=ACT.Copy, scale=g_rows[:, j : j + 1])
+                nc.scalar.activation(out=ot[:].rearrange("p t m -> p (t m)"), in_=o[:], func=ACT.Copy, scale=g_rows[:, j - 2 : j - 1])
                 free.append(bank)
                 turned[(c, j)] = ot
 
@@ -499,6 +499,7 @@ def tile_ordinaldepththresholdfeaturegradient_x1_kernel(tc, x, g, w, s, b, y, t,
         d_subs(0, range(4))
         d_inter(0, D_POOL_FIRST)
         x_muls(2)
+        warm_tensor(w_codes[:, 0], w_scales[:, 0], 2)
         g_copy()
         sigms(1, (3, 2))
 
@@ -516,13 +517,12 @@ def tile_ordinaldepththresholdfeaturegradient_x1_kernel(tc, x, g, w, s, b, y, t,
         d_subs(1)
         o_muls(0, 0)
         mm1s(2)
-        d_inter(1, D_POOL_LONG)
-        back_copies(0, (2,))
+        back_copies(0, T)
+        d_inter(1, D_POOL_WIDE)
         pair_muls(0, 1, 0)
+        o_store(0, 1, 0, 4, HALF, 512)
         sigms(2)
         x_turns(3)
-        back_copies(0, (3,))
-        o_store(0, 1, 0, 4, HALF, 512)
 
         d_quant(1)
         o_alloc(1, 1)
@@ -534,8 +534,8 @@ def tile_ordinaldepththresholdfeaturegradient_x1_kernel(tc, x, g, w, s, b, y, t,
         d_subs(2, range(4))
         d_inter(2, D_POOL_WIDE)
         x_muls(3)
-        mm2s(1, 0, skip=2)
         turn_back(1, TB)
+        mm2s(1, 0)
         pair_muls(1, 1, 0)
         back_copies(1, T)
         o_store(1, 1, 0, 4, HALF, 512)
@@ -549,13 +549,13 @@ def tile_ordinaldepththresholdfeaturegradient_x1_kernel(tc, x, g, w, s, b, y, t,
         o_alloc(2, 0)
         o_muls(1, 0)
         pair_products(2, 1, 0)
-        quad_products(2, 2)
         sigms(3, (1, 0))
         turned_products(2, (3,))
         sigms(3, (3, 2))
         turned_scale(2, (3,))
 
         mm2s(2, 0)
+        quad_products(2, 2)
         turn_back(2, (3,))
         o_quant(0, 1)
         code_store(0)

@@ -424,9 +424,9 @@ def tile_ordinaldepththresholdfeaturegradient_x1_kernel(tc, x, g, w, s, b, y, t,
         col_load(nc.scalar, y_col[:], y)
         w_load(0)
         col_load(nc.scalar, t_col[:].unsqueeze(1), t)
-        w_load(1)
-        col_load(nc.scalar, s_col[:].unsqueeze(1), s)
         x_load(1, 0, 1)
+        col_load(nc.scalar, s_col[:].unsqueeze(1), s)
+        w_load(1)
         x_load(1, 1, 2)
         col_load(nc.sync, b_col[:].unsqueeze(1), b)
         x_load(2, 0, 2)
@@ -460,31 +460,26 @@ def tile_ordinaldepththresholdfeaturegradient_x1_kernel(tc, x, g, w, s, b, y, t,
             x_muls(0, (2 * tp, 2 * tp + 1))
             x_quant_part(0, 2 * tp)
             x_quant_part(0, 2 * tp + 1)
+        x_turns(1, (0, 1))
         wt_turn(1, 0)
-        wt_turn(1, 1)
         dst, src = w_views(0)
         nc.scalar.copy(out=dst, in_=src)
         y_copy(1)
         dst, src = w_views(1)
-        nc.scalar.copy(out=dst[:, :, 0:2], in_=src[:, :, 0:2])
-        x_turns(1)
+        nc.scalar.copy(out=dst[:, :, 0:3], in_=src[:, :, 0:3])
+        x_turns(1, (2, 3))
         labels(0, 2)
+        x_muls(1, (1, 0))
+        wt_turn(1, 1)
         w_quant(0)
-        nc.gpsimd.tensor_scalar(
-            out=w_gr[:, 0, HALF:K, :].rearrange("p (q m) j -> p m q j", q=2),
-            in0=w_raw[1][:].rearrange("p (j m q) -> p m q j", j=4, q=4)[:, :, 2:4, :],
-            scalar1=1.0,
-            scalar2=-0.0,
-            op0=ALU.mult,
-            op1=ALU.add,
-        )
-        x_muls(1, (1, 0, 3, 2))
-        mm1s(0, range(4), (0,))
+        nc.vector.tensor_copy(out=dst[:, :, 3:4], in_=src[:, :, 3:4])
+        mm1s(0, (0, 1), (0,))
+        x_muls(1, (3, 2))
+        mm1s(0, (2, 3), (0,))
         for h in (1, 0):
             wt_copy(h, 1)
             wt_copy(h, 0)
-        w_quant(1, 0, HALF)
-        w_quant(1, HALF, K, 0)
+        w_quant(1)
         mm1s(0, range(4), (1,))
         x_quant(1)
         x_turns(2, (0, 1))
@@ -498,7 +493,7 @@ def tile_ordinaldepththresholdfeaturegradient_x1_kernel(tc, x, g, w, s, b, y, t,
         g_turn()
         d_subs(0, range(4))
         d_inter(0, D_POOL_FIRST)
-        x_muls(2)
+        x_muls(2, (1, 0, 3, 2))
         warm_tensor(w_codes[:, 0], w_scales[:, 0], 2)
         g_copy()
         sigms(1, (3, 2))

@@ -25,7 +25,7 @@ LAST_FIRST = (3, 2, 1, 0)
 
 RUN = 4
 D_POOL_FIRST = 224
-D_POOL_MID = 384
+D_POOL_MID = 288
 D_POOL_LAST = 416
 D_POOL_WIDE = 448
 D_POOL_LONG = 416
@@ -243,8 +243,8 @@ def tile_ordinaldepththresholdfeaturegradient_x1_kernel(tc, x, g, w, s, b, y, t,
 
         def inter(dst, src, lo, hi):
             nc.scalar.copy(
-                out=dst[:, lo:hi, :].rearrange("p (a i) q -> p a q i", i=RUN),
-                in_=src[:, :, lo:hi].rearrange("p q (a i) -> p a q i", i=RUN),
+                out=dst[:, lo:hi, :].rearrange("p (a i) (u e) -> p a u i e", i=RUN, u=2),
+                in_=src[:, :, lo:hi].rearrange("p (u e) (a i) -> p a u i e", i=RUN, u=2),
             )
 
         def inter_shared(dst, src, lo, mid, hi):
@@ -311,7 +311,9 @@ def tile_ordinaldepththresholdfeaturegradient_x1_kernel(tc, x, g, w, s, b, y, t,
                     op=ALU.mult,
                 )
                 free.append(banks[(c, dh, tt)][1])
-                if tt % 2 == 0:
+                if c >= 2:
+                    o_store(c, dh, tt, tt + 1, 0, 512)
+                elif tt % 2 == 0:
                     o_store(c, dh, tt, tt + 2, 0, 512)
 
         def pair_products(c, dh, lo, skip=0):
@@ -320,7 +322,7 @@ def tile_ordinaldepththresholdfeaturegradient_x1_kernel(tc, x, g, w, s, b, y, t,
                 for tt in range(2):
                     mm2(banks[(c, dh, tp, lo)][0][:, tt, :], c, 2 * tp + tt, dh * 512 + lo, dh * 512 + lo + HALF)
 
-        def pair_muls(c, dh, lo, tps=(1, 0)):
+        def pair_muls(c, dh, lo, tps=(1, 0), by_bank=False):
             for tp in tps:
                 nc.vector.tensor_tensor(
                     out=outp[(c, dh)]["o"][:, 2 * tp : 2 * tp + 2, lo : lo + HALF],
@@ -329,22 +331,10 @@ def tile_ordinaldepththresholdfeaturegradient_x1_kernel(tc, x, g, w, s, b, y, t,
                     op=ALU.mult,
                 )
                 free.append(banks[(c, dh, tp, lo)][1])
-            if len(tps) == 2 or 0 in tps:
+                if by_bank:
+                    o_store(c, dh, 2 * tp, 2 * tp + 2, lo, lo + HALF)
+            if not by_bank:
                 o_store(c, dh, 0, 4, lo, lo + HALF)
-
-        def quad_products(c, j):
-            banks[(c, j)] = take_bank([P, 4, P])
-            for tt in range(4):
-                mm2(banks[(c, j)][0][:, tt, :], c, tt, 512 + j * P, 512 + (j + 1) * P)
-
-        def quad_mul(c, j):
-            nc.vector.tensor_tensor(
-                out=outp[(c, 1)]["o"][:, :, j * P : (j + 1) * P],
-                in0=banks[(c, j)][0][:],
-                in1=g_bc[:, 512 + j * P : 512 + (j + 1) * P].unsqueeze(1).to_broadcast([P, 4, P]),
-                op=ALU.mult,
-            )
-            free.append(banks[(c, j)][1])
 
         def warm_tensor(codes, scales, skip):
             for _ in range(4):
@@ -395,7 +385,6 @@ def tile_ordinaldepththresholdfeaturegradient_x1_kernel(tc, x, g, w, s, b, y, t,
             for j in js:
                 cols = slice(j * P, (j + 1) * P)
                 nc.scalar.copy(out=outp[(c, 1)]["o"][:, :, cols], in_=back[(c, j)][0][:])
-                inter(outp[(c, 1)]["gr"][:, cols, :], back[(c, j)][0], 0, P)
                 free.append(back[(c, j)][1])
 
         def o_inter(c, dh, lo=0, hi=512):
@@ -525,44 +514,45 @@ def tile_ordinaldepththresholdfeaturegradient_x1_kernel(tc, x, g, w, s, b, y, t,
         turned_products(1, T)
         pair_products(1, 1, 0)
         o_inter(0, 0)
+        o_inter(0, 1, HALF, 512)
         turned_scale(1, TB)
         d_subs(2, range(4))
         d_inter(2, D_POOL_WIDE)
+        o_inter(0, 1, 0, HALF)
         x_muls(3)
+        mm2s(1, 0, skip=2)
         turn_back(1, TB)
-        mm2s(1, 0)
         pair_muls(1, 1, 0)
         back_copies(1, T)
         o_store(1, 1, 0, 4, HALF, 512)
-        o_inter(0, 1, 0, HALF)
+        o_inter(1, 1, 0, HALF)
         x_quant(3)
         mm1s(3)
         d_quant(2)
-        labels(3, 4, (0, 1, 3, 2))
-        o_quant(0, 0)
         o_alloc(2, 1)
         o_alloc(2, 0)
         o_muls(1, 0)
+        turned_products(2, T)
         pair_products(2, 1, 0)
-        sigms(3, (1, 0))
-        turned_products(2, (3,))
-        sigms(3, (3, 2))
-        turned_scale(2, (3,))
+        labels(3, 4, (0, 1, 3, 2))
+        o_quant(0, 0)
+        code_store(0, 0, 512)
+        sigms(3)
+        turned_scale(2, TB)
 
         mm2s(2, 0)
-        quad_products(2, 2)
-        turn_back(2, (3,))
+        turn_back(2, TB)
         o_quant(0, 1)
-        code_store(0)
+        code_store(0, 512, D)
         pair_muls(2, 1, 0)
-        o_inter(1, 0)
-        back_copies(2, (3,))
+        o_inter(1, 1, HALF, 512)
+        back_copies(2, T)
+        o_store(2, 1, 0, 4, HALF, 512)
+        o_inter(1, 0, 0, HALF)
         d_subs(3)
         d_inter(3, D_POOL_MID)
-        quad_mul(2, 2)
-        o_store(2, 1, 0, 4, HALF, 512)
-        o_inter(1, 1, 0, HALF)
-        o_inter(2, 1, 0, HALF + P)
+        o_inter(1, 0, HALF, 512)
+        o_inter(2, 1)
         o_muls(2, 0)
         warm_tensor(w_codes[:, 0], w_scales[:, 0], 4)
         o_inter(2, 0)
@@ -571,14 +561,15 @@ def tile_ordinaldepththresholdfeaturegradient_x1_kernel(tc, x, g, w, s, b, y, t,
         o_alloc(3, 1)
         for dh, lo in ((0, 0), (0, HALF), (1, HALF), (1, 0)):
             pair_products(3, dh, lo)
-        o_quant(1, 0)
         o_quant(1, 1)
-        code_store(1)
-        pair_muls(3, 0, 0)
+        code_store(1, 512, D)
+        o_quant(1, 0)
+        code_store(1, 0, 512)
+        pair_muls(3, 0, 0, by_bank=True)
         o_inter_shared(3, 0, 0, HALF, HALF)
-        pair_muls(3, 0, HALF)
+        pair_muls(3, 0, HALF, by_bank=True)
         o_inter(3, 0, HALF, 512)
-        pair_muls(3, 1, 0)
+        pair_muls(3, 1, 0, by_bank=True)
         o_inter(3, 1, 0, HALF)
         pair_muls(3, 1, HALF)
         o_inter(3, 1, HALF, 512)

@@ -59,6 +59,13 @@ def tile_ordinaldepththresholdfeaturegradient_x1_kernel(tc, x, g, w, s, b, y, t,
             for tp in range(tp0, tp1):
                 x_raw[(c, tp)] = xr[:].bitcast(F32)[:, 2 * (tp - tp0) : 2 * (tp - tp0 + 1), :]
 
+        first = {}
+
+        def first_load(h):
+            first[h] = keep.tile([P, 2, 512], BF16, align_bytes=64, name="x_first%d" % h)
+            xv = x[0:CH, 512 * h : 512 * (h + 1)].rearrange("(p t) d -> p t d", t=4)
+            nc.sync.dma_start(out=first[h][:], in_=xv[:, 0:2, :])
+
         def w_load(h):
             w_raw[h] = keep.tile([P, 4 * K], BF16, align_bytes=64, name="wr%d" % h)
             nc.sync.dma_start(out=w_raw[h][:], in_=w[h * 512 : (h + 1) * 512, :].rearrange("(p j) k -> p (j k)", j=4))
@@ -118,7 +125,7 @@ def tile_ordinaldepththresholdfeaturegradient_x1_kernel(tc, x, g, w, s, b, y, t,
                     for u in range(2):
                         nc.tensor.transpose(
                             xts[(c, i)][0][:, u, tt * P : (tt + 1) * P],
-                            x_raw[(c, tp)][:, tt, HALF * h + u : HALF * (h + 1) : 2],
+                            first[h][:].bitcast(F32)[:, tt, u:HALF:2] if (c, tp) == (0, 0) else x_raw[(c, tp)][:, tt, HALF * h + u : HALF * (h + 1) : 2],
                             id32[:],
                         )
 
@@ -336,8 +343,8 @@ def tile_ordinaldepththresholdfeaturegradient_x1_kernel(tc, x, g, w, s, b, y, t,
             if not by_bank:
                 o_store(c, dh, 0, 4, lo, lo + HALF)
 
-        def warm_tensor(codes, scales, skip):
-            for _ in range(4):
+        def warm_tensor(codes, scales, skip, passes):
+            for _ in range(passes):
                 acc, bank = take_bank([P, 512], skip=skip)
                 nc.tensor.matmul_mx(
                     out=acc[:],
@@ -407,14 +414,15 @@ def tile_ordinaldepththresholdfeaturegradient_x1_kernel(tc, x, g, w, s, b, y, t,
                 in_=o_codes[:, c, lo:hi].bitcast(I32),
             )
 
-        x_load(0, 0, 1)
+        first_load(0)
         col_load(nc.scalar, g_col[:], g)
-        x_load(0, 1, 2)
+        first_load(1)
         col_load(nc.scalar, y_col[:], y)
-        w_load(0)
+        x_load(0, 1, 2)
         col_load(nc.scalar, t_col[:].unsqueeze(1), t)
-        x_load(1, 0, 1)
+        w_load(0)
         col_load(nc.scalar, s_col[:].unsqueeze(1), s)
+        x_load(1, 0, 1)
         w_load(1)
         x_load(1, 1, 2)
         col_load(nc.sync, b_col[:].unsqueeze(1), b)
@@ -483,7 +491,6 @@ def tile_ordinaldepththresholdfeaturegradient_x1_kernel(tc, x, g, w, s, b, y, t,
         d_subs(0, range(4))
         d_inter(0, D_POOL_FIRST)
         x_muls(2, (1, 0, 3, 2))
-        warm_tensor(w_codes[:, 0], w_scales[:, 0], 2)
         g_copy()
         sigms(1, (3, 2))
 
@@ -554,7 +561,7 @@ def tile_ordinaldepththresholdfeaturegradient_x1_kernel(tc, x, g, w, s, b, y, t,
         o_inter(1, 0, HALF, 512)
         o_inter(2, 1)
         o_muls(2, 0)
-        warm_tensor(w_codes[:, 0], w_scales[:, 0], 4)
+        warm_tensor(w_codes[:, 0], w_scales[:, 0], 4, 4)
         o_inter(2, 0)
         d_quant(3)
         o_alloc(3, 0)

@@ -25,11 +25,11 @@ LAST_FIRST = (3, 2, 1, 0)
 
 RUN = 4
 D_POOL_FIRST = 224
-D_POOL_MID = 288
+D_POOL_MID = 272
 D_POOL_LAST = 416
 D_POOL_WIDE = 448
 D_POOL_LONG = 416
-O_POOL = 192
+O_POOL = 160
 O_GR_BUFS = 7
 
 
@@ -329,7 +329,7 @@ def tile_ordinaldepththresholdfeaturegradient_x1_kernel(tc, x, g, w, s, b, y, t,
                 for tt in range(2):
                     mm2(banks[(c, dh, tp, lo)][0][:, tt, :], c, 2 * tp + tt, dh * 512 + lo, dh * 512 + lo + HALF)
 
-        def pair_muls(c, dh, lo, tps=(1, 0), by_bank=False):
+        def pair_muls(c, dh, lo, tps=(1, 0), by_bank=False, store=True):
             for tp in tps:
                 nc.vector.tensor_tensor(
                     out=outp[(c, dh)]["o"][:, 2 * tp : 2 * tp + 2, lo : lo + HALF],
@@ -340,7 +340,7 @@ def tile_ordinaldepththresholdfeaturegradient_x1_kernel(tc, x, g, w, s, b, y, t,
                 free.append(banks[(c, dh, tp, lo)][1])
                 if by_bank:
                     o_store(c, dh, 2 * tp, 2 * tp + 2, lo, lo + HALF)
-            if not by_bank:
+            if store and not by_bank:
                 o_store(c, dh, 0, 4, lo, lo + HALF)
 
         def warm_tensor(codes, scales, skip, passes):
@@ -360,9 +360,9 @@ def tile_ordinaldepththresholdfeaturegradient_x1_kernel(tc, x, g, w, s, b, y, t,
         turned = {}
         back = {}
 
-        def turned_products(c, js):
+        def turned_products(c, js, skip=0):
             for j in js:
-                turned[(c, j)] = take_bank([P, CH])
+                turned[(c, j)] = take_bank([P, CH], skip=skip)
                 cols = slice(512 + j * P, 512 + (j + 1) * P)
                 nc.tensor.matmul_mx(
                     out=turned[(c, j)][0][:],
@@ -466,7 +466,7 @@ def tile_ordinaldepththresholdfeaturegradient_x1_kernel(tc, x, g, w, s, b, y, t,
         nc.scalar.copy(out=dst[:, :, 0:3], in_=src[:, :, 0:3])
         x_turns(1, (2, 3))
         labels(0, 2)
-        x_muls(1, (1, 0))
+        x_muls(1, (0, 1))
         wt_turn(1, 1)
         w_quant(0)
         nc.vector.tensor_copy(out=dst[:, :, 3:4], in_=src[:, :, 3:4])
@@ -505,7 +505,7 @@ def tile_ordinaldepththresholdfeaturegradient_x1_kernel(tc, x, g, w, s, b, y, t,
         turned_scale(0, TB)
         turn_back(0, TB)
         pair_products(0, 1, 0)
-        d_subs(1)
+        d_subs(1, range(4))
         o_muls(0, 0)
         mm1s(2)
         back_copies(0, T)
@@ -524,37 +524,41 @@ def tile_ordinaldepththresholdfeaturegradient_x1_kernel(tc, x, g, w, s, b, y, t,
         o_inter(0, 1, HALF, 512)
         turned_scale(1, TB)
         d_subs(2, range(4))
-        d_inter(2, D_POOL_WIDE)
+        d_inter(2, CH)
         o_inter(0, 1, 0, HALF)
         x_muls(3)
-        mm2s(1, 0, skip=2)
+        mm2s(1, 0, (0, 1), skip=2)
         turn_back(1, TB)
+        mm2s(1, 0, (2, 3))
         pair_muls(1, 1, 0)
         back_copies(1, T)
         o_store(1, 1, 0, 4, HALF, 512)
         o_inter(1, 1, 0, HALF)
         x_quant(3)
-        mm1s(3)
+        mm1s(3, (0, 1))
         d_quant(2)
         o_alloc(2, 1)
         o_alloc(2, 0)
         o_muls(1, 0)
-        turned_products(2, T)
+        turned_products(2, T, skip=2)
+        mm1s(3, (2, 3))
         pair_products(2, 1, 0)
         labels(3, 4, (0, 1, 3, 2))
         o_quant(0, 0)
         code_store(0, 0, 512)
-        sigms(3)
+        sigms(3, (1, 0))
         turned_scale(2, TB)
-
-        mm2s(2, 0)
         turn_back(2, TB)
+        mm2s(2, 0, (0, 1))
+        sigms(3, (3, 2))
+
+        mm2s(2, 0, (2, 3))
         o_quant(0, 1)
         code_store(0, 512, D)
         pair_muls(2, 1, 0)
-        o_inter(1, 1, HALF, 512)
         back_copies(2, T)
         o_store(2, 1, 0, 4, HALF, 512)
+        o_inter(1, 1, HALF, 512)
         o_inter(1, 0, 0, HALF)
         d_subs(3)
         d_inter(3, D_POOL_MID)
@@ -566,19 +570,22 @@ def tile_ordinaldepththresholdfeaturegradient_x1_kernel(tc, x, g, w, s, b, y, t,
         d_quant(3)
         o_alloc(3, 0)
         o_alloc(3, 1)
-        for dh, lo in ((0, 0), (0, HALF), (1, HALF), (1, 0)):
-            pair_products(3, dh, lo)
+        mm2s(3, 0)
+        pair_products(3, 1, HALF)
+        pair_products(3, 1, 0)
         o_quant(1, 1)
         code_store(1, 512, D)
         o_quant(1, 0)
         code_store(1, 0, 512)
-        pair_muls(3, 0, 0, by_bank=True)
-        o_inter_shared(3, 0, 0, HALF, HALF)
-        pair_muls(3, 0, HALF, by_bank=True)
-        o_inter(3, 0, HALF, 512)
-        pair_muls(3, 1, 0, by_bank=True)
+        o_muls(3, 0, (1, 0, 3, 2))
+        o_inter_shared(3, 0, 0, O_POOL, 512)
+        pair_muls(3, 1, 0, (0,), store=False)
+        pair_muls(3, 1, HALF, (0,), store=False)
+        o_store(3, 1, 0, 2, 0, 512)
+        pair_muls(3, 1, 0, (1,), store=False)
         o_inter(3, 1, 0, HALF)
-        pair_muls(3, 1, HALF)
+        pair_muls(3, 1, HALF, (1,), store=False)
+        o_store(3, 1, 2, 4, 0, 512)
         o_inter(3, 1, HALF, 512)
         o_quant(2, 0)
         o_quant(2, 1)

from contextlib import ExitStack

import concourse.mybir as mybir
from concourse.masks import make_identity

N, D, K = 2048, 1024, 512
FLOPS = 4 * N * D * K

F32 = mybir.dt.float32
BF16 = mybir.dt.bfloat16
U32 = mybir.dt.uint32
I32 = mybir.dt.int32
U8 = mybir.dt.uint8
FP8X4 = mybir.dt.float8_e4m3fn_x4
ALU = mybir.AluOpType
ACT = mybir.ActivationFunctionType

P = 128
CH = 512
NCH = N // CH
NH = D // 512
HALF = 256
TURNED = D - HALF
LAST_FIRST = (3, 2, 1, 0)

RUN = 4
D_POOL_FIRST = 224
D_POOL_MID = 272
D_POOL_LAST = 416
D_POOL_WIDE = 448
D_POOL_LONG = 416
O_POOL = 160
O_GR_BUFS = 7


def tile_ordinaldepththresholdfeaturegradient_x1_kernel(tc, x, g, w, s, b, y, t, out_0, out_1, out_2):
    nc = tc.nc
    with ExitStack() as ctx:
        keep = ctx.enter_context(tc.tile_pool(name="keep", bufs=1))
        work = ctx.enter_context(tc.tile_pool(name="work", bufs=2))
        big = ctx.enter_context(tc.tile_pool(name="big", bufs=8))
        outs = ctx.enter_context(tc.tile_pool(name="outs", bufs=O_GR_BUFS))
        psum = ctx.enter_context(tc.psum_pool(name="psum", bufs=1))
        ctx.enter_context(tc.manual_schedule())

        free = list(range(8))

        def take_bank(shape, dtype=F32, skip=0):
            i = free.pop(skip)
            return psum.tile(shape, dtype, name="bank%d" % i), i

        x_raw = {}
        w_raw = {}

        def x_load(c, tp0, tp1):
            xr = keep.tile([P, 2 * (tp1 - tp0), D], BF16, align_bytes=64, name="xr%d%d" % (c, tp0))
            xv = x[c * CH : (c + 1) * CH, :].rearrange("(p t) d -> p t d", t=4)
            nc.sync.dma_start(out=xr[:], in_=xv[:, 2 * tp0 : 2 * tp1, :])
            for tp in range(tp0, tp1):
                x_raw[(c, tp)] = xr[:].bitcast(F32)[:, 2 * (tp - tp0) : 2 * (tp - tp0 + 1), :]

        first = {}

        def first_load(h):
            first[h] = keep.tile([P, 2, 512], BF16, align_bytes=64, name="x_first%d" % h)
            xv = x[0:CH, 512 * h : 512 * (h + 1)].rearrange("(p t) d -> p t d", t=4)
            nc.sync.dma_start(out=first[h][:], in_=xv[:, 0:2, :])

        def w_load(h):
            w_raw[h] = keep.tile([P, 4 * K], BF16, align_bytes=64, name="wr%d" % h)
            nc.sync.dma_start(out=w_raw[h][:], in_=w[h * 512 : (h + 1) * 512, :].rearrange("(p j) k -> p (j k)", j=4))

        def col_load(queue, dst, v):
            queue.dma_start(out=dst, in_=v.rearrange("(a p i) -> p a i", p=P, i=4))

        g_col = keep.tile([P, NH, 4], BF16, align_bytes=64, name="g_col")
        y_col = keep.tile([P, NCH, 4], BF16, align_bytes=64, name="y_col")
        t_col = keep.tile([P, 4], BF16, align_bytes=64, name="t_col")
        s_col = keep.tile([P, 4], BF16, align_bytes=64, name="s_col")
        b_col = keep.tile([P, 4], BF16, align_bytes=64, name="b_col")
        s32 = keep.tile([P, 4], F32, align_bytes=64, name="s32")
        t32 = keep.tile([P, 4], F32, align_bytes=64, name="t32")
        warm = keep.tile([P, 1], F32, name="warm")
        warm2 = keep.tile([P, 1], F32, name="warm2")
        id32 = keep.tile([P, P], F32, align_bytes=64, name="id32")
        id16 = keep.tile([P, P], BF16, align_bytes=64, name="id16")
        g4 = g_col[:].rearrange("p h (u e) -> p h u e", u=2)

        y_bc = keep.tile([P, N], BF16, align_bytes=64, name="y_bc")
        ys = {}

        def y_spread(hf):
            ys[hf] = take_bank([P, 4, P])
            words = y_col[:].rearrange("p c t -> p (c t)").bitcast(F32)
            for i in range(4):
                nc.tensor.transpose(ys[hf][0][:, i, :], words[:, 4 * hf + i : 4 * hf + i + 1].to_broadcast([P, P]), id32[:])

        def y_copy(hf):
            nc.scalar.copy(
                out=y_bc[:, hf * N // 2 : (hf + 1) * N // 2].rearrange("p (i e m) -> p i e m", i=4, e=2),
                in_=ys[hf][0][:].bitcast(BF16).rearrange("p i (m e) -> p i e m", e=2),
            )
            free.append(ys[hf][1])

        w_gr = big.tile([P, NH, K, 4], BF16, align_bytes=64, name="big")
        w_codes = keep.tile([P, NH, K], U32, align_bytes=64, name="w_codes")
        w_scales = keep.tile([P, NH, K], U8, align_bytes=64, name="w_scales")

        def w_views(h):
            dst = w_gr[:, h].rearrange("p (q a m) j -> p a q m j", q=4, m=2)
            return dst, w_raw[h][:].rearrange("p (j a m q) -> p a q m j", j=4, m=2, q=4)

        def quantise(codes, scales, src):
            nc.vector.quantize_mx(out=codes.bitcast(FP8X4), scales=scales, in_=src)

        x_gr = {}
        x_q = {}
        xts = {}

        def x_turns(c, parts=range(4), skip=0):
            for i in parts:
                tp, h = i // 2, i % 2
                xts[(c, i)] = take_bank([P, 2, HALF], skip=skip)
                for tt in range(2):
                    for u in range(2):
                        nc.tensor.transpose(
                            xts[(c, i)][0][:, u, tt * P : (tt + 1) * P],
                            first[h][:].bitcast(F32)[:, tt, u:HALF:2] if (c, tp) == (0, 0) else x_raw[(c, tp)][:, tt, HALF * h + u : HALF * (h + 1) : 2],
                            id32[:],
                        )

        def x_muls(c, parts=LAST_FIRST):
            for i in parts:
                tp, h = i // 2, i % 2
                nc.vector.tensor_tensor(
                    out=x_gr[c][:, h, HALF * tp : HALF * (tp + 1), :].rearrange("p n (u e) -> p n u e", u=2),
                    in0=xts[(c, i)][0][:].bitcast(BF16).rearrange("p u (n e) -> p n u e", e=2),
                    in1=g4[:, h].unsqueeze(1).to_broadcast([P, HALF, 2, 2]),
                    op=ALU.mult,
                )
                free.append(xts[(c, i)][1])

        def x_planes(c):
            codes = work.tile([P, NH, CH], U32, align_bytes=64, name="x_codes")
            scales = work.tile([P, NH, CH], U8, align_bytes=64, name="x_scales")
            x_q[c] = (codes, scales)
            return codes, scales

        def x_quant_part(c, i):
            tp, h = i // 2, i % 2
            rows = slice(HALF * tp, HALF * (tp + 1))
            quantise(x_q[c][0][:, h, rows], x_q[c][1][:, h, rows], x_gr[c][:, h, rows, :].rearrange("p n j -> p (n j)"))

        def x_quant(c):
            codes, scales = x_planes(c)
            quantise(
                codes[:].rearrange("p h n -> p (h n)"),
                scales[:].rearrange("p h n -> p (h n)"),
                x_gr[c][:].rearrange("p h n j -> p (h n j)"),
            )

        wt_gr = big.tile([P, D, 4], BF16, align_bytes=64, name="big")
        wt_codes = keep.tile([P, D], U32, align_bytes=64, name="wt_codes")
        wt_scales = keep.tile([P, D], U8, align_bytes=64, name="wt_scales")
        wts = {}

        def wt_turn(h, jp):
            words = w_raw[h][:].bitcast(F32).rearrange("p (j k) -> p j k", j=4)
            wts[(h, jp)] = take_bank([P, 2, 2, P])
            for jj in range(2):
                for u in range(2):
                    nc.tensor.transpose(wts[(h, jp)][0][:, jj, u, :], words[:, 2 * jp + jj, u:HALF:2], id32[:])

        def wt_copy(h, jp):
            dst = wt_gr[:].rearrange("p d e -> p (d e)").bitcast(F32).rearrange("p (h m j u) -> p h m j u", h=NH, j=4, u=2)
            nc.scalar.copy(out=dst[:, h, :, 2 * jp : 2 * jp + 2, :], in_=wts[(h, jp)][0][:].rearrange("p j u m -> p m j u"))
            free.append(wts[(h, jp)][1])

        g_bc = keep.tile([P, D], BF16, align_bytes=64, name="g_bc")
        g_rows = keep.tile([P, 2], F32, align_bytes=64, name="g_rows")

        gs = []

        def g_turn():
            gs.extend(take_bank([P, 2, P], BF16))
            for j in range(2):
                nc.tensor.transpose(gs[0][:, j, :], g_bc[:, TURNED + j * P : TURNED + (j + 1) * P], id16[:])

        def g_copy():
            nc.scalar.copy(out=g_rows[:], in_=gs[0][:, :, 0])
            free.append(gs[1])

        ls = keep.tile([P, 4, N], BF16, align_bytes=64, name="ls")
        ds = {}
        zs = {}

        def labels(c0, c1, qs=LAST_FIRST):
            cols = slice(c0 * CH, c1 * CH)
            for q in qs:
                nc.vector.tensor_scalar(
                    out=ls[:, q, cols],
                    in0=y_bc[:, cols],
                    scalar1=t32[:, q : q + 1],
                    scalar2=s32[:, q : q + 1],
                    op0=ALU.is_gt,
                    op1=ALU.mult,
                )

        def d_tile(c, name, shape, dtype):
            if (c, name) not in ds:
                ds[(c, name)] = work.tile(shape, dtype, align_bytes=64, name=name)
            return ds[(c, name)]

        def mm1s(c, qs=range(4), hs=range(NH), skip=0):
            for q in qs:
                for h in hs:
                    if h == 0:
                        zs[(c, q)] = take_bank([P, CH], skip=skip)
                    nc.tensor.matmul_mx(
                        out=zs[(c, q)][0][:],
                        lhsT=w_codes[:, h, q * P : (q + 1) * P].bitcast(FP8X4),
                        lhsT_scale=w_scales[:, h, q * P : (q + 1) * P],
                        rhs=x_q[c][0][:, h].bitcast(FP8X4),
                        rhs_scale=x_q[c][1][:, h],
                        start=(h == 0),
                        stop=(h == NH - 1),
                    )

        def sigms(c, qs=(1, 0, 3, 2)):
            for q in qs:
                nc.scalar.activation(
                    out=d_tile(c, "sig", [P, 4, CH], F32)[:, q, :],
                    in_=zs[(c, q)][0][:],
                    func=ACT.Sigmoid,
                    bias=b_col[:, q : q + 1],
                    scale=s32[:, q : q + 1],
                )
                free.append(zs[(c, q)][1])

        def d_subs(c, qs=(2, 3, 1, 0)):
            for q in qs:
                nc.vector.scalar_tensor_tensor(
                    out=d_tile(c, "d16", [P, 4, CH], BF16)[:, q, :],
                    in0=ds[(c, "sig")][:, q, :],
                    scalar=s32[:, q : q + 1],
                    in1=ls[:, q, c * CH : (c + 1) * CH],
                    op0=ALU.mult,
                    op1=ALU.subtract,
                )

        def inter(dst, src, lo, hi):
            nc.scalar.copy(
                out=dst[:, lo:hi, :].rearrange("p (a i) (u e) -> p a u i e", i=RUN, u=2),
                in_=src[:, :, lo:hi].rearrange("p (u e) (a i) -> p a u i e", i=RUN, u=2),
            )

        def inter_shared(dst, src, lo, mid, hi):
            nc.gpsimd.tensor_scalar(
                out=dst[:, lo:mid, :],
                in0=src[:, :, lo:mid].rearrange("p q n -> p n q"),
                scalar1=1.0,
                scalar2=-0.0,
                op0=ALU.mult,
                op1=ALU.add,
            )
            if mid < hi:
                inter(dst, src, mid, hi)

        def d_inter(c, pool_rows):
            inter_shared(d_tile(c, "d_gr", [P, CH, 4], BF16), ds[(c, "d16")], 0, pool_rows, CH)

        def d_quant(c):
            quantise(
                d_tile(c, "d_codes", [P, CH], U32)[:],
                d_tile(c, "d_scales", [P, CH], U8)[:],
                ds[(c, "d_gr")][:].rearrange("p n j -> p (n j)"),
            )

        outp = {}
        banks = {}
        o_codes = keep.tile([P, NCH, D], U32, align_bytes=64, name="o_codes")
        o_scales = keep.tile([P, D], U8, align_bytes=64, name="o_scales")

        def o_alloc(c, dh):
            outp[(c, dh)] = dict(
                o=big.tile([P, 4, 512], F32, align_bytes=64, name="big"),
                gr=outs.tile([P, 512, 4], BF16, align_bytes=64, name="o_gr"),
            )

        def mm2(out, c, tt, d0, d1):
            nc.tensor.matmul_mx(
                out=out,
                lhsT=ds[(c, "d_codes")][:, tt * P : (tt + 1) * P].bitcast(FP8X4),
                lhsT_scale=ds[(c, "d_scales")][:, tt * P : (tt + 1) * P],
                rhs=wt_codes[:, d0:d1].bitcast(FP8X4),
                rhs_scale=wt_scales[:, d0:d1],
                start=True,
                stop=True,
            )

        def mm2s(c, dh, tts=range(4), skip=0):
            for tt in tts:
                banks[(c, dh, tt)] = take_bank([P, 512], skip=skip)
                mm2(banks[(c, dh, tt)][0][:], c, tt, dh * 512, (dh + 1) * 512)

        def o_store(c, dh, t0, t1, lo, hi):
            nc.sync.dma_start(
                out=out_0[c * CH : (c + 1) * CH, dh * 512 + lo : dh * 512 + hi].rearrange("(p t) d -> p t d", t=4)[:, t0:t1, :],
                in_=outp[(c, dh)]["o"][:, t0:t1, lo:hi],
            )

        def o_muls(c, dh, tts=LAST_FIRST):
            for tt in tts:
                nc.vector.tensor_tensor(
                    out=outp[(c, dh)]["o"][:, tt, :],
                    in0=banks[(c, dh, tt)][0][:],
                    in1=g_bc[:, dh * 512 : (dh + 1) * 512],
                    op=ALU.mult,
                )
                free.append(banks[(c, dh, tt)][1])
                if c >= 2:
                    o_store(c, dh, tt, tt + 1, 0, 512)
                elif tt % 2 == 0:
                    o_store(c, dh, tt, tt + 2, 0, 512)

        def pair_products(c, dh, lo, skip=0):
            for tp in range(2):
                banks[(c, dh, tp, lo)] = take_bank([P, 2, HALF], skip=skip)
                for tt in range(2):
                    mm2(banks[(c, dh, tp, lo)][0][:, tt, :], c, 2 * tp + tt, dh * 512 + lo, dh * 512 + lo + HALF)

        def pair_muls(c, dh, lo, tps=(1, 0), by_bank=False, store=True):
            for tp in tps:
                nc.vector.tensor_tensor(
                    out=outp[(c, dh)]["o"][:, 2 * tp : 2 * tp + 2, lo : lo + HALF],
                    in0=banks[(c, dh, tp, lo)][0][:],
                    in1=g_bc[:, dh * 512 + lo : dh * 512 + lo + HALF].unsqueeze(1).to_broadcast([P, 2, HALF]),
                    op=ALU.mult,
                )
                free.append(banks[(c, dh, tp, lo)][1])
                if by_bank:
                    o_store(c, dh, 2 * tp, 2 * tp + 2, lo, lo + HALF)
            if store and not by_bank:
                o_store(c, dh, 0, 4, lo, lo + HALF)

        def warm_tensor(codes, scales, skip, passes):
            for _ in range(passes):
                acc, bank = take_bank([P, 512], skip=skip)
                nc.tensor.matmul_mx(
                    out=acc[:],
                    lhsT=codes[:, 0:P].bitcast(FP8X4),
                    lhsT_scale=scales[:, 0:P],
                    rhs=codes.bitcast(FP8X4),
                    rhs_scale=scales,
                    start=True,
                    stop=True,
                )
                free.append(bank)

        turned = {}
        back = {}

        def turned_products(c, js, skip=0):
            for j in js:
                turned[(c, j)] = take_bank([P, CH], skip=skip)
                cols = slice(512 + j * P, 512 + (j + 1) * P)
                nc.tensor.matmul_mx(
                    out=turned[(c, j)][0][:],
                    lhsT=wt_codes[:, cols].bitcast(FP8X4),
                    lhsT_scale=wt_scales[:, cols],
                    rhs=ds[(c, "d_codes")][:].bitcast(FP8X4),
                    rhs_scale=ds[(c, "d_scales")][:],
                    start=True,
                    stop=True,
                )

        def turned_scale(c, js):
            for j in js:
                o, bank = turned[(c, j)]
                ot = work.tile([P, 4, P], F32, align_bytes=64, name="o_turned", bufs=4)
                nc.scalar.activation(out=ot[:].rearrange("p t m -> p (t m)"), in_=o[:], func=ACT.Copy, scale=g_rows[:, j - 2 : j - 1])
                free.append(bank)
                turned[(c, j)] = ot

        def turn_back(c, js):
            for j in js:
                back[(c, j)] = take_bank([P, 4, P])
                for tt in range(4):
                    nc.tensor.transpose(back[(c, j)][0][:, tt, :], turned[(c, j)][:, tt, :], id32[:])

        def back_copies(c, js):
            for j in js:
                cols = slice(j * P, (j + 1) * P)
                nc.scalar.copy(out=outp[(c, 1)]["o"][:, :, cols], in_=back[(c, j)][0][:])
                free.append(back[(c, j)][1])

        def o_inter(c, dh, lo=0, hi=512):
            inter(outp[(c, dh)]["gr"], outp[(c, dh)]["o"], lo, hi)

        def o_inter_shared(c, dh, lo, mid, hi):
            inter_shared(outp[(c, dh)]["gr"], outp[(c, dh)]["o"], lo, mid, hi)

        def o_quant(c, dh, lo=0, hi=512):
            e = outp[(c, dh)]
            quantise(
                o_codes[:, c, dh * 512 + lo : dh * 512 + hi],
                o_scales[4 * c : P, dh * 512 + lo : dh * 512 + hi],
                e["gr"][:, lo:hi, :].rearrange("p d j -> p (d j)"),
            )

        def code_store(c, lo=0, hi=D):
            nc.sync.dma_start(
                out=out_1[c, :, lo:hi, :].rearrange("p m t -> p (m t)").bitcast(I32),
                in_=o_codes[:, c, lo:hi].bitcast(I32),
            )

        first_load(0)
        col_load(nc.scalar, g_col[:], g)
        first_load(1)
        col_load(nc.scalar, y_col[:], y)
        x_load(0, 1, 2)
        col_load(nc.scalar, t_col[:].unsqueeze(1), t)
        w_load(0)
        col_load(nc.scalar, s_col[:].unsqueeze(1), s)
        x_load(1, 0, 1)
        w_load(1)
        x_load(1, 1, 2)
        col_load(nc.sync, b_col[:].unsqueeze(1), b)
        x_load(2, 0, 2)
        nc.sync.dma_start(out=g_bc[:], in_=g.partition_broadcast(P))
        x_load(3, 0, 2)
        nc.vector.memset(warm[:], 0.0)
        nc.scalar.activation(out=warm2[:], in_=warm[:], func=ACT.Sigmoid)
        make_identity(nc, id32[:])
        make_identity(nc, id16[:])
        for c in range(NCH):
            x_gr[c] = big.tile([P, NH, CH, 4], BF16, align_bytes=64, name="big")

        def w_quant(h, lo=0, hi=K, held=None):
            src = w_gr[:, h if held is None else held, lo:hi, :]
            quantise(w_codes[:, h, lo:hi], w_scales[:, h, lo:hi], src.rearrange("p k j -> p (k j)"))

        def wt_quant():
            quantise(wt_codes[:], wt_scales[:], wt_gr[:].rearrange("p d j -> p (d j)"))

        x_turns(0, (0, 1))
        y_spread(0)
        x_turns(0, (2, 3))
        y_spread(1)
        y_copy(0)
        nc.gpsimd.tensor_copy(out=t32[:], in_=t_col[:])
        nc.gpsimd.tensor_copy(out=s32[:], in_=s_col[:])
        wt_turn(0, 0)
        wt_turn(0, 1)
        x_planes(0)
        for tp in range(2):
            x_muls(0, (2 * tp, 2 * tp + 1))
            x_quant_part(0, 2 * tp)
            x_quant_part(0, 2 * tp + 1)
        x_turns(1, (0, 1))
        wt_turn(1, 0)
        dst, src = w_views(0)
        nc.scalar.copy(out=dst, in_=src)
        y_copy(1)
        dst, src = w_views(1)
        nc.scalar.copy(out=dst[:, :, 0:3], in_=src[:, :, 0:3])
        x_turns(1, (2, 3))
        labels(0, 2)
        x_muls(1, (0, 1))
        wt_turn(1, 1)
        w_quant(0)
        nc.vector.tensor_copy(out=dst[:, :, 3:4], in_=src[:, :, 3:4])
        mm1s(0, (0, 1), (0,))
        x_muls(1, (3, 2))
        mm1s(0, (2, 3), (0,))
        for h in (1, 0):
            wt_copy(h, 1)
            wt_copy(h, 0)
        w_quant(1)
        mm1s(0, range(4), (1,))
        x_quant(1)
        x_turns(2, (0, 1))
        sigms(0)
        mm1s(1, (0, 1))
        x_turns(2, (2, 3))
        labels(2, 3)
        wt_quant()
        sigms(1, (1, 0))
        mm1s(1, (2, 3))
        g_turn()
        d_subs(0, range(4))
        d_inter(0, D_POOL_FIRST)
        x_muls(2, (1, 0, 3, 2))
        g_copy()
        sigms(1, (3, 2))

        T = (2, 3)
        TB = (3, 2)
        d_quant(0)
        o_alloc(0, 1)
        o_alloc(0, 0)
        turned_products(0, T)
        mm2s(0, 0)
        x_quant(2)
        turned_scale(0, TB)
        turn_back(0, TB)
        pair_products(0, 1, 0)
        d_subs(1, range(4))
        o_muls(0, 0)
        mm1s(2)
        back_copies(0, T)
        d_inter(1, D_POOL_WIDE)
        pair_muls(0, 1, 0)
        o_store(0, 1, 0, 4, HALF, 512)
        sigms(2)
        x_turns(3)

        d_quant(1)
        o_alloc(1, 1)
        o_alloc(1, 0)
        turned_products(1, T)
        pair_products(1, 1, 0)
        o_inter(0, 0)
        o_inter(0, 1, HALF, 512)
        turned_scale(1, TB)
        d_subs(2, range(4))
        d_inter(2, CH)
        o_inter(0, 1, 0, HALF)
        x_muls(3)
        mm2s(1, 0, (0, 1), skip=2)
        turn_back(1, TB)
        mm2s(1, 0, (2, 3))
        pair_muls(1, 1, 0)
        back_copies(1, T)
        o_store(1, 1, 0, 4, HALF, 512)
        o_inter(1, 1, 0, HALF)
        x_quant(3)
        mm1s(3, (0, 1))
        d_quant(2)
        o_alloc(2, 1)
        o_alloc(2, 0)
        o_muls(1, 0)
        turned_products(2, T, skip=2)
        mm1s(3, (2, 3))
        pair_products(2, 1, 0)
        labels(3, 4, (0, 1, 3, 2))
        o_quant(0, 0)
        code_store(0, 0, 512)
        sigms(3, (1, 0))
        turned_scale(2, TB)
        turn_back(2, TB)
        mm2s(2, 0, (0, 1))
        sigms(3, (3, 2))

        mm2s(2, 0, (2, 3))
        o_quant(0, 1)
        code_store(0, 512, D)
        pair_muls(2, 1, 0)
        back_copies(2, T)
        o_store(2, 1, 0, 4, HALF, 512)
        o_inter(1, 1, HALF, 512)
        o_inter(1, 0, 0, HALF)
        d_subs(3)
        d_inter(3, D_POOL_MID)
        o_inter(1, 0, HALF, 512)
        o_inter(2, 1)
        o_muls(2, 0)
        warm_tensor(w_codes[:, 0], w_scales[:, 0], 4, 4)
        o_inter(2, 0)
        d_quant(3)
        o_alloc(3, 0)
        o_alloc(3, 1)
        mm2s(3, 0)
        pair_products(3, 1, HALF)
        pair_products(3, 1, 0)
        o_quant(1, 1)
        code_store(1, 512, D)
        o_quant(1, 0)
        code_store(1, 0, 512)
        o_muls(3, 0, (1, 0, 3, 2))
        o_inter_shared(3, 0, 0, O_POOL, 512)
        pair_muls(3, 1, 0, (0,), store=False)
        pair_muls(3, 1, HALF, (0,), store=False)
        o_store(3, 1, 0, 2, 0, 512)
        pair_muls(3, 1, 0, (1,), store=False)
        o_inter(3, 1, 0, HALF)
        pair_muls(3, 1, HALF, (1,), store=False)
        o_store(3, 1, 2, 4, 0, 512)
        o_inter(3, 1, HALF, 512)
        o_quant(2, 0)
        o_quant(2, 1)
        code_store(2)
        o_quant(3, 0)
        o_quant(3, 1, 0, HALF)
        code_store(3, 0, D - HALF)
        o_quant(3, 1, HALF, 512)
        code_store(3, D - HALF, D)
        for qd in range(4):
            queue = nc.scalar if qd % 2 else nc.sync
            queue.dma_start(
                out=out_2[:, 4 * qd : 4 * qd + 4, :].bitcast(I32),
                in_=o_scales[32 * qd : 32 * qd + 16, :].bitcast(I32),
            )
